import numpy as np, ml_dtypes
CORES = [24,25,26,27,28,29,30,31]
N = 8
BF = ml_dtypes.bfloat16
def gentries(a):
    return np.ascontiguousarray(a.reshape(8, 16, -1).transpose(0, 2, 1)).reshape(8, -1)
def gtable(e):
    e = np.asarray(e); return np.ascontiguousarray(e.reshape(8, -1, 16).transpose(0, 2, 1)).reshape(128, -1).astype(np.int32)
W, L, T, TH, A, B, FO = 3072, 256, 6, 64, 6, 11, 2
def parts(rng):
    return (rng.integers(0, 16, (N, 8, 16, W)), rng.integers(0, W, (N, 8, 16, W)), rng.integers(0, 64, (N, 8, 16, L)), rng.integers(0, W, (N, 8, 16, L)),
            rng.integers(0, W, (N, 8, 16, L)), rng.integers(0, 16, (N, 8, 16, L)), rng.integers(0, W, (N, 8, L)), rng.integers(0, 64, (N, 8, 16)))
def keys(x, w, p):
    z = np.take_along_axis(x, p[:, :, None, :], 3)
    return np.add.reduce(z * w[..., None], axis=2) & 63
def pack(x, d, m, u, n, q, o, w):
    return {"feat": np.ascontiguousarray(x.reshape(N, 128, W)).astype(np.float32).astype(BF), "kids": np.ascontiguousarray(d.reshape(N, 128, W)).astype(np.int32),
            "mkey": np.ascontiguousarray(m.reshape(N, 128, L)).astype(np.float32).astype(BF), "mobj": np.ascontiguousarray(u.reshape(N, 128, L)).astype(np.int32),
            "cand": np.stack([gtable(a.transpose(0, 2, 1).reshape(8, -1)) for a in n]), "want": np.ascontiguousarray(q.reshape(N, 128, L)).astype(np.float32).astype(BF),
            "last": np.ascontiguousarray(o).astype(np.int32), "wts": np.ascontiguousarray(w.reshape(N, 128, 1)).astype(np.int32)}
def setup_inputs(rng):
    return pack(*parts(rng))
def setup_inputs_corners(rng):
    x, d, m, u, n, q, o, w = parts(rng); own = np.arange(W)[None, None, None, :]
    kind = rng.integers(0, 7, (N, 8, 1, W))
    d = np.where(kind == 0, own, d); d = np.where(kind == 1, (own + 1) % W, d)
    d = np.where(kind == 2, (W - 1) * rng.integers(0, 2, d.shape), d); d = np.where(kind == 3, d[:, :, :1, :], d)
    d[2] = d[2] & -2
    x[3, :, 0] = (x[3, :, 0] & 14) | (own[0, 0] & 1); w[3] = w[3] & 62; w[3, :, 0] = w[3, :, 0] | 1
    p = rng.integers(0, W, (N, 8, L)); p[1] = 1 + np.argsort(rng.random((8, W - 2)), axis=1)[:, :L]
    p[:, :, 0] = 0; p[:, :, L - 1] = W - 1; p[3] = p[3] | 1
    n0 = n[0]; n = np.repeat(p[:, :, None, :], 16, axis=2); n[0] = np.where(rng.random((8, 1, L)) < 0.5, n0, n[0])
    j = rng.choice(np.array([0, A - 1, A, B - 1, B, 15, 16]), (N, 8, L))
    j[1] = np.where(j[1] == 16, 15, j[1]); j[2] = 16; j[3] = np.where(j[3] == 16, 0, j[3]); j[3, 7, L - 1] = 16
    c = keys(x, w, p)[:, :, None, :]; rows = np.arange(16)[None, None, :, None]; jj = j[:, :, None, :]
    off = rng.integers(1, 64, m.shape); off[3] = 2 * rng.integers(1, 32, off[3].shape)
    m = np.where((rows == jj) | ((rows > jj) & (rng.random(m.shape) < 0.2)), c, (c + off) & 63)
    m[1, :, :, 1] = c[1, :, :, 1]
    s = rng.integers(0, 5, u.shape); u = np.where(s == 0, 0, np.where(s == 1, W - 1, np.where(s == 2, p[:, :, None, :], u)))
    s = rng.integers(0, 4, o.shape); o = np.where(s == 0, 0, np.where(s == 1, W - 1, np.where(s == 2, p, o)))
    u[1, :, :, 1] = rng.integers(1, W - 1, (8, 16)); u[1, :, :, L - 1] = rng.integers(1, W - 1, (8, 16))
    z = np.take_along_axis(x[1], p[1][:, None, :], 2)
    q[1, 6] = z[6]; q[1, 7] = np.where(z[7] >= 8, 0, 15); u[1, 6, 0, 0] = W - 1; o[1, 6, 0] = 0
    return pack(x, d, m, u, n, q, o, w)
def setup_inputs_ends(rng):
    x, d, m, u, n, q, o, w = parts(rng)
    x = 15 * (rng.random((N, 8, 16, W)) < rng.choice(np.array([0.0, 0.3, 0.5, 0.5, 0.7, 1.0]), (N, 8, 1, W))).astype(np.int64)
    for g in range(8):
        x[:, g, :, 0] = 15 * (g & 1); x[:, g, :, W - 1] = 15 * (g & 1)
        x[:, g, :, W - 2] = 15 * (g & 1); x[:, g, 15, W - 2] = 15 - 15 * (g & 1)
    w = 63 * rng.integers(0, 2, w.shape); w[:, 6:] = 63; w[:, 0] = 0
    q = 15 * rng.integers(0, 2, q.shape)
    d = np.where(rng.random(d.shape) < 0.7, (W - 1) * rng.integers(0, 2, d.shape), d)
    n = np.where(rng.random(n.shape) < 0.7, (W - 1) * rng.integers(0, 2, n.shape), n)
    u = np.where(rng.random(u.shape) < 0.7, (W - 1) * rng.integers(0, 2, u.shape), u)
    o = np.where(rng.random(o.shape) < 0.75, (W - 1) * rng.integers(0, 2, o.shape), o)
    m = np.where(rng.random(m.shape) < 0.7, 63 * rng.integers(0, 2, m.shape), (49 * rng.integers(0, 17, m.shape)) & 63)
    for l in (0, 1, 2, 3, L - 4, L - 3, L - 2, L - 1): n[:, :, 0::2, l] = W - 1; n[:, :, 1::2, l] = 0
    for l, k in ((2, 1), (3, 13), (L - 4, 1), (L - 3, 13)): n[:, :, k, l] = W - 2; n[:, :, 14, l] = W - 2
    for g in range(8):
        for l in (1, 2, 3, L - 4, L - 3, L - 1): q[:, g, :, l] = 15 - 15 * (g & 1)
        for l in (0, L - 2): q[:, g, :, l] = 15 * (g & 1)
    kk = keys(x, w, np.full((N, 8, 1), W - 1))
    m[:, :, 12:, L - 1] = 63; u[:, :, 12:, L - 1] = W - 1
    m[:, :, 11, 1] = kk[:, :, 0]; m[:, :, 11, L - 1] = kk[:, :, 0]
    h = W // FO
    d[:, 7, 15, h - 1::h] = W - 1; d[:, 7, 15, h - 2::h] = W - 1; d[:, :, 0, 0::h] = 0
    return pack(x, d, m, u, n, q, o, w)
def setup_inputs_shared(rng):
    x, d, m, u, n, q, o, w = parts(rng)
    hot = np.stack([np.concatenate([np.array([0, W - 1]), 1 + rng.permutation(W - 2)[:22]]) for g in range(8)])
    gg = np.arange(8)[None, :, None, None]
    d = hot[gg, rng.integers(0, 24, d.shape)]; n = hot[gg, rng.integers(0, 24, n.shape)]
    u = np.where(rng.random(u.shape) < 0.5, hot[gg, rng.integers(0, 24, u.shape)], u)
    kh = keys(x, w, np.repeat(hot[None], N, axis=0))
    m = np.where(rng.random(m.shape) < 0.6, kh[np.arange(N)[:, None, None, None], gg, rng.integers(0, 24, m.shape)], m)
    for r, g, i in ((0, 0, 2), (N - 1, 7, 1)):
        n[r, g] = hot[g, i]; m[r, g, 0] = kh[r, g, i]; u[r, g, 0, 0] = hot[g, 3]
    return pack(x, d, m, u, n, q, o, w)
def setup_inputs_spread(rng):
    x, d, m, u, n, q, o, w = parts(rng)
    def uneven(top, shape, kshape):
        return np.minimum((top * rng.random(shape) ** np.exp2(rng.integers(-2, 3, kshape))).astype(np.int64), top - 1)
    x = uneven(16, x.shape, (N, 8, 1, W)); q = uneven(16, q.shape, (N, 8, 1, L)); d = uneven(W, d.shape, (N, 8, 16, 1))
    u = uneven(W, u.shape, (N, 8, 1, L)); n = uneven(W, n.shape, (N, 8, 16, 1)); o = uneven(W, o.shape, (N, 8, 1)); w = uneven(64, w.shape, (N, 8, 1))
    m = m & rng.choice(np.array([63, 63, 7, 56, 1]), (N, 8, 1, L))
    return pack(x, d, m, u, n, q, o, w)
def setup_inputs_ties(rng):
    x, d, m, u, n, q, o, w = parts(rng); h = W // 2
    x[..., h:] = x[..., :h][..., ::-1]
    p = rng.integers(0, W, (N, 8, L)); p[:, :, L - 1] = W - 1
    z = np.take_along_axis(x, p[:, :, None, :], 3); tot = TH + rng.integers(-1, 2, (N, 8, 1, L))
    dl = (tot >> 4) + (np.arange(16)[None, None, :, None] < (tot & 15))
    q = np.where(z >= 8, z - dl, z + dl)
    twin = np.where(rng.random(n.shape) < 0.5, p[:, :, None, :], W - 1 - p[:, :, None, :])
    n = np.where(rng.random(n.shape) < 0.6, twin, n)
    c = keys(x, w, p)[:, :, None, :]
    m = np.where(rng.random((N, 8, 1, L)) < 0.4, (c + (m & 3)) & 63, m)
    return pack(x, d, m, u, n, q, o, w)
def check_inputs(d):
    bad = []
    for k, lo, hi in (("feat", 0, 15), ("kids", 0, W - 1), ("mkey", 0, 63), ("mobj", 0, W - 1), ("cand", 0, W - 1), ("want", 0, 15), ("last", 0, W - 1), ("wts", 0, 63)):
        v = np.asarray(d[k]).astype(np.float64)
        if not (np.min(v) >= lo and np.max(v) <= hi and np.all(v == np.rint(v))): bad.append("range of " + k)
    return bad
def reference(feat, kids, mkey, mobj, cand, want, last, wts):
    x = np.ascontiguousarray(feat.astype(np.int32).reshape(N, 8, 16, W).transpose(0, 1, 3, 2))
    d = np.array(kids.astype(np.int64).reshape(N, 8, 16, W).transpose(0, 1, 3, 2))
    m = np.array(mkey.astype(np.int64).reshape(N, 8, 16, L).transpose(0, 1, 3, 2))
    u = np.array(mobj.astype(np.int64).reshape(N, 8, 16, L).transpose(0, 1, 3, 2))
    n = np.stack([gentries(a) for a in cand]).astype(np.int64).reshape(N, 8, L, 16)
    q = np.array(want.astype(np.int32).reshape(N, 8, 16, L).transpose(0, 1, 3, 2))
    prev = np.array(last.astype(np.int64)); w = wts.astype(np.int64).reshape(N, 8, 1, 16)
    count = np.zeros(N, np.int64); gi = np.arange(8)[:, None]
    for t in range(T):
        seen = np.zeros(N, np.int64)
        for r in range(N):
            s = (r + t) % N
            dist = np.add.reduce(np.abs(x[s][gi[:, :, None], n[r]] - q[r][:, :, None, :]), axis=3)
            like = dist < TH + (count[s] & 15); alike = np.any(like, axis=2)
            k = np.where(alike, np.argmax(like, axis=2), np.argmin(dist, axis=2))
            o = np.take_along_axis(n[r], k[:, :, None], 2)[:, :, 0]
            xo = x[s][gi, o]; c = np.add.reduce(xo * w[s], axis=2) & 63
            hit = m[s] == c[:, :, None]; covered = np.any(hit, axis=2); j = np.argmax(hit, axis=2)
            own = d[s][gi, o]; e = d[s][gi, np.take_along_axis(u[s], j[:, :, None], 2)[:, :, 0]]
            top = covered & (j < B); low = covered & ((j < A) | (j >= B))
            new = np.concatenate([np.where(top[:, :, None], e[:, :, :8], own[:, :, :8]), np.where(low[:, :, None], e[:, :, 8:], own[:, :, 8:])], axis=2)
            g, l = np.nonzero(covered); first = np.unique(g * W + o[g, l], return_index=True)[1]
            g, l = g[first], l[first]; d[s, g, o[g, l]] = new[g, l]
            g, l = np.nonzero(~alike); row = (l + 5 * t) & 15
            m[s, g, l, row] = c[g, l]; u[s, g, l, row] = prev[r, g, l]
            seen[s] = np.count_nonzero(covered); prev[r] = o; n[r] = new; q[r] = np.abs(q[r] - xo)
        count = seen
    dd = d.transpose(0, 1, 3, 2).reshape(N, 128, FO, W // FO)
    return {"yn": n.transpose(0, 1, 3, 2).reshape(N, 128, L).astype(np.float32), "ymu": (64 * u + m).transpose(0, 1, 3, 2).reshape(N, 128, L).astype(np.float32),
            "yd": np.add.reduce(dd * np.arange(1, FO + 1)[:, None], axis=2).astype(np.float32)}

@@ -1,0 +1,640 @@
+from concourse.mybir import AluOpType, AxisListType, ActivationFunctionType
+
+W, L, STEPS = 3072, 256, 6
+MAGIC = 12582912.0
+SCH = (184, 256)
+VCH = [(0, 64), (64, 128), (128, 184)]
+NVL = SCH[0]
+BIG = 1000000.0
+
+SCRATCH = {}
+
+
+def _buffers():
+    for dtype, names in (
+        ("float32", "colf 256 cmf 256 cgf 128 pcol 40 m16 16 w16 16 ct1 128 ct2 128 onef 128 rst 256 dump 16 "
+                    "t64 64 t64b 64 t64c 64 tba 48 tbb 64 kc 256 comp 256 tr 256 sc 256 r16 16 ka 256 kb 256 new 256 ctv 16 cs 1 "
+                    "lim 2 odm 16 wt1 16 my 256 yl 256 ydb 1536"),
+        ("bfloat16", "featb 3072 keytab 3072 ntab 3072 tb 3072 mk 256 ident 128 nident 128 selp 144 blk 128 nblk 128 sumb 144 tri 128 onesg 240 wr 256 "
+                     "blk8 8 pre 128 rs 128 nbias 128 oneb 512 kwf 128 wx 4096 d 4096 da 4096 fs 2048 ck 256 "
+                     "hit 256 fi 256 sel 256 nsel 256 xo 256 code 256 lo 256 eq 3072 nus 256 mt1 256"),
+        ("float16", "last16 256 i16 128 back 128 sumf 144 sper 512 g8 144 rot 768 ej 2048 od 32 fe 256 pv 16 nap 32 nr 32 mt2 256"),
+        ("int32", "candi 256 kt 3328 mobi 256 lasti 256 wti 1 pint 16 cint 2"),
+        ("uint16", "el 16 wo 16"),
+    ):
+        words = names.split()
+        for k in range(0, len(words), 2):
+            SCRATCH[words[k]] = ("sbuf", [128, int(words[k + 1])], dtype)
+    for t in range(STEPS):
+        SCRATCH["cw%d" % t] = ("sbuf", [128, 272], "uint16")
+        SCRATCH["co%d" % t] = ("sbuf", [128, 272], "uint16")
+        SCRATCH["wt_%d" % t] = ("sbuf", [128, 256], "bfloat16")
+        if t < STEPS - 1:
+            SCRATCH["wn%d" % t] = ("sbuf", [128, 256], "bfloat16")
+    for b in range(8):
+        SCRATCH["b%d" % b] = ("psum", [128, 512], "float32")
+
+
+_buffers()
+LOADS = ["cand", "feat0", "feat1", "feat2", "want", "wts", "last", "mkey", "mobj", "kids"]
+SEMAPHORES = ["sv", "ss", "sp", "sg", "lsem", "arry", "oyn", "omu"] + ["ld_" + x for x in LOADS] + ["oyd%d" % k for k in range(3)]
+SEMAPHORES += ["arrw%d" % k for k in range(1, STEPS)] + ["arrc%d" % k for k in range(1, STEPS)]
+
+
+def A(name, c0, c1, step=1, p0=0, p1=128):
+    return (name, p0, p1, c0, c1, step)
+
+
+def overlap(a, b):
+    if a[1] >= b[2] or b[1] >= a[2] or a[3] >= b[4] or b[3] >= a[4]:
+        return False
+    if a[5] > 1 and a[5] == b[5] and (a[3] - b[3]) % a[5]:
+        return False
+    return True
+
+
+def covers(a, b):
+    return a[5] == 1 and a[1] <= b[1] and a[2] >= b[2] and a[3] <= b[3] and a[4] >= b[4]
+
+
+def machine(g, T):
+    q = {"V": g.vector, "S": g.scalar, "P": g.tensor, "G": g, "Y": g.sync}
+    sem = {"V": "sv", "S": "ss", "P": "sp", "G": "sg"}
+    count = {}
+    clock = {e: {} for e in q}
+    hist = {}
+
+    def need(e, ent):
+        s, v, ck = ent[3], ent[4], ent[5]
+        mine = clock[e]
+        if mine.get(s, 0) < v:
+            q[e].wait_ge(T.sem[s], v)
+            for k in ck:
+                if mine.get(k, 0) < ck[k]:
+                    mine[k] = ck[k]
+            if mine.get(s, 0) < v:
+                mine[s] = v
+
+    def order(e, R, Wr):
+        found = []
+        for regs, w in ((R, False), (Wr, True)):
+            for r in regs:
+                psum = r[0][0] == "b" and r[0][1:].isdigit()
+                for ent in hist.get(r[0], []):
+                    if (psum and ent[2] != e) or ((w or ent[1]) and overlap(r, ent[0])):
+                        found.append(ent)
+        found.sort(key=lambda ent: -ent[4])
+        for ent in found:
+            need(e, ent)
+
+    def log(e, R, Wr, s, v):
+        ck = dict(clock[e])
+        for regs, w in ((R, False), (Wr, True)):
+            for r in regs:
+                h = hist.setdefault(r[0], [])
+                if w:
+                    h[:] = [x for x in h if not covers(r, x[0])]
+                h[:] = [x for x in h if not (x[2] == e and x[3] == s and x[0] == r and x[1] == w)]
+                h.append([r, w, e, s, v, ck])
+
+    def ap(x):
+        if x[0] == "ind":
+            return ap(x[1]).indirect(ap(x[2]))
+        t = T[x[0]]
+        if x[5] == 1:
+            return t[x[1]:x[2], x[3]:x[4]]
+        return t[x[1]:x[2], x[3]:x[4]:x[5]]
+
+    def run(e, call, R, Wr, acc=False):
+        R2, W2 = [], []
+        for x in R:
+            if isinstance(x, tuple):
+                R2 += [x[1], x[2]] if x[0] == "ind" else [x]
+        for x in Wr:
+            if x[0] == "ind":
+                W2.append(x[1])
+                R2.append(x[2])
+            else:
+                W2.append(x)
+        order(e, R2, [] if acc else W2)
+        if acc:
+            for x in W2:
+                for ent in hist.get(x[0], []):
+                    if ent[2] != e:
+                        need(e, ent)
+        s = sem[e]
+        count[s] = count.get(s, 0) + 1
+        call().then_inc(T.sem[s], 1)
+        log(e, R2, W2, s, count[s])
+
+    def sc(x):
+        return ap(x) if isinstance(x, tuple) else x
+
+    def tt(out, a, b, op):
+        run("V", lambda: g.vector.tensor_tensor(ap(out), ap(a), ap(b), op), [a, b], [out])
+
+    def ts(out, a, s1, op0, s2=None, op1=None):
+        if op1 is None:
+            run("V", lambda: g.vector.tensor_scalar(ap(out), ap(a), sc(s1), None, op0), [a, s1], [out])
+        else:
+            run("V", lambda: g.vector.tensor_scalar(ap(out), ap(a), sc(s1), sc(s2), op0, op1), [a, s1, s2], [out])
+
+    def cp(out, a):
+        run("V", lambda: g.vector.tensor_copy(ap(out), ap(a)), [a], [out])
+
+    def fill(out, c):
+        run("V", lambda: g.vector.memset(ap(out), c), [], [out])
+
+    def red(out, a):
+        run("V", lambda: g.vector.tensor_reduce(ap(out), ap(a), AxisListType.X, AluOpType.add), [a], [out])
+
+    def scan(out, d0, d1, init, op0, op1):
+        run("V", lambda: g.vector.tensor_tensor_scan(ap(out), ap(d0), ap(d1), init, op0, op1), [d0, d1], [out])
+
+    def tr(out, a):
+        run("V", lambda: g.vector.transpose(ap(out), ap(a)), [a], [out])
+
+    def act(out, a, func, bias=0.0, scale=1.0, acc=None):
+        if acc is None:
+            run("S", lambda: g.scalar.activation(ap(out), ap(a), func, bias=sc(bias), scale=sc(scale)), [a, bias, scale], [out])
+        else:
+            run("S", lambda: g.scalar.activation(ap(out), ap(a), func, bias=sc(bias), scale=sc(scale), accum_out=ap(acc)),
+                [a, bias, scale], [out, acc])
+
+    def mm(out, lhsT, rhs, start=True, stop=True):
+        run("P", lambda: g.tensor.matmul(ap(out), ap(lhsT), ap(rhs), start, stop), [lhsT, rhs], [out], acc=not start)
+
+    def iota(out, pattern, base, cm, small=True):
+        if small:
+            run("G", lambda: g.iota(ap(out), pattern, base, cm, allow_small_or_imprecise_dtypes=True), [], [out])
+        else:
+            run("G", lambda: g.iota(ap(out), pattern, base, cm), [], [out])
+
+    def pick(out, a, op, base, cm, step, n):
+        run("G", lambda: g.affine_select(ap(out), ap(a), [[step, n]], op, 0.0, base, cm), [a], [out])
+
+    def pick2(out, a, pattern):
+        run("G", lambda: g.affine_select(ap(out), ap(a), pattern, AluOpType.is_equal, 0.0, 0, 0), [a], [out])
+
+    def load(e, out, src, s):
+        q[e].dma_start(ap(out), src).then_inc(T.sem[s], 16)
+        hist.setdefault(out[0], []).append([out, True, "D", s, 16, {}])
+
+    def store(e, dst, a, s):
+        order(e, [a], [])
+        q[e].dma_start(dst, ap(a)).then_inc(T.sem[s], 16)
+        count[s] = 16
+
+    def landed(out, s, v):
+        hist.setdefault(out[0], []).append([out, True, "R", s, v, {}])
+
+    def send(a, out, s, addr, mask, n):
+        order("G", [a], [])
+        g.remote_dma(ap(out), ap(a), T.sem[s], T.sem["lsem"], addr[1], addr[0], mask)
+        count["lsem"] = count.get("lsem", 0) + n
+
+    def finish(extra):
+        for s, v in list(count.items()) + extra:
+            if clock["G"].get(s, 0) < v:
+                g.wait_ge(T.sem[s], v)
+
+    return dict(tt=tt, ts=ts, cp=cp, fill=fill, red=red, scan=scan, tr=tr, act=act, mm=mm, iota=iota, pick=pick, pick2=pick2, load=load,
+                store=store, landed=landed, send=send, finish=finish)
+
+
+def rank_program(g, core, T, topo):
+    rank = T.rank_of(core)
+    if rank is None:
+        return
+    O, F = AluOpType, ActivationFunctionType
+    m = machine(g, T)
+    tt, ts, cp, fill, red, scan, tr, act, mm, iota, pick = (
+        m[k] for k in ("tt", "ts", "cp", "fill", "red", "scan", "tr", "act", "mm", "iota", "pick"))
+    n = len(T.cores)
+    nxt, home = T.cores[(rank + 1) % n], T.cores[(rank - STEPS + 1) % n]
+
+    def link(dst):
+        return topo.addr(dst), topo.mask(core, dst), len(topo.engines(core, dst))
+
+    def full(name, w=128):
+        return A(name, 0, w)
+
+    load = m["load"]
+    load("S", full("wti", 1), T.wts[:, :], "ld_wts")
+    load("Y", full("candi", 256), T.cand[:, :], "ld_cand")
+    load("S", full("wt_0", 256), T.want[:, :], "ld_want")
+    for k in range(3):
+        load("Y", A("featb", 1024 * k, 1024 * k + 1024), T.feat[:, 1024 * k:1024 * k + 1024], "ld_feat%d" % k)
+    load("S", A("lasti", 0, 256, 1, 0, 8), T.last[:, :], "ld_last")
+    load("S", full("mk", 256), T.mkey[:, :], "ld_mkey")
+    load("S", full("mobi", 256), T.mobj[:, :], "ld_mobj")
+    load("Y", A("kt", 0, W), T.kids[:, :], "ld_kids")
+
+    iota(full("pint", 1), [[0, 1]], 0, 1, False)
+    iota(full("cgf", 128), [[1, 8], [0, 16]], 0, 0)
+    iota(full("colf", 256), [[1, 256]], 0, 0)
+    iota(full("oneb", 128), [[0, 128]], 1, 0)
+    pick(full("ident"), full("oneb"), O.is_equal, 0, 1, -1, 128)
+    iota(full("cmf", 256), [[0, 16], [1, 16]], 0, 0)
+    iota(A("oneb", 128, 256), [[0, 128]], -1, 0)
+    pick(full("nident"), A("oneb", 128, 256), O.is_equal, 0, 1, -1, 128)
+    iota(A("oneb", 256, 384), [[0, 128]], -16, 0)
+    pick(full("tri"), A("oneb", 256, 384), O.is_ge, 0, 1, -1, 128)
+
+    iota(full("sc", 256), [[0, 256]], int(BIG), 0)
+    m["pick2"](full("rst", 256), full("sc", 256), [[0, 16], [1, 16]])
+    iota(full("onef"), [[0, 128]], 1, 0)
+    iota(full("onesg", 240), [[0, 240]], 1, 0)
+    pick(full("onesg", 240), full("onesg", 240), O.is_ge, -112, 0, 1, 240)
+    pick(full("onesg", 240), full("onesg", 240), O.is_ge, 127, 0, -1, 240)
+    iota(A("kt", W, W + L), [[0, 256]], 0, 0, False)
+
+    def pi(k):
+        return A("pint", k, k + 1)
+
+    def pc(k):
+        return A("pcol", k, k + 1)
+    PF, PM, PG, P16, P1615, HA, HB, PP16, PM16, KCOL, CA, CB, PARE, PARO, BS, MA, MB, WF, WF64, G15 = range(20)
+    PR = 24
+    ts(pi(2), pi(0), 4, O.arith_shift_right)
+    ts(pi(1), pi(0), 15, O.bitwise_and)
+    cp(pc(PG), pi(2))
+    cp(pc(PM), pi(1))
+    cp(pc(PF), pi(0))
+    ts(full("blk"), full("cgf"), pc(PG), O.is_equal, 1.0, O.mult)
+    ts(pc(P1615), pc(PG), 16.0, O.mult, 15.0, O.add)
+    ts(full("selp", 143), full("colf", 143), pc(P1615), O.is_equal, 16.0, O.mult)
+
+    def build_wx(t):
+        for k in range(16):
+            out, src = A("wx", k, 16 * NVL, 16), A("wt_%d" % t, 0, NVL)
+            if t and k >= 16 - GWX:
+                pick(out, src, O.is_ge, 1, 0, 0, NVL)
+            else:
+                cp(out, src)
+
+    def key_a(k):
+        b, c, x, z = A("b%d" % k, 0, 512), A("featb", 512 * k, 512 * k + 512), A("ntab", 512 * k, 512 * k + 512), A("kf", 512 * k, 512 * k + 512)
+        if k < 3:
+            mm(b, full("kwf"), c)
+            act(z, b, F.Copy, bias=-31.5)
+        else:
+            z = b
+            mm(b, full("kwf"), c, True, False)
+            mm(b, A("nbias", 0, 128, 1, 0, 1), A("nbone", 0, 512, 1, 0, 1), False, True)
+        ts(x, z, 64.0 * MAGIC, O.add, 64.0 * MAGIC, O.subtract)
+
+    def key_b(k):
+        b, c, x = A("b%d" % k, 0, 512), A("featb", 512 * k, 512 * k + 512), A("ntab", 512 * k, 512 * k + 512)
+        mm(b, full("kwf"), c, True, False)
+        mm(b, full("nident"), x, False, True)
+        act(A("keytab", 512 * k, 512 * k + 512), b, F.Copy)
+
+    def consts1():
+        ts(pc(KCOL), pc(PM), 0.625, O.add)
+        fill(A("lim", 0, 1), -1008.0)
+        ts(pi(3), pi(0), 16, O.bitwise_and)
+        ts(pc(PP16), pc(PF), 16.0, O.add)
+        ts(pc(PM16), pc(PF), -16.0, O.add)
+        ts(pc(HB), pi(3), 256.0, O.mult)
+        ts(pc(HA), pc(HB), -1.0, O.mult, 4096.0, O.add)
+        ts(A("sper", 256, 384), full("colf"), pc(PM16), O.is_equal, pc(HB), O.mult)
+        ts(A("sper", 384, 512), full("colf"), pc(PF), O.is_equal, pc(HB), O.mult)
+        ts(A("sper", 0, 128), full("colf"), pc(PF), O.is_equal, pc(HA), O.mult)
+        ts(A("sper", 128, 256), full("colf"), pc(PP16), O.is_equal, pc(HA), O.mult)
+
+    def consts_bits():
+        ts(full("m16", 16), full("colf", 16), pc(PM), O.is_equal, 1.0, O.mult)
+        fill(full("t64c", 16), 0.5)
+        fill(full("t64b", 16), 0.0)
+        scan(full("w16", 16), full("t64c", 16), full("t64b", 16), 1.0, O.mult, O.add)
+        tt(full("w16", 16), full("m16", 16), full("w16", 16), O.mult)
+        ts(pc(MB), pc(PM), 6.0, O.is_lt)
+        ts(pc(CA), pc(PM), 12.0, O.is_lt)
+        red(pc(BS), full("w16", 16))
+        tt(pc(MA), pc(CA), pc(MB), O.subtract)
+        for mul, k, out, mask in ((64.0, 48, "tba", MA), (1.0, 64, "tbb", MB)):
+            ts(full("t64", k), full("colf", k), mul, O.mult, 0.5, O.add)
+            ts(full("t64", k), full("t64", k), pc(BS), O.mult)
+            ts(full("t64b", k), full("t64", k), MAGIC, O.add, MAGIC, O.subtract)
+            tt(full("t64c", k), full("t64", k), full("t64b", k), O.subtract)
+            ts(full("t64c", k), full("t64c", k), 0.0, O.is_gt, 2.0, O.mult)
+            ts(full(out, k), full("t64c", k), -1.0, O.add, pc(mask), O.mult)
+
+    def bit_table(k0, k1):
+        for k in range(k0, k1):
+            act(A("tb", 64 * k, 64 * k + 64), full("tbb", 64), F.Identity, bias=A("tba", k, k + 1))
+
+    def consts2():
+        ts(full("ct1"), A("cmf", 0, 128), pc(PM), O.is_gt, 2.0, O.mult)
+        ts(full("ct2"), A("cmf", 0, 128), pc(PM), O.is_equal, 1.0, O.mult)
+        ts(pc(CA), pc(PM), 11.0, O.is_lt)
+        tt(full("ct1"), full("ct1"), full("ct2"), O.subtract)
+        ts(pc(CB), pc(PM), 6.0, O.is_lt)
+        tt(full("pre"), full("ct1"), full("blk"), O.mult)
+        ts(full("sumf", 143), full("colf", 143), pc(P1615), O.is_equal, 1.0, O.mult)
+        tt(pc(CB), pc(CB), pc(CA), O.subtract)
+        ts(A("b7", 0, 256), full("mobi", 256), -1536.0, O.add)
+        ts(pc(CB), pc(CB), 1.0, O.add)
+        ts(full("ct1"), A("cmf", 0, 128), 8.0, O.is_lt)
+        tt(pc(CA), pc(CA), pc(CB), O.subtract)
+        ts(full("ct2"), full("ct1"), pc(CA), O.mult, pc(CB), O.add)
+        ts(full("blk8", 8), full("colf", 8), pc(PG), O.is_equal, 1.0, O.mult)
+        ts(pi(4), pi(2), 1, O.bitwise_and)
+        tt(full("rs"), full("ct2"), full("blk"), O.mult)
+        ts(pc(PARO), pi(4), 1.0, O.mult)
+        ts(pc(PARE), pc(PARO), -1.0, O.mult, 1.0, O.add)
+
+    def consts3():
+        ts(full("dump", 16), full("colf", 16), 16.0, O.mult, pc(PM), O.add)
+        ts(full("dump", 16), full("dump", 16), 1536.0, O.add)
+        ts(A("last16", 0, 256, 1, 0, 8), A("lasti", 0, 256, 1, 0, 8), -1536.0, O.add)
+        ts(pc(G15), pc(PF), 16.0, O.mult, 15.0, O.add)
+        ts(A("g8", 0, 143, 1, 0, 8), A("colf", 0, 143, 1, 0, 8), A("pcol", G15, G15 + 1, 1, 0, 8), O.is_equal, 1.0, O.mult)
+        for k in range(16):
+            mm(A("b6", 96, 112), A("g8", 15 - k, 143 - k, 1, 0, 8), A("last16", k, 256, 16, 0, 8), k == 0, k == 15)
+        cp(full("pv", 16), A("b6", 96, 112))
+        ts(pc(P16), pc(PG), 16.0, O.mult)
+
+    def consts_ej():
+        ts(full("i16"), full("colf"), pc(PF), O.is_equal, 1.0, O.mult)
+        for k in range(16):
+            ts(A("ej", 128 * k, 128 * k + 128), full("i16"), A("m16", k, k + 1), O.mult)
+
+    def const_rot(t):
+        if t == 0:
+            ts(pi(5), pi(1), 11.0, O.add)
+            ts(pi(6), pi(5), 15, O.bitwise_and)
+            tt(pc(PR), pi(6), pc(P16), O.add)
+            ts(A("rot", 0, 128), full("colf"), pc(PF), O.is_equal, 1.0, O.mult)
+            ts(full("back"), full("colf"), pc(PR), O.is_equal, 1.0, O.mult)
+        else:
+            mm(A("b4", 256, 384), full("back"), A("rot", 128 * t - 128, 128 * t))
+            cp(A("rot", 128 * t, 128 * t + 128), A("b4", 256, 384))
+
+    consts_bits()
+    ts(pc(WF), full("wti", 1), 1.0, O.mult)
+    ts(full("kwf"), full("blk"), pc(WF), O.mult)
+    cp(A("cw0", 0, 256), full("candi", 256))
+    build_wx(0)
+    consts1()
+    fill(A("nbias", 0, 128, 1, 0, 1), -31.5)
+    fill(A("nbone", 0, 512, 1, 0, 1), 1.0)
+
+    def keytable(k0, k1):
+        for k in range(k0, k1):
+            if k < 6:
+                key_a(k)
+            if k:
+                key_b(k - 1)
+    key_a(0)
+    key_a(1)
+    bit_table(0, 26)
+    act(full("nblk"), full("blk"), F.Copy, scale=-1.0)
+    act(full("sumb", 143), full("selp", 143), F.Copy, scale=1.0 / 16.0)
+    consts_ej()
+    key_b(0)
+    keytable(2, KEY0)
+    FEAT, KEYS, BITS = full("featb", W), full("keytab", W), full("tb", W)
+    KIDS, KALL = A("kt", 0, W), A("kt", 0, W + L)
+    late = {}
+
+    def dist_to(l0, l1):
+        return A("b4", l0, l1) if l1 <= 128 else A("b5", l0 - 128, l1 - 128)
+
+    for t in range(STEPS):
+        cw, wt, co = "cw%d" % t, "wt_%d" % t, "co%d" % t
+        final = t == STEPS - 1
+        OL = A(co, 256, 272)
+        s0, s1 = SCH
+        sw = s1 - s0
+        kb = 512 // sw
+        act(A("fs", 0, 16 * sw), ("ind", FEAT, A(cw, s0, s1)), F.Copy)
+        for l0, l1 in VCH:
+            r = A("d", 16 * l0, 16 * l1)
+            tt(r, ("ind", FEAT, A(cw, l0, l1)), A("wx", 16 * l0, 16 * l1), O.subtract)
+            if t == 0 and l0 == 0:
+                keytable(KEY0, 7)
+        if t:
+            late["w"]()
+
+        def abs_v(l0, l1):
+            act(A("da", 16 * l0, 16 * l1), A("d", 16 * l0, 16 * l1), F.Abs)
+            for k in range(16):
+                mm(dist_to(l0, l1), A("selp", 15 - k, 143 - k), A("da", 16 * l0 + k, 16 * l1, 16), k == 0, k == 15)
+        for k in range(16):
+            c = A("b%d" % (k // kb), (k % kb) * sw, (k % kb) * sw + sw)
+            mm(c, full("nident"), A(wt, s0, s1), True, False)
+            mm(c, full("ident"), A("fs", k, 16 * sw, 16), False, True)
+        abs_v(*VCH[0])
+        if t:
+            late["wl"]()
+            const_rot(t)
+        steps = late["wo"]() if t else iter(())
+        next(steps, None)
+        ts(full("kc", 256), A(cw, 0, 256), 1.0 / 4096.0, O.mult, pc(KCOL), O.add)
+        next(steps, None)
+        if t:
+            ts(full("pv", 16), A(cw, 256, 272), -1536.0, O.add)
+        next(steps, None)
+        for k in range(0, 16, kb):
+            e = min(k + kb, 16)
+            act(A("da", 16 * s0 + sw * k, 16 * s0 + sw * e), A("b%d" % (k // kb), 0, sw * (e - k)), F.Abs)
+        for k in range(16):
+            mm(dist_to(s0, s1), A("selp", 15 - k, 143 - k), A("da", 16 * s0 + sw * k, 16 * s0 + sw * k + sw), k == 0, k == 15)
+        if t:
+            late["scatter"]()
+        for c in VCH[1:]:
+            abs_v(*c)
+        act(A("b6", 0, 128), A("b4", 0, 128), F.Relu, bias=A("lim", 0, 1))
+        act(A("b5", 128, 256), A("b5", 0, 128), F.Relu, bias=A("lim", 0, 1))
+        if t == 0:
+            bit_table(26, 48)
+            consts2()
+        if t:
+            late["mount2"]()
+        for h in range(2):
+            a, b = 128 * h, 128 * h + 128
+            tt(A("comp", a, b), A("b5", 128, 256) if h else A("b6", 0, 128), A("kc", a, b), O.add)
+            tr(A("tr", a, b), A("comp", a, b))
+            scan(A("sc", a, b), A("rst", a, b), A("tr", a, b), BIG, O.max, O.min)
+        best = A("sc", 15, 256, 16)
+        ts(full("r16", 16), best, MAGIC, O.add, MAGIC, O.subtract)
+        ts(A("od", 16, 32), best, 16.5, O.is_ge, 1.0 / 4096.0, O.mult)
+        tt(A("od", 0, 16), best, full("r16", 16), O.subtract)
+        for dd in range(2):
+            for bb in range(2):
+                k = 2 * dd + bb
+                mm(A("b6", dd, 32, 2), A("sper", 128 * k, 128 * k + 128), A("od", bb, 32, 2), bb == 0, bb == 1)
+        ts(OL, A("b6", 0, 16), 1536.0, O.add)
+        halves = ((0, 128), (128, 256))
+        for a, b in halves:
+            tt(A("hit", a, b), ("ind", KEYS, A(co, 256 + a // 16, 256 + b // 16)), A("mk", a, b), O.is_equal)
+        if not final:
+            act(full("xo", 256), ("ind", FEAT, OL), F.Copy)
+        act(full("code", 256), ("ind", BITS, OL), F.Copy)
+        for a, b in halves:
+            mm(A("b5" if a == 0 else "b4", 0, 128), full("pre"), A("hit", a, b))
+        for a, b in halves:
+            ts(A("fi", a, b), A("b5" if a == 0 else "b4", 0, 128), 0.0, O.is_lt)
+        if not final:
+            mm(A("b0", 0, 256), full("ident"), A(wt, 0, 256), True, False)
+            mm(A("b0", 0, 256), full("nident"), full("xo", 256), False, True)
+            act(A("wn%d" % t, 0, 256), A("b0", 0, 256), F.Abs)
+            ad, ma, ne = link(nxt)
+            m["send"](A("wn%d" % t, 0, 256), A("wt_%d" % (t + 1), 0, 256), "arrw%d" % (t + 1), ad, ma, ne)
+        for a, b in halves:
+            tt(A("fe", a, b), A("fi", a, b), A("b7", a, b), O.mult)
+        ts(full("lo", 256), full("code", 256), pc(PARO), O.mult)
+        mm(A("b4", 0, 256), full("rs"), full("fi", 256))
+        act(full("nsel", 256), A("b4", 0, 256), F.Copy, bias=1.0, scale=-1.0)
+        act(full("sel", 256), A("b4", 0, 256), F.Copy)
+        for k in range(16):
+            mm(A("b5", 0, 16), A("sumf", 15 - k, 143 - k), A("fe", k, 256, 16), k == 0, k == 15)
+        for h in range(2):
+            mm(A("b1", 8 * h, 8 * h + 8), A("fi", 128 * h, 128 * h + 128), full("blk8", 8))
+        act(full("ctv", 16), A("b1", 0, 16), F.Copy, acc=full("cs", 1))
+        tt(full("ka", 256), ("ind", KIDS, OL), full("nsel", 256), O.mult)
+        ts(full("el", 16), A("b5", 0, 16), 1536.0, O.add)
+
+        def match(gg):
+            b = "b%d" % ((gg + 2) % 4)
+            p0 = 32 * (gg // 2)
+            p1 = p0 + 16 + 16 * (gg % 2)
+            lh = "lo" if gg % 2 else "code"
+            for c0, lp, ln, tri in ((0, 0, 0, True), (128, 0, 128, False), (256, 128, 128, True)):
+                mm(A(b, c0, c0 + 128), A(lh, lp, lp + 128, 1, p0, p1), A("code", ln, ln + 128, 1, p0, p1), True, not tri)
+                if tri:
+                    mm(A(b, c0, c0 + 128), full("ident"), full("tri"), False, True)
+            for h, (c0, c1) in enumerate(((0, 256), (256, 384))):
+                o, cv = A("eq", 384 * gg + c0, 384 * gg + c1), A("ctv", 8 * h + gg, 8 * h + gg + 1)
+                if final and gg % 4 == 3:
+                    ts(o, A(b, c0, c1), 12.0, O.is_equal, cv, O.mult)
+                else:
+                    act(o, A(b, c0, c1), F.Relu, bias=-11.0, scale=cv)
+        act(A("b4", 256, 512), full("ka", 256), F.Copy)
+        match(0)
+        for a, b in halves:
+            tt(A("kb", a, b), ("ind", KIDS, A("el", a // 16, b // 16)), A("sel", a, b), O.mult)
+        for a, b in halves:
+            tt(A("new", a, b), A("kb", a, b), A("b4", 256 + a, 256 + b), O.add)
+        if not final:
+            for a, b in halves:
+                cp(A(co, a, b), A("new", a, b))
+            ad, ma, ne = link(nxt)
+            m["send"](A(co, 0, 272), A("cw%d" % (t + 1), 0, 272), "arrc%d" % (t + 1), ad, ma, ne)
+            m["landed"](A("wt_%d" % (t + 1), 0, 256), "arrw%d" % (t + 1), ne)
+            m["landed"](A("cw%d" % (t + 1), 0, 272), "arrc%d" % (t + 1), ne)
+        else:
+            ad, ma, ne = link(home)
+            m["send"](full("new", 256), full("yl", 256), "arry", ad, ma, ne)
+            m["landed"](full("yl", 256), "arry", ne)
+        for gg in range(1, 8 if final else 4):
+            match(gg)
+        act(full("ck", 256), ("ind", KEYS, OL), F.Copy)
+        if not final:
+            match(4)
+        if t == 0:
+            consts3()
+            const_rot(0)
+        tt(full("odm", 16), A("b6", 0, 16), full("dump", 16), O.subtract)
+        cp(A("nap", 0, 16), A("b6", 16, 32))
+        tt(A("nap", 16, 32), A("b6", 16, 32), full("pv", 16), O.mult)
+        if not final:
+            mm(A("b6", 32, 33), full("onef"), full("cs", 1))
+
+        def writers():
+            for h in range(2):
+                out = A("b3", 128 * h, 128 + 128 * h)
+                for gg in range(8):
+                    lh = A("onesg", 112 - 16 * gg, 240 - 16 * gg)
+                    mm(out, lh, A("eq", 384 * gg + 128 * h, 384 * gg + 128 * h + 128), gg == 0, False)
+                    if h:
+                        mm(out, lh, A("eq", 384 * gg + 256, 384 * gg + 384), False, False)
+                mm(out, full("nblk"), A("fi", 128 * h, 128 * h + 128), False, True)
+
+        def late_w():
+            act(full("wr", 256), A("b3", 0, 256), F.Relu, scale=-1.0 / 16.0)
+
+        def late_wl():
+            for k in range(16):
+                mm(A("b3", 256, 272), A("sumb", 15 - k, 143 - k), A("wr", k, 256, 16), k == 0, k == 15)
+
+        def late_wo():
+            tt(full("wt1", 16), A("b3", 256, 272), full("odm", 16), O.mult)
+            yield
+            tt(full("wt1", 16), full("wt1", 16), full("dump", 16), O.add)
+            yield
+            ts(full("wo", 16), full("wt1", 16), 1536.0, O.add)
+            yield
+
+        def late_scatter(final=final):
+            cp(("ind", A("kf", 0, W + L) if final else KALL, full("wo", 16)), full("new", 256))
+        if final:
+            iota(A("kf", W, W + L), [[0, 256]], 0, 0)
+            cp(full("kf", W), KIDS)
+            writers()
+        mm(A("b6", 64, 96), A("rot", 128 * t, 128 * t + 128), full("nap", 32))
+        cp(full("nr", 32), A("b6", 64, 96))
+        if final:
+            late_w()
+            late_wl()
+            for _ in late_wo():
+                pass
+            late_scatter()
+        if not final:
+            cp(A("cint", 0, 1), A("b6", 32, 33))
+            build_wx(t + 1)
+            ts(A("cint", 1, 2), A("cint", 0, 1), 15, O.bitwise_and)
+        for k in range(16):
+            mm(A("b5", (k - 5 * t) % 16, 256, 16), A("ej", 128 * k, 128 * k + 128), A("nr", 0, 16))
+        if not final:
+            match(5)
+        mm(A("b4", 0, 256), full("ident"), full("ck", 256), True, False)
+        mm(A("b4", 0, 256), full("nident"), full("mk", 256), False, True)
+
+        def late_mount0():
+            tt(full("mt1", 256), full("nus", 256), A("b4", 0, 256), O.mult)
+            tt(full("mt2", 256), full("nus", 256), A("b7", 0, 256), O.mult)
+
+        def late_mount2(final=final, t=t):
+            mm(A("b0", 0, 256), full("ident"), full("ck", 256), True, False)
+            mm(A("b0", 0, 256), full("nident"), full("mt1", 256), False, True)
+            mm(A("b1", 0, 256), full("i16"), full("mt2", 256), True, False)
+            for k in range(16):
+                mm(A("b1", (k - 5 * t) % 16, 256, 16), A("ej", 128 * k, 128 * k + 128), A("nr", 16, 32), False, k == 15)
+            if not final:
+                act(full("mk", 256), A("b0", 0, 256), F.Copy)
+                act(A("b7", 0, 256), A("b1", 0, 256), F.Copy)
+
+        late["w"], late["wl"], late["wo"], late["scatter"], late["mount0"], late["mount2"] = (
+            late_w, late_wl, late_wo, late_scatter, late_mount0, late_mount2)
+        act(full("nus", 256), A("b5", 0, 256), F.Copy, bias=1.0, scale=-1.0)
+        if not final:
+            match(6)
+            match(7)
+            late_mount0()
+            ts(A("lim", 0, 1), A("cint", 1, 2), -16.0, O.mult, -1008.0, O.add)
+            writers()
+
+    m["store"]("Y", T.yn[:, :], full("yl", 256), "oyn")
+    for k in range(3):
+        c0, c1 = 512 * k, 512 * k + 512
+        b = "b%d" % (5 + k % 2)
+        act(A(b, 0, 512), A("kf", 1536 + c0, 1536 + c1), F.Copy, scale=2.0)
+        tt(A("ydb", c0, c1), A("kf", c0, c1), A(b, 0, 512), O.add)
+        m["store"]("Y", T.yd[:, c0:c1], A("ydb", c0, c1), "oyd%d" % k)
+        if k == 0:
+            late["mount0"]()
+            late["mount2"]()
+        if k == 1:
+            act(full("my", 256), A("b1", 0, 256), F.Copy, scale=64.0, bias=98304.0)
+            tt(full("my", 256), full("my", 256), A("b0", 0, 256), O.add)
+            m["store"]("Y", T.ymu[:, :], full("my", 256), "omu")
+    m["finish"]([("arry", link(home)[2])] + [("ld_" + x, 16) for x in LOADS])
+
+
+GWX = 4
+KEY0 = 4
+SCRATCH["nbone"] = ("sbuf", [128, 512], "bfloat16")
+SCRATCH["kf"] = ("sbuf", [128, W + L], "float32")

@@ -1,26 +1,24 @@
-from concourse.mybir import AluOpType, AxisListType, ActivationFunctionType
+from concourse.mybir import AluOpType, ActivationFunctionType
 
 W, L, STEPS = 3072, 256, 6
 MAGIC = 12582912.0
-SCH = (184, 256)
-VCH = [(0, 64), (64, 128), (128, 184)]
-NVL = SCH[0]
-BIG = 1000000.0
+BIG = 4000.0
+Q12 = 1.0 / 4096.0
 
 SCRATCH = {}
 
 
 def _buffers():
     for dtype, names in (
-        ("float32", "colf 256 cmf 256 cgf 128 pcol 40 m16 16 w16 16 ct1 128 ct2 128 onef 128 rst 256 dump 16 "
-                    "t64 64 t64b 64 t64c 64 tba 48 tbb 64 kc 256 comp 256 tr 256 sc 256 r16 16 ka 256 kb 256 new 256 ctv 16 cs 1 "
-                    "lim 2 odm 16 wt1 16 my 256 yl 256 ydb 1536"),
-        ("bfloat16", "featb 3072 keytab 3072 ntab 3072 tb 3072 mk 256 ident 128 nident 128 selp 144 blk 128 nblk 128 sumb 144 tri 128 onesg 240 wr 256 "
-                     "blk8 8 pre 128 rs 128 nbias 128 oneb 512 kwf 128 wx 4096 d 4096 da 4096 fs 2048 ck 256 "
-                     "hit 256 fi 256 sel 256 nsel 256 xo 256 code 256 lo 256 eq 3072 nus 256 mt1 256"),
-        ("float16", "last16 256 i16 128 back 128 sumf 144 sper 512 g8 144 rot 768 ej 2048 od 32 fe 256 pv 16 nap 32 nr 32 mt2 256"),
-        ("int32", "candi 256 kt 3328 mobi 256 lasti 256 wti 1 pint 16 cint 2"),
-        ("uint16", "el 16 wo 16"),
+        ("float32", "colf 144 cmf 256 pcol 32 m16 16 s1 16 s2 16 ct1 128 ct2 128 ct3 128 krow 136 kc 272 sc 272 r8 16 xk 256 nw 256 new 256 "
+                    "rr 288 ds 288 h2 16 u16 16 cs 2 junk 128 my 256 mt 256 yl 256 ydb 1536"),
+        ("bfloat16", "featb 3072 keys 3072 cg 512 expn 512 mk0 256 want0 256 ident 128 nident 128 blk 128 blk16 8 pre 128 kw 128 "
+                     "fs 4096 da 4096 xo 256 hit 256 selc 256"),
+        ("float16", "c16 256 c16o 256 turn 136 ones 128 krow16 136 lim 136 bp 8 bn 8 nb 128 zm 256 zin 288 zz 288 zin2 272 zz2 272 rs 128 "
+                    "crow 592 sumf 144 sj 2304 dsrc 128 dj 2048 i64 128 i16 128 n64 128 rk 3072 me 768 ff 512 oc 16 vc 16 nas 32 sp 64 "
+                    "prev 16 last16 256 g8 144"),
+        ("int32", "candi 256 kt 3088 kf 3088 mobi 256 lasti 256 wti 1 pint 16"),
+        ("uint16", "el 16 wo 32"),
     ):
         words = names.split()
         for k in range(0, len(words), 2):
@@ -36,9 +34,9 @@ def _buffers():
 
 
 _buffers()
-LOADS = ["cand", "feat0", "feat1", "feat2", "want", "wts", "last", "mkey", "mobj", "kids"]
-SEMAPHORES = ["sv", "ss", "sp", "sg", "lsem", "arry", "oyn", "omu"] + ["ld_" + x for x in LOADS] + ["oyd%d" % k for k in range(3)]
-SEMAPHORES += ["arrw%d" % k for k in range(1, STEPS)] + ["arrc%d" % k for k in range(1, STEPS)]
+LOADS = ["cand", "feat0", "feat1", "want", "wts", "last", "mkey", "mobj", "kids", "kf"]
+SEMAPHORES = ["sv", "ss", "sp", "sg", "lsem", "arry0", "arry1", "oyn", "omu"] + ["ld_" + x for x in LOADS] + ["oyd%d" % k for k in range(4)]
+SEMAPHORES += ["arr%s%d%d" % (x, k, h) for x in "wc" for k in range(1, STEPS) for h in range(2)]
 
 
 def A(name, c0, c1, step=1, p0=0, p1=128):
@@ -75,12 +73,14 @@ def machine(g, T):
             if mine.get(s, 0) < v:
                 mine[s] = v
 
-    def order(e, R, Wr):
+    def order(e, R, Wr, others=False):
         found = []
         for regs, w in ((R, False), (Wr, True)):
             for r in regs:
                 psum = r[0][0] == "b" and r[0][1:].isdigit()
                 for ent in hist.get(r[0], []):
+                    if w and others and ent[2] == e:
+                        continue
                     if (psum and ent[2] != e) or ((w or ent[1]) and overlap(r, ent[0])):
                         found.append(ent)
         found.sort(key=lambda ent: -ent[4])
@@ -116,12 +116,7 @@ def machine(g, T):
                 R2.append(x[2])
             else:
                 W2.append(x)
-        order(e, R2, [] if acc else W2)
-        if acc:
-            for x in W2:
-                for ent in hist.get(x[0], []):
-                    if ent[2] != e:
-                        need(e, ent)
+        order(e, R2, W2, acc)
         s = sem[e]
         count[s] = count.get(s, 0) + 1
         call().then_inc(T.sem[s], 1)
@@ -145,14 +140,8 @@ def machine(g, T):
     def fill(out, c):
         run("V", lambda: g.vector.memset(ap(out), c), [], [out])
 
-    def red(out, a):
-        run("V", lambda: g.vector.tensor_reduce(ap(out), ap(a), AxisListType.X, AluOpType.add), [a], [out])
-
     def scan(out, d0, d1, init, op0, op1):
         run("V", lambda: g.vector.tensor_tensor_scan(ap(out), ap(d0), ap(d1), init, op0, op1), [d0, d1], [out])
-
-    def tr(out, a):
-        run("V", lambda: g.vector.transpose(ap(out), ap(a)), [a], [out])
 
     def act(out, a, func, bias=0.0, scale=1.0, acc=None):
         if acc is None:
@@ -170,36 +159,38 @@ def machine(g, T):
         else:
             run("G", lambda: g.iota(ap(out), pattern, base, cm), [], [out])
 
-    def pick(out, a, op, base, cm, step, n):
-        run("G", lambda: g.affine_select(ap(out), ap(a), [[step, n]], op, 0.0, base, cm), [a], [out])
-
-    def pick2(out, a, pattern):
-        run("G", lambda: g.affine_select(ap(out), ap(a), pattern, AluOpType.is_equal, 0.0, 0, 0), [a], [out])
-
     def load(e, out, src, s):
         q[e].dma_start(ap(out), src).then_inc(T.sem[s], 16)
         hist.setdefault(out[0], []).append([out, True, "D", s, 16, {}])
 
-    def store(e, dst, a, s):
-        order(e, [a], [])
-        q[e].dma_start(dst, ap(a)).then_inc(T.sem[s], 16)
-        count[s] = 16
+    def copy(e, out, a, s):
+        order(e, [a], [out])
+        q[e].dma_start(ap(out), ap(a)).then_inc(T.sem[s], 16)
+        hist.setdefault(out[0], []).append([out, True, "D", s, 16, dict(clock[e])])
+        hist.setdefault(a[0], []).append([a, False, "D", s, 16, dict(clock[e])])
 
-    def landed(out, s, v):
-        hist.setdefault(out[0], []).append([out, True, "R", s, v, {}])
+    def store(e, dst, a, s):
+        order(e, a, [])
+        q[e].dma_start(dst, ap(a[0])).then_inc(T.sem[s], 16)
+        count[s] = 16
 
     def send(a, out, s, addr, mask, n):
         order("G", [a], [])
         g.remote_dma(ap(out), ap(a), T.sem[s], T.sem["lsem"], addr[1], addr[0], mask)
         count["lsem"] = count.get("lsem", 0) + n
+        hist.setdefault(out[0], []).append([out, True, "R", s, n, {}])
 
     def finish(extra):
         for s, v in list(count.items()) + extra:
             if clock["G"].get(s, 0) < v:
                 g.wait_ge(T.sem[s], v)
 
-    return dict(tt=tt, ts=ts, cp=cp, fill=fill, red=red, scan=scan, tr=tr, act=act, mm=mm, iota=iota, pick=pick, pick2=pick2, load=load,
-                store=store, landed=landed, send=send, finish=finish)
+    return dict(tt=tt, ts=ts, cp=cp, fill=fill, scan=scan, act=act, mm=mm, iota=iota, load=load, copy=copy, store=store, send=send, finish=finish)
+
+
+ORDER = [
+    'SCAN R NA OD Z pv ZM nz OL HIT nm X ck nas OC G2 ext FI FM c16 FE EM v2 v1 SELC G3 XO KA sub2 cnt kc EL dp sub3 KB abs2 VC dm kcc FIX OUT v0 v3 ds abs3 rnd W dk WABS sub0 sub1 p0 sumb h2 abs0 abs1 suma lim p1 uu dq spread wo', 's G2 s s v1 s G3 SCAN s R v0 OD s Z ZM s sub2 mkc sub3 v2 abs2 s abs3 OL c16 XO sub0 s HIT X kc s kcc v3 sub1 s FI s FE s s FM EM OC s NA p0 s abs1 EL kf SELC KA sumb abs0 VC suma KB FIX OUT p1 W WABS', 'c16 c2 k0 k1 l0 G2 k3 k2 sub2 k5 kc k4 kcc c1 abs2 v0 v3 G3 l1 v1 l2 l3 sub0 v2 sub3 l4 sub1 abs0 l5 abs3 p0 sumb abs1 suma p1', 'v1 G3 v0 SCAN R c16 OD Z G2 sub0 ZM sub2 v3 OL HIT X XO sub3 abs2 OC v2 FI FM kc c3 abs0 W SELC abs3 sub1 abs1 FE EM c4 kcc p0 sumb KA c7 EL VC KB c5 WABS FIX NA OUT suma p1 c6', 'dm0 SCAN NA R OD pv Z ZM OL ck HIT nz nm X FI ds0 FE FM h20 uu0 wo0 ext EM OC SELC nas dk dq VC dm1 EL KA KB ds1 dp spread h21 s uu1 my0 s s s s s s FIX s wo1 s s s OUT my1 my2 s s s yn s s yd1 yd0 yd2 yd3',
+]
 
 
 def rank_program(g, core, T, topo):
@@ -208,8 +199,7 @@ def rank_program(g, core, T, topo):
         return
     O, F = AluOpType, ActivationFunctionType
     m = machine(g, T)
-    tt, ts, cp, fill, red, scan, tr, act, mm, iota, pick = (
-        m[k] for k in ("tt", "ts", "cp", "fill", "red", "scan", "tr", "act", "mm", "iota", "pick"))
+    tt, ts, cp, fill, scan, act, mm, iota = (m[k] for k in ("tt", "ts", "cp", "fill", "scan", "act", "mm", "iota"))
     n = len(T.cores)
     nxt, home = T.cores[(rank + 1) % n], T.cores[(rank - STEPS + 1) % n]
 
@@ -219,422 +209,353 @@ def rank_program(g, core, T, topo):
     def full(name, w=128):
         return A(name, 0, w)
 
+    def row(name, c0, c1):
+        return A(name, c0, c1, 1, 0, 1)
+
+    def other(name, h, p1=128):
+        return A(name, 128 - 128 * h, 256 - 128 * h, 1, 0, p1)
+
     load = m["load"]
-    load("S", full("wti", 1), T.wts[:, :], "ld_wts")
     load("Y", full("candi", 256), T.cand[:, :], "ld_cand")
-    load("S", full("wt_0", 256), T.want[:, :], "ld_want")
-    for k in range(3):
-        load("Y", A("featb", 1024 * k, 1024 * k + 1024), T.feat[:, 1024 * k:1024 * k + 1024], "ld_feat%d" % k)
-    load("S", A("lasti", 0, 256, 1, 0, 8), T.last[:, :], "ld_last")
-    load("S", full("mk", 256), T.mkey[:, :], "ld_mkey")
-    load("S", full("mobi", 256), T.mobj[:, :], "ld_mobj")
+    load("S", full("want0", 256), T.want[:, :], "ld_want")
+    load("Y", full("wti", 1), T.wts[:, :], "ld_wts")
+    load("S", A("featb", 0, W // 2), T.feat[:, 0:W // 2], "ld_feat0")
+    load("Y", A("featb", W // 2, W), T.feat[:, W // 2:W], "ld_feat1")
+    load("Y", full("mk0", 256), T.mkey[:, :], "ld_mkey")
+    load("Y", full("mobi", 256), T.mobj[:, :], "ld_mobj")
     load("Y", A("kt", 0, W), T.kids[:, :], "ld_kids")
+    load("Y", A("lasti", 0, 256, 1, 0, 8), T.last[:, :], "ld_last")
 
     iota(full("pint", 1), [[0, 1]], 0, 1, False)
-    iota(full("cgf", 128), [[1, 8], [0, 16]], 0, 0)
-    iota(full("colf", 256), [[1, 256]], 0, 0)
-    iota(full("oneb", 128), [[0, 128]], 1, 0)
-    pick(full("ident"), full("oneb"), O.is_equal, 0, 1, -1, 128)
+    iota(full("colf", 144), [[1, 144]], 0, 0)
     iota(full("cmf", 256), [[0, 16], [1, 16]], 0, 0)
-    iota(A("oneb", 128, 256), [[0, 128]], -1, 0)
-    pick(full("nident"), A("oneb", 128, 256), O.is_equal, 0, 1, -1, 128)
-    iota(A("oneb", 256, 384), [[0, 128]], -16, 0)
-    pick(full("tri"), A("oneb", 256, 384), O.is_ge, 0, 1, -1, 128)
-
-    iota(full("sc", 256), [[0, 256]], int(BIG), 0)
-    m["pick2"](full("rst", 256), full("sc", 256), [[0, 16], [1, 16]])
-    iota(full("onef"), [[0, 128]], 1, 0)
-    iota(full("onesg", 240), [[0, 240]], 1, 0)
-    pick(full("onesg", 240), full("onesg", 240), O.is_ge, -112, 0, 1, 240)
-    pick(full("onesg", 240), full("onesg", 240), O.is_ge, 127, 0, -1, 240)
-    iota(A("kt", W, W + L), [[0, 256]], 0, 0, False)
+    iota(full("cg", 512), [[1, 32], [0, 16]], 0, 0)
+    iota(row("krow", 0, 136), [[0, 8], [-1, 17]], 16, 0)
+    iota(full("rr", 288), [[0, 16], [-1, 18]], 16, 0)
+    iota(A("kt", W, W + 16), [[0, 16]], 0, 0, False)
 
     def pi(k):
         return A("pint", k, k + 1)
 
     def pc(k):
         return A("pcol", k, k + 1)
-    PF, PM, PG, P16, P1615, HA, HB, PP16, PM16, KCOL, CA, CB, PARE, PARO, BS, MA, MB, WF, WF64, G15 = range(20)
-    PR = 24
+    PF, PM, PG, P32, PP, P1615, CA, CB, WF, G15, DUMP, PG8 = range(12)
+
+    fill(full("ones"), 1.0)
+    for name in ("zin", "zz"):
+        fill(full(name, 288), 0.0)
     ts(pi(2), pi(0), 4, O.arith_shift_right)
     ts(pi(1), pi(0), 15, O.bitwise_and)
+    ts(pi(3), pi(0), 31, O.bitwise_and)
+    cp(pc(PF), pi(0))
     cp(pc(PG), pi(2))
     cp(pc(PM), pi(1))
-    cp(pc(PF), pi(0))
-    ts(full("blk"), full("cgf"), pc(PG), O.is_equal, 1.0, O.mult)
+    cp(pc(P32), pi(3))
+    for name in ("zin2", "zz2"):
+        fill(full(name, 272), 0.0)
+    ts(pc(PP), pc(PG), 17.0, O.mult, 16.0, O.add)
+    ts(pc(CA), pc(PM), 11.0, O.is_lt)
+    ts(pc(CB), pc(PM), 6.0, O.is_lt)
     ts(pc(P1615), pc(PG), 16.0, O.mult, 15.0, O.add)
-    ts(full("selp", 143), full("colf", 143), pc(P1615), O.is_equal, 16.0, O.mult)
-
-    def build_wx(t):
-        for k in range(16):
-            out, src = A("wx", k, 16 * NVL, 16), A("wt_%d" % t, 0, NVL)
-            if t and k >= 16 - GWX:
-                pick(out, src, O.is_ge, 1, 0, 0, NVL)
-            else:
-                cp(out, src)
-
-    def key_a(k):
-        b, c, x, z = A("b%d" % k, 0, 512), A("featb", 512 * k, 512 * k + 512), A("ntab", 512 * k, 512 * k + 512), A("kf", 512 * k, 512 * k + 512)
-        if k < 3:
-            mm(b, full("kwf"), c)
-            act(z, b, F.Copy, bias=-31.5)
-        else:
-            z = b
-            mm(b, full("kwf"), c, True, False)
-            mm(b, A("nbias", 0, 128, 1, 0, 1), A("nbone", 0, 512, 1, 0, 1), False, True)
-        ts(x, z, 64.0 * MAGIC, O.add, 64.0 * MAGIC, O.subtract)
-
-    def key_b(k):
-        b, c, x = A("b%d" % k, 0, 512), A("featb", 512 * k, 512 * k + 512), A("ntab", 512 * k, 512 * k + 512)
-        mm(b, full("kwf"), c, True, False)
-        mm(b, full("nident"), x, False, True)
-        act(A("keytab", 512 * k, 512 * k + 512), b, F.Copy)
+    tt(pc(PP), pc(PP), pc(PM), O.subtract)
+    tt(pc(CB), pc(CB), pc(CA), O.subtract)
+    ts(full("ident"), full("colf"), pc(PF), O.is_equal)
+    ts(pc(CB), pc(CB), 1.0, O.add)
+    ts(full("blk16", 8), full("colf", 8), pc(PG), O.is_equal, 16.0, O.mult)
+    ts(full("nident"), full("ident"), -1.0, O.mult)
+    tt(pc(CA), pc(CA), pc(CB), O.subtract)
+    ts(full("turn", 136), full("colf", 136), pc(PP), O.is_equal, Q12, O.mult)
+    for name, v in (("bp", 4096.0), ("bn", -4096.0)):
+        ts(full(name, 8), full("colf", 8), pc(PG), O.is_equal, v, O.mult)
+    ts(full("sumf", 143), full("colf", 143), pc(P1615), O.is_equal)
+    ts(full("n64"), full("ident"), -64.0, O.mult)
+    ts(full("i16"), full("ident"), 1.0, O.mult)
+    ts(full("zm", 256), full("cmf", 256), pc(PM), O.is_le)
+    ts(full("ct1"), full("cmf"), pc(PM), O.is_gt, 2.0, O.mult)
+    ts(full("ct2"), full("cmf"), pc(PM), O.is_equal)
+    fill(A("zm", 0, 256, 16), 0.0)
+    ts(full("ct3"), full("cmf"), 8.0, O.is_lt)
+    tt(full("ct1"), full("ct1"), full("ct2"), O.subtract)
+    ts(full("expn", 512), full("cg", 512), pc(P32), O.is_equal, -1.0, O.mult)
+    ts(full("blk"), full("cg"), pc(PG), O.is_equal)
+    fill(A("krow", 0, 136, 17, 0, 1), BIG)
+    ts(pc(WF), full("wti", 1), 1.0, O.mult)
+    for h in range(2):
+        cp(A("cw0", 144 * h, 144 * h + 128), other("candi", h))
+        mm(A("b5", 128 * h, 128 * h + 128), other("want0", h), full("ident"))
+    act(full("wt_0", 256), A("b5", 0, 256), F.Copy)
+    ts(full("kw"), full("blk"), pc(WF), O.mult)
+    cp(row("krow16", 0, 136), row("krow", 0, 136))
+    ts(row("lim", 0, 136), row("krow", 0, 136), -1008.0, O.add)
+    ts(row("krow", 0, 136), row("krow", 0, 136), -1128.0, O.add)
 
     def consts1():
-        ts(pc(KCOL), pc(PM), 0.625, O.add)
-        fill(A("lim", 0, 1), -1008.0)
-        ts(pi(3), pi(0), 16, O.bitwise_and)
-        ts(pc(PP16), pc(PF), 16.0, O.add)
-        ts(pc(PM16), pc(PF), -16.0, O.add)
-        ts(pc(HB), pi(3), 256.0, O.mult)
-        ts(pc(HA), pc(HB), -1.0, O.mult, 4096.0, O.add)
-        ts(A("sper", 256, 384), full("colf"), pc(PM16), O.is_equal, pc(HB), O.mult)
-        ts(A("sper", 384, 512), full("colf"), pc(PF), O.is_equal, pc(HB), O.mult)
-        ts(A("sper", 0, 128), full("colf"), pc(PF), O.is_equal, pc(HA), O.mult)
-        ts(A("sper", 128, 256), full("colf"), pc(PP16), O.is_equal, pc(HA), O.mult)
-
-    def consts_bits():
-        ts(full("m16", 16), full("colf", 16), pc(PM), O.is_equal, 1.0, O.mult)
-        fill(full("t64c", 16), 0.5)
-        fill(full("t64b", 16), 0.0)
-        scan(full("w16", 16), full("t64c", 16), full("t64b", 16), 1.0, O.mult, O.add)
-        tt(full("w16", 16), full("m16", 16), full("w16", 16), O.mult)
-        ts(pc(MB), pc(PM), 6.0, O.is_lt)
-        ts(pc(CA), pc(PM), 12.0, O.is_lt)
-        red(pc(BS), full("w16", 16))
-        tt(pc(MA), pc(CA), pc(MB), O.subtract)
-        for mul, k, out, mask in ((64.0, 48, "tba", MA), (1.0, 64, "tbb", MB)):
-            ts(full("t64", k), full("colf", k), mul, O.mult, 0.5, O.add)
-            ts(full("t64", k), full("t64", k), pc(BS), O.mult)
-            ts(full("t64b", k), full("t64", k), MAGIC, O.add, MAGIC, O.subtract)
-            tt(full("t64c", k), full("t64", k), full("t64b", k), O.subtract)
-            ts(full("t64c", k), full("t64c", k), 0.0, O.is_gt, 2.0, O.mult)
-            ts(full(out, k), full("t64c", k), -1.0, O.add, pc(mask), O.mult)
-
-    def bit_table(k0, k1):
-        for k in range(k0, k1):
-            act(A("tb", 64 * k, 64 * k + 64), full("tbb", 64), F.Identity, bias=A("tba", k, k + 1))
+        tt(full("pre"), full("ct1"), full("blk"), O.mult)
+        for h in range(2):
+            ts(A("me", 256 + 128 * h, 384 + 128 * h), other("mobi", h), -1536.0, O.add, -Q12, O.mult)
+            cp(A("me", 512 + 128 * h, 640 + 128 * h), other("mk0", h))
+        mm(A("b4", 0, 512), full("i16"), A("me", 256, 768))
 
     def consts2():
-        ts(full("ct1"), A("cmf", 0, 128), pc(PM), O.is_gt, 2.0, O.mult)
-        ts(full("ct2"), A("cmf", 0, 128), pc(PM), O.is_equal, 1.0, O.mult)
-        ts(pc(CA), pc(PM), 11.0, O.is_lt)
-        tt(full("ct1"), full("ct1"), full("ct2"), O.subtract)
-        ts(pc(CB), pc(PM), 6.0, O.is_lt)
-        tt(full("pre"), full("ct1"), full("blk"), O.mult)
-        ts(full("sumf", 143), full("colf", 143), pc(P1615), O.is_equal, 1.0, O.mult)
-        tt(pc(CB), pc(CB), pc(CA), O.subtract)
-        ts(A("b7", 0, 256), full("mobi", 256), -1536.0, O.add)
-        ts(pc(CB), pc(CB), 1.0, O.add)
-        ts(full("ct1"), A("cmf", 0, 128), 8.0, O.is_lt)
-        tt(pc(CA), pc(CA), pc(CB), O.subtract)
-        ts(full("ct2"), full("ct1"), pc(CA), O.mult, pc(CB), O.add)
-        ts(full("blk8", 8), full("colf", 8), pc(PG), O.is_equal, 1.0, O.mult)
-        ts(pi(4), pi(2), 1, O.bitwise_and)
+        fill(row("crow", 256, 592), 0.0)
+        ts(full("ct2"), full("ct3"), pc(CA), O.mult, pc(CB), O.add)
+        fill(row("crow", 0, 128), -5632.0)
+        ts(full("ct2"), full("ct2"), -1.0, O.mult)
+        fill(row("crow", 128, 256), -4096.0)
         tt(full("rs"), full("ct2"), full("blk"), O.mult)
-        ts(pc(PARO), pi(4), 1.0, O.mult)
-        ts(pc(PARE), pc(PARO), -1.0, O.mult, 1.0, O.add)
+        fill(row("crow", 264, 280), 2047.0)
+        fill(A("crow", 288 + 17, 288 + 288, 18, 0, 1), -2047.0 / 64.0)
 
     def consts3():
-        ts(full("dump", 16), full("colf", 16), 16.0, O.mult, pc(PM), O.add)
-        ts(full("dump", 16), full("dump", 16), 1536.0, O.add)
-        ts(A("last16", 0, 256, 1, 0, 8), A("lasti", 0, 256, 1, 0, 8), -1536.0, O.add)
+        ts(full("m16", 16), full("colf", 16), pc(PM), O.is_equal)
+        ts(full("ct1"), full("ident"), -2.0, O.mult)
+        ts(pc(PG8), pc(PG), 8.0, O.add)
+        ts(full("s1", 16), full("m16", 16), -1.0, O.add, 1.0 / 64.0, O.mult)
+        tt(full("ct1"), full("ct1"), full("blk"), O.add)
+        ts(full("s2", 16), full("m16", 16), 1.0 / 64.0, O.mult)
+        for k in range(4):
+            ts(A("nb", 32 * k, 32 * k + 32), full("cmf", 32), pc(PG8 if k % 2 else PG), O.is_equal, 1.0 if k // 2 else -1.0, O.mult)
+        ts(full("dsrc"), full("ct1"), 1.0 / 64.0, O.mult)
+
+    def consts4():
+        ts(full("i64"), full("ident"), 1.0 / 64.0, O.mult)
+        ts(full("rr", 288), full("rr", 288), pc(PM), O.is_equal)
+        ts(pc(DUMP), pc(PM), float(W), O.add)
         ts(pc(G15), pc(PF), 16.0, O.mult, 15.0, O.add)
-        ts(A("g8", 0, 143, 1, 0, 8), A("colf", 0, 143, 1, 0, 8), A("pcol", G15, G15 + 1, 1, 0, 8), O.is_equal, 1.0, O.mult)
+        for h in range(2):
+            ts(A("last16", 128 * h, 128 * h + 128, 1, 0, 8), other("lasti", h, 8), -1536.0, O.add, Q12, O.mult)
+        ts(A("g8", 0, 143, 1, 0, 8), A("colf", 0, 143, 1, 0, 8), A("pcol", G15, G15 + 1, 1, 0, 8), O.is_equal)
         for k in range(16):
-            mm(A("b6", 96, 112), A("g8", 15 - k, 143 - k, 1, 0, 8), A("last16", k, 256, 16, 0, 8), k == 0, k == 15)
-        cp(full("pv", 16), A("b6", 96, 112))
-        ts(pc(P16), pc(PG), 16.0, O.mult)
+            mm(A("b7", 496, 512), A("g8", 15 - k, 143 - k, 1, 0, 8), A("last16", k, 256, 16, 0, 8), k == 0, k == 15)
 
-    def consts_ej():
-        ts(full("i16"), full("colf"), pc(PF), O.is_equal, 1.0, O.mult)
+    def consts5():
+        cp(full("prev", 16), A("b7", 496, 512))
         for k in range(16):
-            ts(A("ej", 128 * k, 128 * k + 128), full("i16"), A("m16", k, k + 1), O.mult)
+            ts(A("sj", 144 * k, 144 * k + 143), full("sumf", 143), A("m16", k, k + 1), O.mult)
 
-    def const_rot(t):
-        if t == 0:
-            ts(pi(5), pi(1), 11.0, O.add)
-            ts(pi(6), pi(5), 15, O.bitwise_and)
-            tt(pc(PR), pi(6), pc(P16), O.add)
-            ts(A("rot", 0, 128), full("colf"), pc(PF), O.is_equal, 1.0, O.mult)
-            ts(full("back"), full("colf"), pc(PR), O.is_equal, 1.0, O.mult)
-        else:
-            mm(A("b4", 256, 384), full("back"), A("rot", 128 * t - 128, 128 * t))
-            cp(A("rot", 128 * t, 128 * t + 128), A("b4", 256, 384))
-
-    consts_bits()
-    ts(pc(WF), full("wti", 1), 1.0, O.mult)
-    ts(full("kwf"), full("blk"), pc(WF), O.mult)
-    cp(A("cw0", 0, 256), full("candi", 256))
-    build_wx(0)
-    consts1()
-    fill(A("nbias", 0, 128, 1, 0, 1), -31.5)
-    fill(A("nbone", 0, 512, 1, 0, 1), 1.0)
-
-    def keytable(k0, k1):
+    def consts6(k0, k1):
         for k in range(k0, k1):
-            if k < 6:
-                key_a(k)
-            if k:
-                key_b(k - 1)
-    key_a(0)
-    key_a(1)
-    bit_table(0, 26)
-    act(full("nblk"), full("blk"), F.Copy, scale=-1.0)
-    act(full("sumb", 143), full("selp", 143), F.Copy, scale=1.0 / 16.0)
-    consts_ej()
-    key_b(0)
-    keytable(2, KEY0)
-    FEAT, KEYS, BITS = full("featb", W), full("keytab", W), full("tb", W)
-    KIDS, KALL = A("kt", 0, W), A("kt", 0, W + L)
-    late = {}
+            ts(A("dj", 128 * k, 128 * k + 128), full("dsrc"), A("s1", k, k + 1), O.max, A("s2", k, k + 1), O.min)
 
-    def dist_to(l0, l1):
-        return A("b4", l0, l1) if l1 <= 128 else A("b5", l0 - 128, l1 - 128)
+    KB_ = ("b3", "b7", "b5", "b4")
 
-    for t in range(STEPS):
-        cw, wt, co = "cw%d" % t, "wt_%d" % t, "co%d" % t
+    def key_a(k):
+        b = A(KB_[k % 2], 0, 512)
+        mm(b, full("kw"), A("featb", 512 * k, 512 * k + 512))
+        act(A("rk", 512 * k, 512 * k + 512), b, F.Copy, bias=1536.0 - 31.5 / 64.0, scale=1.0 / 64.0)
+
+    def key_b(k):
+        b = A(("b5", "b7")[k % 2], 0, 512)
+        mm(b, full("n64"), A("rk", 512 * k, 512 * k + 512), True, False)
+        mm(b, full("kw"), A("featb", 512 * k, 512 * k + 512), False, True)
+        ts(A("keys", 512 * k, 512 * k + 512), b, 64.0 * 1536.0, O.add)
+
+    start = {"c1": consts1, "c2": consts2, "c3": consts3, "c4": consts4, "c5": consts5, "c6": lambda: consts6(0, 8), "c7": lambda: consts6(8, 16)}
+    for k in range(6):
+        start["k%d" % k], start["l%d" % k] = lambda k=k: key_a(k), lambda k=k: key_b(k)
+
+    FEAT, KEYS, KIDS = full("featb", W), full("keys", W), A("kt", 0, W)
+    ONE = row("ones", 0, 128)
+    SUB = ("b0", "b1", "b6")
+
+    def dist(t, h):
+        cw, wt, pb = "cw%d" % t, "wt_%d" % t, "b%d" % (2 + h)
+        c0, f0 = 144 * h, 2048 * h
+        d = {}
+
+        def gather(e, l0, l1):
+            out, src = A("fs", f0 + 16 * l0, f0 + 16 * l1), ("ind", FEAT, A(cw, c0 + l0, c0 + l1))
+            return (lambda: cp(out, src)) if e == "V" else (lambda: act(out, src, F.Copy))
+
+        def sub(c, b):
+            mm(A(b, 0, 512), A(wt, 128 * h, 128 * h + 128, 1, 32 * c, 32 * c + 32), A("expn", 0, 512, 1, 32 * c, 32 * c + 32), True, False)
+            mm(A(b, 0, 512), full("ident"), A("fs", f0 + 512 * c, f0 + 512 * c + 512), False, True)
+
+        def kc():
+            mm(A(pb, 136, 272), A("c16", 128 * h, 128 * h + 128), full("turn", 136), True, False)
+            mm(A(pb, 136, 272), ONE, row("krow16", 0, 136), False, True)
+
+        def sums(l0, l1):
+            for k in range(16):
+                mm(A(pb, 16 - k, 136, 17, l0, l1), A("da", f0 + 16 * l0 + k, f0 + 16 * l1, 16), full("blk16", 8), False, False)
+        for c in range(8):
+            d["v%d" % c], d["g%d" % c] = gather("V", 16 * c, 16 * c + 16), gather("S", 16 * c, 16 * c + 16)
+        for c in range(4):
+            d["V%d" % c], d["G%d" % c] = gather("V", 32 * c, 32 * c + 32), gather("S", 32 * c, 32 * c + 32)
+        d["suma"], d["sumb"], d["sum"] = lambda: sums(0, 64), lambda: sums(64, 128), lambda: sums(0, 128)
+        d["c16"] = lambda: ts(A("c16", 128 * h, 128 * h + 128), A(cw, c0, c0 + 128), -1536.0, O.add)
+        d["kc"] = kc
+        d["p0"] = lambda: mm(A(pb, 0, 136), A("c16", 128 * h, 128 * h + 128), full("turn", 136), True, False)
+        d["p1"] = lambda: mm(A(pb, 0, 136), ONE, row("lim", 0, 136), False, True)
+        d["kcc"] = lambda: act(A("kc", 136 * h, 136 * h + 136), A(pb, 136, 272), F.Copy)
+        for j, c in enumerate((2, 0, 3, 1)):
+            b = SUB[(4 * h + 8 * t + j) % 3]
+            d["sub%d" % c] = lambda c=c, b=b: sub(c, b)
+            d["abs%d" % c] = lambda c=c, b=b: act(A("da", f0 + 512 * c, f0 + 512 * c + 512), A(b, 0, 512), F.Abs)
+        return d
+
+    def chain(t, h):
+        wt, co, pb = "wt_%d" % t, "co%d" % t, "b%d" % (2 + h)
         final = t == STEPS - 1
-        OL = A(co, 256, 272)
-        s0, s1 = SCH
-        sw = s1 - s0
-        kb = 512 // sw
-        act(A("fs", 0, 16 * sw), ("ind", FEAT, A(cw, s0, s1)), F.Copy)
-        for l0, l1 in VCH:
-            r = A("d", 16 * l0, 16 * l1)
-            tt(r, ("ind", FEAT, A(cw, l0, l1)), A("wx", 16 * l0, 16 * l1), O.subtract)
-            if t == 0 and l0 == 0:
-                keytable(KEY0, 7)
-        if t:
-            late["w"]()
+        a, b = 128 * h, 128 * h + 128
+        best, r8 = A("sc", 136 * h + 16, 136 * h + 136, 17), A("r8", 8 * h, 8 * h + 8)
+        z0 = 144 * h
+        OL, olp = A(co, 128 + 8 * h, 136 + 8 * h), A(pb, 272, 280)
+        fp, xp, wp = A("b5", 2 * a, 2 * a + 128), A(pb, 0, 128), A("b5", 2 * a + 128, 2 * a + 256)
+        fe, fi = A("ff", 384 * h, 384 * h + 128), A("ff", 128 + a, 256 + a)
+        ep, up = A(pb, 280 + 8 * h, 288 + 8 * h), A(pb, 288 - 8 * h, 296 - 8 * h)
+        el = A("el", 8 * h, 8 * h + 8)
+        d = {}
 
-        def abs_v(l0, l1):
-            act(A("da", 16 * l0, 16 * l1), A("d", 16 * l0, 16 * l1), F.Abs)
+        def zm():
+            mm(olp, A("zz", z0, z0 + 128), full("bp", 8), True, False)
+            mm(olp, A("zz", z0 + 1, z0 + 129), full("bn", 8), False, False)
+            mm(olp, A("zin", z0 + 1, z0 + 129), full("bp", 8), False, True)
+
+        def wm():
+            mm(wp, full("nident"), A(wt, a, b), True, False)
+            mm(wp, A("xo", a, b), full("ident"), False, True)
+
+        def wabs():
+            act(A("wn%d" % t, a, b), wp, F.Abs)
+            m["send"](A("wn%d" % t, a, b), A("wt_%d" % (t + 1), a, b), "arrw%d%d" % (t + 1, h), *link(nxt))
+
+        def fm():
+            mm(fp, ONE, row("crow", 128 * final, 128 * final + 128), True, False)
+            mm(fp, full("rs"), fi, False, True)
+
+        def em():
+            mm(A(pb, 280, 296), ONE, row("crow", 256 + 16 * h, 272 + 16 * h), True, False)
             for k in range(16):
-                mm(dist_to(l0, l1), A("selp", 15 - k, 143 - k), A("da", 16 * l0 + k, 16 * l1, 16), k == 0, k == 15)
-        for k in range(16):
-            c = A("b%d" % (k // kb), (k % kb) * sw, (k % kb) * sw + sw)
-            mm(c, full("nident"), A(wt, s0, s1), True, False)
-            mm(c, full("ident"), A("fs", k, 16 * sw, 16), False, True)
-        abs_v(*VCH[0])
-        if t:
-            late["wl"]()
-            const_rot(t)
-        steps = late["wo"]() if t else iter(())
-        next(steps, None)
-        ts(full("kc", 256), A(cw, 0, 256), 1.0 / 4096.0, O.mult, pc(KCOL), O.add)
-        next(steps, None)
-        if t:
-            ts(full("pv", 16), A(cw, 256, 272), -1536.0, O.add)
-        next(steps, None)
-        for k in range(0, 16, kb):
-            e = min(k + kb, 16)
-            act(A("da", 16 * s0 + sw * k, 16 * s0 + sw * e), A("b%d" % (k // kb), 0, sw * (e - k)), F.Abs)
-        for k in range(16):
-            mm(dist_to(s0, s1), A("selp", 15 - k, 143 - k), A("da", 16 * s0 + sw * k, 16 * s0 + sw * k + sw), k == 0, k == 15)
-        if t:
-            late["scatter"]()
-        for c in VCH[1:]:
-            abs_v(*c)
-        act(A("b6", 0, 128), A("b4", 0, 128), F.Relu, bias=A("lim", 0, 1))
-        act(A("b5", 128, 256), A("b5", 0, 128), F.Relu, bias=A("lim", 0, 1))
-        if t == 0:
-            bit_table(26, 48)
-            consts2()
-        if t:
-            late["mount2"]()
-        for h in range(2):
-            a, b = 128 * h, 128 * h + 128
-            tt(A("comp", a, b), A("b5", 128, 256) if h else A("b6", 0, 128), A("kc", a, b), O.add)
-            tr(A("tr", a, b), A("comp", a, b))
-            scan(A("sc", a, b), A("rst", a, b), A("tr", a, b), BIG, O.max, O.min)
-        best = A("sc", 15, 256, 16)
-        ts(full("r16", 16), best, MAGIC, O.add, MAGIC, O.subtract)
-        ts(A("od", 16, 32), best, 16.5, O.is_ge, 1.0 / 4096.0, O.mult)
-        tt(A("od", 0, 16), best, full("r16", 16), O.subtract)
-        for dd in range(2):
-            for bb in range(2):
-                k = 2 * dd + bb
-                mm(A("b6", dd, 32, 2), A("sper", 128 * k, 128 * k + 128), A("od", bb, 32, 2), bb == 0, bb == 1)
-        ts(OL, A("b6", 0, 16), 1536.0, O.add)
-        halves = ((0, 128), (128, 256))
-        for a, b in halves:
-            tt(A("hit", a, b), ("ind", KEYS, A(co, 256 + a // 16, 256 + b // 16)), A("mk", a, b), O.is_equal)
-        if not final:
-            act(full("xo", 256), ("ind", FEAT, OL), F.Copy)
-        act(full("code", 256), ("ind", BITS, OL), F.Copy)
-        for a, b in halves:
-            mm(A("b5" if a == 0 else "b4", 0, 128), full("pre"), A("hit", a, b))
-        for a, b in halves:
-            ts(A("fi", a, b), A("b5" if a == 0 else "b4", 0, 128), 0.0, O.is_lt)
-        if not final:
-            mm(A("b0", 0, 256), full("ident"), A(wt, 0, 256), True, False)
-            mm(A("b0", 0, 256), full("nident"), full("xo", 256), False, True)
-            act(A("wn%d" % t, 0, 256), A("b0", 0, 256), F.Abs)
-            ad, ma, ne = link(nxt)
-            m["send"](A("wn%d" % t, 0, 256), A("wt_%d" % (t + 1), 0, 256), "arrw%d" % (t + 1), ad, ma, ne)
-        for a, b in halves:
-            tt(A("fe", a, b), A("fi", a, b), A("b7", a, b), O.mult)
-        ts(full("lo", 256), full("code", 256), pc(PARO), O.mult)
-        mm(A("b4", 0, 256), full("rs"), full("fi", 256))
-        act(full("nsel", 256), A("b4", 0, 256), F.Copy, bias=1.0, scale=-1.0)
-        act(full("sel", 256), A("b4", 0, 256), F.Copy)
-        for k in range(16):
-            mm(A("b5", 0, 16), A("sumf", 15 - k, 143 - k), A("fe", k, 256, 16), k == 0, k == 15)
-        for h in range(2):
-            mm(A("b1", 8 * h, 8 * h + 8), A("fi", 128 * h, 128 * h + 128), full("blk8", 8))
-        act(full("ctv", 16), A("b1", 0, 16), F.Copy, acc=full("cs", 1))
-        tt(full("ka", 256), ("ind", KIDS, OL), full("nsel", 256), O.mult)
-        ts(full("el", 16), A("b5", 0, 16), 1536.0, O.add)
+                mm(A(pb, 280, 296), A("sumf", 15 - k, 143 - k), A("ff", 2 * a + k, 2 * a + 256, 16), False, k == 15)
 
-        def match(gg):
-            b = "b%d" % ((gg + 2) % 4)
-            p0 = 32 * (gg // 2)
-            p1 = p0 + 16 + 16 * (gg % 2)
-            lh = "lo" if gg % 2 else "code"
-            for c0, lp, ln, tri in ((0, 0, 0, True), (128, 0, 128, False), (256, 128, 128, True)):
-                mm(A(b, c0, c0 + 128), A(lh, lp, lp + 128, 1, p0, p1), A("code", ln, ln + 128, 1, p0, p1), True, not tri)
-                if tri:
-                    mm(A(b, c0, c0 + 128), full("ident"), full("tri"), False, True)
-            for h, (c0, c1) in enumerate(((0, 256), (256, 384))):
-                o, cv = A("eq", 384 * gg + c0, 384 * gg + c1), A("ctv", 8 * h + gg, 8 * h + gg + 1)
-                if final and gg % 4 == 3:
-                    ts(o, A(b, c0, c1), 12.0, O.is_equal, cv, O.mult)
-                else:
-                    act(o, A(b, c0, c1), F.Relu, bias=-11.0, scale=cv)
-        act(A("b4", 256, 512), full("ka", 256), F.Copy)
-        match(0)
-        for a, b in halves:
-            tt(A("kb", a, b), ("ind", KIDS, A("el", a // 16, b // 16)), A("sel", a, b), O.mult)
-        for a, b in halves:
-            tt(A("new", a, b), A("kb", a, b), A("b4", 256 + a, 256 + b), O.add)
+        def out():
+            if final:
+                m["send"](A("new", a, b), other("yl", h), "arry%d" % h, *link(home))
+            else:
+                ts(A(co, z0, z0 + 128), A("c16o", a, b), 1536.0, O.add)
+                m["send"](A(co, 136 * h, 136 * h + 136), A("cw%d" % (t + 1), 136 * h, 136 * h + 136), "arrc%d%d" % (t + 1, h), *link(nxt))
+        d["SCAN"] = lambda: scan(A("sc", 136 * h, 136 * h + 136), A(pb, 0, 136), A("kc", 136 * h, 136 * h + 136), BIG, O.min, O.max)
+        d["R"] = lambda: ts(r8, best, MAGIC, O.add, MAGIC, O.subtract)
+        d["OD"] = lambda: tt(A("zin", z0, z0 + 128, 16), best, r8, O.subtract)
+        d["NA"] = lambda: ts(A("zin2", a, b, 16), best, 15.5, O.is_ge)
+        d["Z"] = lambda: scan(A("zz", z0, z0 + 128), A("zm", 0, 128), A("zin", z0, z0 + 128), 0.0, O.mult, O.add)
+        d["ZM"], d["FM"], d["EM"], d["OUT"] = zm, fm, em, out
         if not final:
-            for a, b in halves:
-                cp(A(co, a, b), A("new", a, b))
-            ad, ma, ne = link(nxt)
-            m["send"](A(co, 0, 272), A("cw%d" % (t + 1), 0, 272), "arrc%d" % (t + 1), ad, ma, ne)
-            m["landed"](A("wt_%d" % (t + 1), 0, 256), "arrw%d" % (t + 1), ne)
-            m["landed"](A("cw%d" % (t + 1), 0, 272), "arrc%d" % (t + 1), ne)
-        else:
-            ad, ma, ne = link(home)
-            m["send"](full("new", 256), full("yl", 256), "arry", ad, ma, ne)
-            m["landed"](full("yl", 256), "arry", ne)
-        for gg in range(1, 8 if final else 4):
-            match(gg)
-        act(full("ck", 256), ("ind", KEYS, OL), F.Copy)
-        if not final:
-            match(4)
-        if t == 0:
-            consts3()
-            const_rot(0)
-        tt(full("odm", 16), A("b6", 0, 16), full("dump", 16), O.subtract)
-        cp(A("nap", 0, 16), A("b6", 16, 32))
-        tt(A("nap", 16, 32), A("b6", 16, 32), full("pv", 16), O.mult)
-        if not final:
-            mm(A("b6", 32, 33), full("onef"), full("cs", 1))
+            d["W"], d["WABS"] = wm, wabs
+            d["XO"] = lambda: act(A("xo", a, b), ("ind", FEAT, OL), F.Copy)
+        d["OL"] = lambda: ts(OL, olp, 1536.0, O.add)
+        d["HIT"] = lambda: tt(A("hit", a, b), ("ind", KEYS, OL), A("me", 512 + a, 512 + b), O.is_equal)
+        d["X"] = lambda: mm(xp, full("pre"), A("hit", a, b))
+        d["FI"] = lambda: ts(fi, xp, 0.0, O.is_lt, -4096.0, O.mult)
+        d["FE"] = lambda: tt(fe, fi, A("b4", a, b), O.mult)
+        d["SELC"] = lambda: act(A("selc", a, b), fp, F.Copy, bias=-4096.0 if final else -7168.0, scale=-2.0)
+        d["EL"] = lambda: ts(el, ep, 1536.0, O.add)
+        d["KA"] = lambda: tt(A("xk", a, b), ("ind", KIDS, OL), A("selc", a, b), O.add)
+        d["KB"] = lambda: tt(A("nw", a, b), ("ind", KIDS, el), A("xk", a, b), O.max)
+        d["FIX"] = lambda: tt(A("new" if final else "c16o", a, b), A("nw", a, b), fp, O.add)
+        d["OC"] = lambda: ts(A("oc", 8 * h, 8 * h + 8), OL, -1536.0, O.add)
+        d["VC"] = lambda: tt(A("vc", 8 * h, 8 * h + 8), up, A("oc", 8 * h, 8 * h + 8), O.max)
+        return d
 
-        def writers():
+    def post(t):
+        co = "co%d" % t
+        final = t == STEPS - 1
+        d = {}
+
+        def cnt():
+            mm(row("b7", 368, 496), A("ones", 0, 1), A("ff", 128, 256), True, False)
+            mm(row("b7", 368, 496), A("ones", 0, 1), A("ff", 256, 384), False, True)
+            act(row("junk", 0, 128), row("b7", 368, 496), F.Copy, bias=120.0 / 128.0, scale=16.0 * Q12, acc=row("cs", 0, 1))
+
+        d["rnd"] = lambda: ts(row("cs", 1, 2), row("cs", 0, 1), 256.0 * MAGIC, O.add, 256.0 * MAGIC, O.subtract)
+        d["lim"] = lambda: ts(row("lim", 0, 136), row("krow", 0, 136), row("cs", 0, 1), O.add, row("cs", 1, 2), O.subtract)
+
+        def nm():
             for h in range(2):
-                out = A("b3", 128 * h, 128 + 128 * h)
-                for gg in range(8):
-                    lh = A("onesg", 112 - 16 * gg, 240 - 16 * gg)
-                    mm(out, lh, A("eq", 384 * gg + 128 * h, 384 * gg + 128 * h + 128), gg == 0, False)
-                    if h:
-                        mm(out, lh, A("eq", 384 * gg + 256, 384 * gg + 384), False, False)
-                mm(out, full("nblk"), A("fi", 128 * h, 128 * h + 128), False, True)
+                o, a = A("b7", 288, 320), 128 * h
+                mm(o, A("zz2", a, a + 128), A("nb", 32 * h, 32 * h + 32), h == 0, False)
+                mm(o, A("zz2", a + 1, a + 129), A("nb", 64 + 32 * h, 96 + 32 * h), False, False)
+                mm(o, A("zin2", a + 1, a + 129), A("nb", 32 * h, 32 * h + 32), False, h == 1)
 
-        def late_w():
-            act(full("wr", 256), A("b3", 0, 256), F.Relu, scale=-1.0 / 16.0)
+        def writers(tag, b0, b1):
+            def dm():
+                mm(A("b7", 18 * b0, 18 * b1), ONE, row("crow", 288 + 18 * b0, 288 + 18 * b1), True, False)
+                for j in range(16):
+                    mm(A("b7", 18 * b0 + 16 - j, 18 * b1, 18), A("dj", 128 * j, 128 * j + 128), A("vc", b0, b1), False, False)
+                mm(A("b7", 18 * b0 + 17, 18 * b1, 18), full("i64"), A("vc", b0, b1), False, True)
+            d["dm" + tag] = dm
+            d["ds" + tag] = lambda: scan(A("ds", 18 * b0, 18 * b1), A("b7", 18 * b0, 18 * b1), A("rr", 18 * b0, 18 * b1), 0.0, O.mult, O.add)
+            d["h2" + tag] = lambda: ts(A("h2", b0, b1), A("ds", 18 * b0 + 17, 18 * b1, 18), 0.0, O.is_equal, 8192.0, O.mult)
+            d["uu" + tag] = lambda: tt(A("u16", b0, b1), A("h2", b0, b1), A("vc", b0, b1), O.add)
+            d["wo" + tag] = lambda: ts(A("wo", 2 * b0, 2 * b1, 2), A("u16", b0, b1), 1536.0, O.add, pc(DUMP), O.min)
+        writers("", 0, 16)
+        writers("0", 0, 8)
+        writers("1", 8, 16)
 
-        def late_wl():
-            for k in range(16):
-                mm(A("b3", 256, 272), A("sumb", 15 - k, 143 - k), A("wr", k, 256, 16), k == 0, k == 15)
+        def shift(j, i):
+            return A("sj", 144 * j + 15 - i, 144 * j + 143 - i)
 
-        def late_wo():
-            tt(full("wt1", 16), A("b3", 256, 272), full("odm", 16), O.mult)
-            yield
-            tt(full("wt1", 16), full("wt1", 16), full("dump", 16), O.add)
-            yield
-            ts(full("wo", 16), full("wt1", 16), 1536.0, O.add)
-            yield
+        def ext():
+            for i in range(16):
+                mm(A("b7", 320, 368), shift((i + 5 * t) % 16, i), A("me", i, 768, 16), i == 0, i == 15)
 
-        def late_scatter(final=final):
-            cp(("ind", A("kf", 0, W + L) if final else KALL, full("wo", 16)), full("new", 256))
-        if final:
-            iota(A("kf", W, W + L), [[0, 256]], 0, 0)
-            cp(full("kf", W), KIDS)
-            writers()
-        mm(A("b6", 64, 96), A("rot", 128 * t, 128 * t + 128), full("nap", 32))
-        cp(full("nr", 32), A("b6", 64, 96))
-        if final:
-            late_w()
-            late_wl()
-            for _ in late_wo():
-                pass
-            late_scatter()
-        if not final:
-            cp(A("cint", 0, 1), A("b6", 32, 33))
-            build_wx(t + 1)
-            ts(A("cint", 1, 2), A("cint", 0, 1), 15, O.bitwise_and)
-        for k in range(16):
-            mm(A("b5", (k - 5 * t) % 16, 256, 16), A("ej", 128 * k, 128 * k + 128), A("nr", 0, 16))
-        if not final:
-            match(5)
-        mm(A("b4", 0, 256), full("ident"), full("ck", 256), True, False)
-        mm(A("b4", 0, 256), full("nident"), full("mk", 256), False, True)
+        def spread():
+            mm(A("b4", 0, 512), full("i16"), A("me", 256, 768), True, False)
+            for i in range(16):
+                mm(A("b4", i, 512, 16), shift(i, (i + 5 * t) % 16), A("sp", 0, 32), False, False)
+                mm(A("b4", i, 512, 16), shift(i, (i + 5 * t) % 16), A("sp", 32, 64), False, i == 15)
 
-        def late_mount0():
-            tt(full("mt1", 256), full("nus", 256), A("b4", 0, 256), O.mult)
-            tt(full("mt2", 256), full("nus", 256), A("b7", 0, 256), O.mult)
+        if t:
+            d["pv"] = lambda: ts(full("prev", 16), A("cw%d" % t, 128, 144), -1536.0, O.add, Q12, O.mult)
+        d["dp"] = lambda: tt(A("sp", 32, 48), full("prev", 16), full("nas", 16), O.mult)
 
-        def late_mount2(final=final, t=t):
-            mm(A("b0", 0, 256), full("ident"), full("ck", 256), True, False)
-            mm(A("b0", 0, 256), full("nident"), full("mt1", 256), False, True)
-            mm(A("b1", 0, 256), full("i16"), full("mt2", 256), True, False)
-            for k in range(16):
-                mm(A("b1", (k - 5 * t) % 16, 256, 16), A("ej", 128 * k, 128 * k + 128), A("nr", 16, 32), False, k == 15)
-            if not final:
-                act(full("mk", 256), A("b0", 0, 256), F.Copy)
-                act(A("b7", 0, 256), A("b1", 0, 256), F.Copy)
+        todo = list(range(8, 16)) + list(range(8))
 
-        late["w"], late["wl"], late["wo"], late["scatter"], late["mount0"], late["mount2"] = (
-            late_w, late_wl, late_wo, late_scatter, late_mount0, late_mount2)
-        act(full("nus", 256), A("b5", 0, 256), F.Copy, bias=1.0, scale=-1.0)
-        if not final:
-            match(6)
-            match(7)
-            late_mount0()
-            ts(A("lim", 0, 1), A("cint", 1, 2), -16.0, O.mult, -1008.0, O.add)
-            writers()
+        def scatter():
+            b = todo.pop()
+            src = A("new", 16 * b, 16 * b + 16) if final else A(co, 16 * b + 16 * (b // 8), 16 * b + 16 * (b // 8) + 16)
+            cp(("ind", A("kf" if final else "kt", 0, W + 16), A("wo", 2 * b, 2 * b + 1)), src)
+        d["cnt"], d["nm"], d["ext"], d["spread"], d["s"] = cnt, nm, ext, spread, scatter
+        d["ck"] = lambda: act(full("me", 256), ("ind", KEYS, A(co, 128, 144)), F.Copy, scale=-1.0)
+        d["nz"] = lambda: scan(full("zz2", 256), full("zm", 256), full("zin2", 256), 0.0, O.mult, O.add)
+        d["nas"] = lambda: cp(full("nas", 32), A("b7", 288, 320))
+        d["dk"] = lambda: tt(A("sp", 48, 64), A("b7", 320, 336), full("nas", 16), O.mult)
+        d["dq"] = lambda: tt(A("sp", 0, 32), A("b7", 336, 368), full("nas", 32), O.mult)
+        d["mkc"] = lambda: act(A("me", 256, 768), A("b4", 0, 512), F.Copy)
+        if t == STEPS - 2:
+            d["kf"] = lambda: m["copy"]("Y", full("kf", W + 16), full("kt", W + 16), "ld_kf")
+        return d
 
-    m["store"]("Y", T.yn[:, :], full("yl", 256), "oyn")
-    for k in range(3):
-        c0, c1 = 512 * k, 512 * k + 512
-        b = "b%d" % (5 + k % 2)
-        act(A(b, 0, 512), A("kf", 1536 + c0, 1536 + c1), F.Copy, scale=2.0)
-        tt(A("ydb", c0, c1), A("kf", c0, c1), A(b, 0, 512), O.add)
-        m["store"]("Y", T.yd[:, c0:c1], A("ydb", c0, c1), "oyd%d" % k)
-        if k == 0:
-            late["mount0"]()
-            late["mount2"]()
-        if k == 1:
-            act(full("my", 256), A("b1", 0, 256), F.Copy, scale=64.0, bias=98304.0)
-            tt(full("my", 256), full("my", 256), A("b0", 0, 256), O.add)
-            m["store"]("Y", T.ymu[:, :], full("my", 256), "omu")
-    m["finish"]([("arry", link(home)[2])] + [("ld_" + x, 16) for x in LOADS])
+    def ymu0():
+        for h in range(2):
+            act(other("mt", h), A("b4", 128 * h, 128 * h + 128), F.Copy, scale=-262144.0, bias=98304.0)
 
+    def ymu1(h):
+        tt(other("my", h), other("mt", h), A("b4", 256 + 128 * h, 384 + 128 * h), O.add)
+        if h:
+            m["store"]("Y", T.ymu[:, :], [full("my", 256)], "omu")
 
-GWX = 4
-KEY0 = 4
-SCRATCH["nbone"] = ("sbuf", [128, 512], "bfloat16")
-SCRATCH["kf"] = ("sbuf", [128, W + L], "float32")
+    def yd(k):
+        c0, c1 = 384 * k, 384 * k + 384
+        b = A(SUB[k % 3], 0, 384)
+        act(b, A("kf", 1536 + c0, 1536 + c1), F.Copy, scale=2.0)
+        tt(A("ydb", c0, c1), A("kf", c0, c1), b, O.add)
+        m["store"]("Y", T.yd[:, c0:c1], [A("ydb", c0, c1)], "oyd%d" % k)
+    ends = {"my0": ymu0, "my1": lambda: ymu1(0), "my2": lambda: ymu1(1), "yn": lambda: m["store"]("S", T.yn[:, :], [full("yl", 256)], "oyn")}
+    for k in range(4):
+        ends["yd%d" % k] = lambda k=k: yd(k)
+
+    ps = {}
+    for p in range(2 * STEPS + 1):
+        t, h = p // 2, p % 2
+        calls = dist(t, h) if t < STEPS else dict(ends)
+        if p:
+            calls.update(chain((p - 1) // 2, 1 - h))
+        if p and h == 0:
+            ps = post(t - 1)
+        calls.update(ps if p > 1 else start)
+        for name in ORDER[2 + p if p < 2 else 4 if t == STEPS else h].split():
+            if name in calls:
+                calls[name]()
+    m["finish"]([("arry0", link(home)[2]), ("arry1", link(home)[2])] + [("ld_" + x, 16) for x in LOADS])

@@ -11,14 +11,13 @@ SCRATCH = {}
 def _buffers():
     for dtype, names in (
         ("float32", "colf 144 cmf 256 pcol 32 m16 16 s1 16 s2 16 ct1 128 ct2 128 ct3 128 krow 136 kc 272 sc 272 r8 16 xk 256 nw 256 new 256 "
-                    "rr 288 ds 288 h2 16 u16 16 cs 2 junk 128 my 256 mt 256 yl 256 ydb 1536"),
-        ("bfloat16", "featb 3072 keys 3072 cg 512 expn 512 mk0 256 want0 256 ident 128 nident 128 blk 128 blk16 8 pre 128 kw 128 "
-                     "fs 4096 da 4096 xo 256 hit 256 selc 256"),
-        ("float16", "c16 256 c16o 256 turn 136 ones 128 krow16 136 lim 136 bp 8 bn 8 nb 128 zm 256 zin 288 zz 288 zin2 272 zz2 272 rs 128 "
-                    "crow 592 sumf 144 sj 2304 dsrc 128 dj 2048 i64 128 i16 128 n64 128 rk 3072 me 768 ff 512 oc 16 vc 16 nas 32 sp 64 "
-                    "prev 16 last16 256 g8 144"),
-        ("int32", "candi 256 kt 3088 kf 3088 mobi 256 lasti 256 wti 1 pint 16"),
-        ("uint16", "el 16 wo 32"),
+                    "rr 216 ds 216 h2 24 u16 16 cs 2 junk 128 my 256 mt 256 yl 256 ydb 1536"),
+        ("bfloat16", "featb 3072 keys 3072 cg 512 mk0 256 want0 256 ident 128 blk 128 blk16 8 pre 128 kw 144 fs 4096 da 4096 hit 256 selc 256"),
+        ("float16", "expn 512 xo 256 ni16 128 turn 136 ones 128 krow16 136 lim 136 bp 8 bn 8 nb 192 zm 256 zin 288 zz 288 zin2 272 zz2 272 rs 128 "
+                    "crow 512 sumf 144 sj 2304 dsrc 128 dj 2048 i64 128 i16 128 rk 384 me 768 ff 512 vc 24 vct 128 pair 72 nas 48 sp 64 "
+                    "last16 256 g8 144"),
+        ("int32", "candi 256 kt 3104 kf 3104 mobi 256 lasti 256 wti 1 pint 16"),
+        ("uint16", "el 16 wo 16"),
     ):
         words = names.split()
         for k in range(0, len(words), 2):
@@ -26,9 +25,8 @@ def _buffers():
     for t in range(STEPS):
         SCRATCH["cw%d" % t] = ("sbuf", [128, 272], "uint16")
         SCRATCH["co%d" % t] = ("sbuf", [128, 272], "uint16")
-        SCRATCH["wt_%d" % t] = ("sbuf", [128, 256], "bfloat16")
-        if t < STEPS - 1:
-            SCRATCH["wn%d" % t] = ("sbuf", [128, 256], "bfloat16")
+        SCRATCH["wt_%d" % t] = ("sbuf", [128, 528], "float16")
+        SCRATCH["wn%d" % t] = ("sbuf", [128, 528], "float16")
     for b in range(8):
         SCRATCH["b%d" % b] = ("psum", [128, 512], "float32")
 
@@ -189,7 +187,12 @@ def machine(g, T):
 
 
 ORDER = [
-    'SCAN R NA OD Z pv ZM nz OL HIT nm X ck nas OC G2 ext FI FM c16 FE EM v2 v1 SELC G3 XO KA sub2 cnt kc EL dp sub3 KB abs2 VC dm kcc FIX OUT v0 v3 ds abs3 rnd W dk WABS sub0 sub1 p0 sumb h2 abs0 abs1 suma lim p1 uu dq spread wo', 's G2 s s v1 s G3 SCAN s R v0 OD s Z ZM s sub2 mkc sub3 v2 abs2 s abs3 OL c16 XO sub0 s HIT X kc s kcc v3 sub1 s FI s FE s s FM EM OC s NA p0 s abs1 EL kf SELC KA sumb abs0 VC suma KB FIX OUT p1 W WABS', 'c16 c2 k0 k1 l0 G2 k3 k2 sub2 k5 kc k4 kcc c1 abs2 v0 v3 G3 l1 v1 l2 l3 sub0 v2 sub3 l4 sub1 abs0 l5 abs3 p0 sumb abs1 suma p1', 'v1 G3 v0 SCAN R c16 OD Z G2 sub0 ZM sub2 v3 OL HIT X XO sub3 abs2 OC v2 FI FM kc c3 abs0 W SELC abs3 sub1 abs1 FE EM c4 kcc p0 sumb KA c7 EL VC KB c5 WABS FIX NA OUT suma p1 c6', 'dm0 SCAN NA R OD pv Z ZM OL ck HIT nz nm X FI ds0 FE FM h20 uu0 wo0 ext EM OC SELC nas dk dq VC dm1 EL KA KB ds1 dp spread h21 s uu1 my0 s s s s s s FIX s wo1 s s s OUT my1 my2 s s s yn s s yd1 yd0 yd2 yd3',
+    'SCAN R NA vt0 OD Z dm0 ZM nz OL XO ds0 HIT ck X OC h20 uu0 FI uv0 nm G3 nas FE v0 v1 FM SELC KA cnt EM EL wo0 kc G2 VD W VC sub3 kcc KB rnd we0 FIX lim vt1 OUT v3 v2 dp s sub2 WABS sub0 dm1 ds1 s h21 uu1 s abs2 sub1 uv1 abs0 we1 ext s dk wo1 dq abs3 p0 abs1 sum p1 REST spread',
+    'v3 G2 SCAN s kc R G3 v0 OD Z ZM sub2 v1 sub0 mkc OL s HIT kcc X abs2 abs0 OC v2 s sub3 NA abs3 FI s sub1 FM SELC FE EM XO W KA abs1 p0 sum EL p1 VC KB FIX VD OUT WABS REST',
+    'd1 c1 c2 kc v1 kcc v3 j0 G2 G3 ks v0 sub2 d0 sub0 km m0 abs2 v2 k1 j1 sub1 d3 k0 d2 sub3 k3 abs0 abs1 k2 abs3 p0 sum p1',
+    'v0 kc v2 j2 G2 SCAN k5 k4 sub2 G3 R OD j3 Z l7 l6 abs2 v1 ZM OL sub0 abs0 v3 kcc NA OC HIT sub3 abs3 c3 X FI FE sub1 c4 XO FM SELC EM EL W abs1 p0 sum p1 VC WABS KA KB FIX VD l REST c5 OUT',
+    'kc G2 v0 s G3 SCAN sub2 v1 mkc R s OD kcc s Z abs2 ZM v2 s sub3 OL NA kf abs3 sub0 abs0 HIT v3 OC X FI FE sub1 FM SELC KA EM EL KB VC p0 VD abs1 sum p1 FIX OUT',
+    'SCAN R OD Z vt0 NA nz dm0 ds0 ZM OL ck h20 HIT uu0 nm we0 uv0 OC X FI FE ext nas dp wo0 dq FM SELC KA EM dk VC EL vt1 VD dm1 s KB s spread s s FIX ds1 h21 uu1 uv1 we1 wo1 s s my0 my1 s OUT my2 s yn yd2 yd1 yd0 yd3',
 ]
 
 
@@ -215,6 +218,10 @@ def rank_program(g, core, T, topo):
     def other(name, h, p1=128):
         return A(name, 128 - 128 * h, 256 - 128 * h, 1, 0, p1)
 
+    def part(name, h, k):
+        c0 = (0, 128, 256)[k] if h == 0 else (400, 272, 264)[k]
+        return A(name, c0, c0 + (8 if k == 2 else 128))
+
     load = m["load"]
     load("Y", full("candi", 256), T.cand[:, :], "ld_cand")
     load("S", full("want0", 256), T.want[:, :], "ld_want")
@@ -231,128 +238,156 @@ def rank_program(g, core, T, topo):
     iota(full("cmf", 256), [[0, 16], [1, 16]], 0, 0)
     iota(full("cg", 512), [[1, 32], [0, 16]], 0, 0)
     iota(row("krow", 0, 136), [[0, 8], [-1, 17]], 16, 0)
-    iota(full("rr", 288), [[0, 16], [-1, 18]], 16, 0)
-    iota(A("kt", W, W + 16), [[0, 16]], 0, 0, False)
+    iota(full("rr", 144), [[0, 8], [-1, 18]], 16, 0)
+    iota(A("ct3", 0, 72), [[2, 4], [0, 18]], 0, 0)
+    iota(A("kt", W, W + 32), [[0, 32]], 0, 0, False)
 
     def pi(k):
         return A("pint", k, k + 1)
 
     def pc(k):
         return A("pcol", k, k + 1)
-    PF, PM, PG, P32, PP, P1615, CA, CB, WF, G15, DUMP, PG8 = range(12)
+    PF, PM, PG, P32, PP, P1615, CA, CB, WF, G15, DUMP, PG8, DUMP2, PM1 = range(14)
 
     fill(full("ones"), 1.0)
-    for name in ("zin", "zz"):
-        fill(full(name, 288), 0.0)
+    for name, k in (("zin", 288), ("zz", 288)):
+        fill(full(name, k), 0.0)
     ts(pi(2), pi(0), 4, O.arith_shift_right)
     ts(pi(1), pi(0), 15, O.bitwise_and)
     ts(pi(3), pi(0), 31, O.bitwise_and)
     cp(pc(PF), pi(0))
+    fill(row("crow", 256, 512), 0.0)
     cp(pc(PG), pi(2))
     cp(pc(PM), pi(1))
     cp(pc(P32), pi(3))
-    for name in ("zin2", "zz2"):
-        fill(full(name, 272), 0.0)
+    ts(full("ident"), full("colf"), pc(PF), O.is_equal)
+    ts(pc(P1615), pc(PG), 16.0, O.mult, 15.0, O.add)
     ts(pc(PP), pc(PG), 17.0, O.mult, 16.0, O.add)
+    ts(full("m16", 16), full("colf", 16), pc(PM), O.is_equal)
     ts(pc(CA), pc(PM), 11.0, O.is_lt)
     ts(pc(CB), pc(PM), 6.0, O.is_lt)
-    ts(pc(P1615), pc(PG), 16.0, O.mult, 15.0, O.add)
+    ts(full("sumf", 143), full("colf", 143), pc(P1615), O.is_equal)
+    for name, v in (("i16", 1.0), ("ni16", -1.0), ("i64", 1.0 / 64.0), ("junk", -2.0 / 64.0)):
+        act(full(name), full("ident"), F.Copy, scale=v)
     tt(pc(PP), pc(PP), pc(PM), O.subtract)
     tt(pc(CB), pc(CB), pc(CA), O.subtract)
-    ts(full("ident"), full("colf"), pc(PF), O.is_equal)
-    ts(pc(CB), pc(CB), 1.0, O.add)
+    ts(full("s1", 16), full("m16", 16), -1.0, O.add, 1.0 / 64.0, O.mult)
+    ts(full("s2", 16), full("m16", 16), 1.0 / 64.0, O.mult)
     ts(full("blk16", 8), full("colf", 8), pc(PG), O.is_equal, 16.0, O.mult)
-    ts(full("nident"), full("ident"), -1.0, O.mult)
-    tt(pc(CA), pc(CA), pc(CB), O.subtract)
+    ts(pc(CB), pc(CB), 1.0, O.add)
     ts(full("turn", 136), full("colf", 136), pc(PP), O.is_equal, Q12, O.mult)
+    ts(pc(PG8), pc(PG), 8.0, O.add)
+    tt(pc(CA), pc(CB), pc(CA), O.subtract)
+    ts(pc(CB), pc(CB), -1.0, O.mult)
     for name, v in (("bp", 4096.0), ("bn", -4096.0)):
         ts(full(name, 8), full("colf", 8), pc(PG), O.is_equal, v, O.mult)
-    ts(full("sumf", 143), full("colf", 143), pc(P1615), O.is_equal)
-    ts(full("n64"), full("ident"), -64.0, O.mult)
-    ts(full("i16"), full("ident"), 1.0, O.mult)
-    ts(full("zm", 256), full("cmf", 256), pc(PM), O.is_le)
     ts(full("ct1"), full("cmf"), pc(PM), O.is_gt, 2.0, O.mult)
     ts(full("ct2"), full("cmf"), pc(PM), O.is_equal)
-    fill(A("zm", 0, 256, 16), 0.0)
-    ts(full("ct3"), full("cmf"), 8.0, O.is_lt)
-    tt(full("ct1"), full("ct1"), full("ct2"), O.subtract)
-    ts(full("expn", 512), full("cg", 512), pc(P32), O.is_equal, -1.0, O.mult)
     ts(full("blk"), full("cg"), pc(PG), O.is_equal)
-    fill(A("krow", 0, 136, 17, 0, 1), BIG)
+    ts(full("dsrc"), full("cg"), pc(PG), O.is_equal, 1.0 / 64.0, O.mult)
     ts(pc(WF), full("wti", 1), 1.0, O.mult)
+    tt(full("ct1"), full("ct1"), full("ct2"), O.subtract)
+    tt(full("dsrc"), full("dsrc"), full("junk"), O.add)
+    fill(A("krow", 0, 136, 17, 0, 1), BIG)
+    ts(full("expn", 512), full("cg", 512), pc(P32), O.is_equal, -1.0, O.mult)
+    act(full("kw", 143), full("sumf", 143), F.Copy, scale=pc(WF))
     for h in range(2):
         cp(A("cw0", 144 * h, 144 * h + 128), other("candi", h))
         mm(A("b5", 128 * h, 128 * h + 128), other("want0", h), full("ident"))
-    act(full("wt_0", 256), A("b5", 0, 256), F.Copy)
-    ts(full("kw"), full("blk"), pc(WF), O.mult)
-    cp(row("krow16", 0, 136), row("krow", 0, 136))
-    ts(row("lim", 0, 136), row("krow", 0, 136), -1008.0, O.add)
-    ts(row("krow", 0, 136), row("krow", 0, 136), -1128.0, O.add)
+        act(part("wt_0", h, 1), other("candi", h), F.Copy, bias=-1536.0)
+    for h in range(2):
+        act(part("wt_0", h, 0), A("b5", 128 * h, 128 * h + 128), F.Copy)
+    act(row("krow16", 0, 136), row("krow", 0, 136), F.Copy)
+    act(row("lim", 0, 136), row("krow", 0, 136), F.Copy, bias=-1008.0)
+    act(row("krow", 0, 136), row("krow", 0, 136), F.Copy, bias=-1128.0)
 
-    def consts1():
-        tt(full("pre"), full("ct1"), full("blk"), O.mult)
+    def mounts0():
         for h in range(2):
-            ts(A("me", 256 + 128 * h, 384 + 128 * h), other("mobi", h), -1536.0, O.add, -Q12, O.mult)
-            cp(A("me", 512 + 128 * h, 640 + 128 * h), other("mk0", h))
+            act(A("me", 256 + 128 * h, 384 + 128 * h), other("mobi", h), F.Copy, bias=1536.0 * Q12, scale=-Q12)
+            act(A("me", 512 + 128 * h, 640 + 128 * h), other("mk0", h), F.Copy)
         mm(A("b4", 0, 512), full("i16"), A("me", 256, 768))
 
+    def lasts0():
+        for h in range(2):
+            act(A("last16", 128 * h, 128 * h + 128, 1, 0, 8), other("lasti", h, 8), F.Copy, bias=-1536.0)
+        for k in range(16):
+            mm(A("b7", 496, 512), A("g8", 15 - k, 143 - k, 1, 0, 8), A("last16", k, 256, 16, 0, 8), k == 0, k == 15)
+        act(A("wt_0", 256, 272), A("b7", 496, 512), F.Copy)
+
+    def consts1():
+        ts(full("zm", 256), full("cmf", 256), pc(PM), O.is_le)
+        ts(full("ct2"), full("cmf"), 8.0, O.is_lt)
+        tt(full("pre"), full("ct1"), full("blk"), O.mult)
+        fill(A("zm", 0, 256, 16), 0.0)
+        ts(full("ct2"), full("ct2"), pc(CA), O.mult, pc(CB), O.add)
+
     def consts2():
-        fill(row("crow", 256, 592), 0.0)
-        ts(full("ct2"), full("ct3"), pc(CA), O.mult, pc(CB), O.add)
         fill(row("crow", 0, 128), -5632.0)
-        ts(full("ct2"), full("ct2"), -1.0, O.mult)
         fill(row("crow", 128, 256), -4096.0)
         tt(full("rs"), full("ct2"), full("blk"), O.mult)
         fill(row("crow", 264, 280), 2047.0)
-        fill(A("crow", 288 + 17, 288 + 288, 18, 0, 1), -2047.0 / 64.0)
+        fill(full("zin2", 272), 0.0)
 
     def consts3():
-        ts(full("m16", 16), full("colf", 16), pc(PM), O.is_equal)
-        ts(full("ct1"), full("ident"), -2.0, O.mult)
-        ts(pc(PG8), pc(PG), 8.0, O.add)
-        ts(full("s1", 16), full("m16", 16), -1.0, O.add, 1.0 / 64.0, O.mult)
-        tt(full("ct1"), full("ct1"), full("blk"), O.add)
-        ts(full("s2", 16), full("m16", 16), 1.0 / 64.0, O.mult)
+        fill(full("zz2", 272), 0.0)
+        fill(A("crow", 288 + 17, 288 + 144, 18, 0, 1), -2047.0 / 64.0)
+        fill(A("crow", 288 + 161, 288 + 216, 18, 0, 1), 1.0)
+        ts(pc(PM1), pc(PF), -1.0, O.add)
+        ts(pc(G15), pc(PF), 16.0, O.mult, 15.0, O.add)
         for k in range(4):
-            ts(A("nb", 32 * k, 32 * k + 32), full("cmf", 32), pc(PG8 if k % 2 else PG), O.is_equal, 1.0 if k // 2 else -1.0, O.mult)
-        ts(full("dsrc"), full("ct1"), 1.0 / 64.0, O.mult)
+            ts(A("nb", 48 * k, 48 * k + 48), full("cmf", 48), pc(PG8 if k % 2 else PG), O.is_equal, 1.0 if k // 2 else -1.0, O.mult)
 
     def consts4():
-        ts(full("i64"), full("ident"), 1.0 / 64.0, O.mult)
-        ts(full("rr", 288), full("rr", 288), pc(PM), O.is_equal)
-        ts(pc(DUMP), pc(PM), float(W), O.add)
-        ts(pc(G15), pc(PF), 16.0, O.mult, 15.0, O.add)
-        for h in range(2):
-            ts(A("last16", 128 * h, 128 * h + 128, 1, 0, 8), other("lasti", h, 8), -1536.0, O.add, Q12, O.mult)
         ts(A("g8", 0, 143, 1, 0, 8), A("colf", 0, 143, 1, 0, 8), A("pcol", G15, G15 + 1, 1, 0, 8), O.is_equal)
-        for k in range(16):
-            mm(A("b7", 496, 512), A("g8", 15 - k, 143 - k, 1, 0, 8), A("last16", k, 256, 16, 0, 8), k == 0, k == 15)
+        ts(A("ds", 0, 72), A("ct3", 0, 72), pc(PF), O.is_equal, 1.0 / 64.0, O.mult)
+        ts(A("ds", 72, 144), A("ct3", 0, 72), pc(PM1), O.is_equal, 1.0 / 64.0, O.mult)
+        ts(full("rr", 144), full("rr", 144), pc(PM), O.is_equal)
+        fill(A("rr", 144, 216), 0.0)
+        tt(full("pair", 72), A("ds", 0, 72), A("ds", 72, 144), O.subtract)
 
     def consts5():
-        cp(full("prev", 16), A("b7", 496, 512))
-        for k in range(16):
-            ts(A("sj", 144 * k, 144 * k + 143), full("sumf", 143), A("m16", k, k + 1), O.mult)
+        ts(pc(DUMP), pc(PM), float(W), O.add)
+        ts(pc(DUMP2), pc(PM), float(W + 16), O.add)
+        fill(A("rr", 144, 216, 18), 1.0)
+        fill(A("pair", 0, 72, 18), 0.0)
+        fill(A("pair", 17, 72, 18), 0.0)
+        for k in range(4):
+            act(A("nb", 48 * k + 32, 48 * k + 48), A("nb", 48 * k + 32, 48 * k + 48), F.Copy, scale=Q12)
 
-    def consts6(k0, k1):
+    def shifts(k0, k1):
+        for k in range(k0, k1):
+            act(A("sj", 144 * k, 144 * k + 143), full("sumf", 143), F.Copy, scale=A("m16", k, k + 1))
+
+    def diffs(k0, k1):
         for k in range(k0, k1):
             ts(A("dj", 128 * k, 128 * k + 128), full("dsrc"), A("s1", k, k + 1), O.max, A("s2", k, k + 1), O.min)
 
-    KB_ = ("b3", "b7", "b5", "b4")
+    def key_sums():
+        for c in range(16):
+            mm(A("b3", 0, 192), A("kw", 15 - c, 143 - c), A("featb", 192 * c, 192 * c + 192), c == 0, c == 15)
+        act(full("rk", 192), A("b3", 0, 192), F.Copy, bias=1536.0 - 31.5 / 64.0, scale=1.0 / 64.0)
 
-    def key_a(k):
-        b = A(KB_[k % 2], 0, 512)
-        mm(b, full("kw"), A("featb", 512 * k, 512 * k + 512))
-        act(A("rk", 512 * k, 512 * k + 512), b, F.Copy, bias=1536.0 - 31.5 / 64.0, scale=1.0 / 64.0)
+    def key_mod():
+        ts(full("my", 192), full("rk", 192), -64.0, O.mult, 64.0 * 1536.0, O.add)
+        tt(A("rk", 192, 384), A("b3", 0, 192), full("my", 192), O.add)
 
-    def key_b(k):
-        b = A(("b5", "b7")[k % 2], 0, 512)
-        mm(b, full("n64"), A("rk", 512 * k, 512 * k + 512), True, False)
-        mm(b, full("kw"), A("featb", 512 * k, 512 * k + 512), False, True)
-        ts(A("keys", 512 * k, 512 * k + 512), b, 64.0 * 1536.0, O.add)
+    def key_rows(k, e):
+        b = ("b5", "b7")[k % 2]
+        for c in (2 * k, 2 * k + 1):
+            o = A(b, 192 * (c % 2), 192 * (c % 2) + 192)
+            mm(o, A("dj", 128 * c, 128 * c + 128), A("rk", 192, 384), True, False)
+            mm(o, full("i64"), A("rk", 192, 384), False, True)
+        if e:
+            act(A("keys", 384 * k, 384 * k + 384), A(b, 0, 384), F.Copy, scale=64.0)
+        else:
+            ts(A("keys", 384 * k, 384 * k + 384), A(b, 0, 384), 64.0, O.mult)
 
-    start = {"c1": consts1, "c2": consts2, "c3": consts3, "c4": consts4, "c5": consts5, "c6": lambda: consts6(0, 8), "c7": lambda: consts6(8, 16)}
-    for k in range(6):
-        start["k%d" % k], start["l%d" % k] = lambda k=k: key_a(k), lambda k=k: key_b(k)
+    start = {"c1": consts1, "c2": consts2, "c3": consts3, "c4": consts4, "c5": consts5, "m0": mounts0, "l": lasts0}
+    for k in range(4):
+        start["j%d" % k], start["d%d" % k] = lambda k=k: shifts(4 * k, 4 * k + 4), lambda k=k: diffs(4 * k, 4 * k + 4)
+    start["ks"], start["km"] = key_sums, key_mod
+    for k in range(8):
+        start["k%d" % k], start["l%d" % k] = lambda k=k: key_rows(k, 0), lambda k=k: key_rows(k, 1)
 
     FEAT, KEYS, KIDS = full("featb", W), full("keys", W), A("kt", 0, W)
     ONE = row("ones", 0, 128)
@@ -368,24 +403,22 @@ def rank_program(g, core, T, topo):
             return (lambda: cp(out, src)) if e == "V" else (lambda: act(out, src, F.Copy))
 
         def sub(c, b):
-            mm(A(b, 0, 512), A(wt, 128 * h, 128 * h + 128, 1, 32 * c, 32 * c + 32), A("expn", 0, 512, 1, 32 * c, 32 * c + 32), True, False)
+            mm(A(b, 0, 512), (wt, 32 * c, 32 * c + 32) + part(wt, h, 0)[3:], A("expn", 0, 512, 1, 32 * c, 32 * c + 32), True, False)
             mm(A(b, 0, 512), full("ident"), A("fs", f0 + 512 * c, f0 + 512 * c + 512), False, True)
 
         def kc():
-            mm(A(pb, 136, 272), A("c16", 128 * h, 128 * h + 128), full("turn", 136), True, False)
+            mm(A(pb, 136, 272), part(wt, h, 1), full("turn", 136), True, False)
             mm(A(pb, 136, 272), ONE, row("krow16", 0, 136), False, True)
 
-        def sums(l0, l1):
+        def sums():
             for k in range(16):
-                mm(A(pb, 16 - k, 136, 17, l0, l1), A("da", f0 + 16 * l0 + k, f0 + 16 * l1, 16), full("blk16", 8), False, False)
+                mm(A(pb, 16 - k, 136, 17), A("da", f0 + k, f0 + 2048, 16), full("blk16", 8), False, False)
         for c in range(8):
             d["v%d" % c], d["g%d" % c] = gather("V", 16 * c, 16 * c + 16), gather("S", 16 * c, 16 * c + 16)
         for c in range(4):
             d["V%d" % c], d["G%d" % c] = gather("V", 32 * c, 32 * c + 32), gather("S", 32 * c, 32 * c + 32)
-        d["suma"], d["sumb"], d["sum"] = lambda: sums(0, 64), lambda: sums(64, 128), lambda: sums(0, 128)
-        d["c16"] = lambda: ts(A("c16", 128 * h, 128 * h + 128), A(cw, c0, c0 + 128), -1536.0, O.add)
-        d["kc"] = kc
-        d["p0"] = lambda: mm(A(pb, 0, 136), A("c16", 128 * h, 128 * h + 128), full("turn", 136), True, False)
+        d["kc"], d["sum"] = kc, sums
+        d["p0"] = lambda: mm(A(pb, 0, 136), part(wt, h, 1), full("turn", 136), True, False)
         d["p1"] = lambda: mm(A(pb, 0, 136), ONE, row("lim", 0, 136), False, True)
         d["kcc"] = lambda: act(A("kc", 136 * h, 136 * h + 136), A(pb, 136, 272), F.Copy)
         for j, c in enumerate((2, 0, 3, 1)):
@@ -395,7 +428,7 @@ def rank_program(g, core, T, topo):
         return d
 
     def chain(t, h):
-        wt, co, pb = "wt_%d" % t, "co%d" % t, "b%d" % (2 + h)
+        wt, wn, co, pb = "wt_%d" % t, "wn%d" % t, "co%d" % t, "b%d" % (2 + h)
         final = t == STEPS - 1
         a, b = 128 * h, 128 * h + 128
         best, r8 = A("sc", 136 * h + 16, 136 * h + 136, 17), A("r8", 8 * h, 8 * h + 8)
@@ -413,12 +446,8 @@ def rank_program(g, core, T, topo):
             mm(olp, A("zin", z0 + 1, z0 + 129), full("bp", 8), False, True)
 
         def wm():
-            mm(wp, full("nident"), A(wt, a, b), True, False)
-            mm(wp, A("xo", a, b), full("ident"), False, True)
-
-        def wabs():
-            act(A("wn%d" % t, a, b), wp, F.Abs)
-            m["send"](A("wn%d" % t, a, b), A("wt_%d" % (t + 1), a, b), "arrw%d%d" % (t + 1, h), *link(nxt))
+            mm(wp, full("ni16"), part(wt, h, 0), True, False)
+            mm(wp, A("xo", a, b), full("i16"), False, True)
 
         def fm():
             mm(fp, ONE, row("crow", 128 * final, 128 * final + 128), True, False)
@@ -433,8 +462,8 @@ def rank_program(g, core, T, topo):
             if final:
                 m["send"](A("new", a, b), other("yl", h), "arry%d" % h, *link(home))
             else:
-                ts(A(co, z0, z0 + 128), A("c16o", a, b), 1536.0, O.add)
-                m["send"](A(co, 136 * h, 136 * h + 136), A("cw%d" % (t + 1), 136 * h, 136 * h + 136), "arrc%d%d" % (t + 1, h), *link(nxt))
+                ts(A(co, z0, z0 + 128), part(wn, h, 1), 1536.0, O.add)
+                m["send"](A(co, z0, z0 + 128), A("cw%d" % (t + 1), z0, z0 + 128), "arrc%d%d" % (t + 1, h), *link(nxt))
         d["SCAN"] = lambda: scan(A("sc", 136 * h, 136 * h + 136), A(pb, 0, 136), A("kc", 136 * h, 136 * h + 136), BIG, O.min, O.max)
         d["R"] = lambda: ts(r8, best, MAGIC, O.add, MAGIC, O.subtract)
         d["OD"] = lambda: tt(A("zin", z0, z0 + 128, 16), best, r8, O.subtract)
@@ -442,7 +471,8 @@ def rank_program(g, core, T, topo):
         d["Z"] = lambda: scan(A("zz", z0, z0 + 128), A("zm", 0, 128), A("zin", z0, z0 + 128), 0.0, O.mult, O.add)
         d["ZM"], d["FM"], d["EM"], d["OUT"] = zm, fm, em, out
         if not final:
-            d["W"], d["WABS"] = wm, wabs
+            d["W"], d["WABS"] = wm, lambda: act(part(wn, h, 0), wp, F.Abs)
+            d["REST"] = lambda: m["send"](A(wn, 264 * h, 264 * h + 264), A("wt_%d" % (t + 1), 264 * h, 264 * h + 264), "arrw%d%d" % (t + 1, h), *link(nxt))
             d["XO"] = lambda: act(A("xo", a, b), ("ind", FEAT, OL), F.Copy)
         d["OL"] = lambda: ts(OL, olp, 1536.0, O.add)
         d["HIT"] = lambda: tt(A("hit", a, b), ("ind", KEYS, OL), A("me", 512 + a, 512 + b), O.is_equal)
@@ -453,9 +483,10 @@ def rank_program(g, core, T, topo):
         d["EL"] = lambda: ts(el, ep, 1536.0, O.add)
         d["KA"] = lambda: tt(A("xk", a, b), ("ind", KIDS, OL), A("selc", a, b), O.add)
         d["KB"] = lambda: tt(A("nw", a, b), ("ind", KIDS, el), A("xk", a, b), O.max)
-        d["FIX"] = lambda: tt(A("new" if final else "c16o", a, b), A("nw", a, b), fp, O.add)
-        d["OC"] = lambda: ts(A("oc", 8 * h, 8 * h + 8), OL, -1536.0, O.add)
-        d["VC"] = lambda: tt(A("vc", 8 * h, 8 * h + 8), up, A("oc", 8 * h, 8 * h + 8), O.max)
+        d["FIX"] = lambda: tt(A("new", a, b) if final else part(wn, h, 1), A("nw", a, b), fp, O.add)
+        d["OC"] = lambda: ts(part(wn, h, 2), OL, -1536.0, O.add)
+        d["VC"] = lambda: tt(A("vc", 12 * h, 12 * h + 8), up, part(wn, h, 2), O.max)
+        d["VD"] = lambda: tt(A("vc", 12 * h + 8, 12 * h + 12), up[:5] + (2,), part(wn, h, 2)[:5] + (2,), O.max)
         return d
 
     def post(t):
@@ -464,41 +495,49 @@ def rank_program(g, core, T, topo):
         d = {}
 
         def cnt():
-            mm(row("b7", 368, 496), A("ones", 0, 1), A("ff", 128, 256), True, False)
-            mm(row("b7", 368, 496), A("ones", 0, 1), A("ff", 256, 384), False, True)
-            act(row("junk", 0, 128), row("b7", 368, 496), F.Copy, bias=120.0 / 128.0, scale=16.0 * Q12, acc=row("cs", 0, 1))
+            for k in range(4):
+                mm(row("b7", 440, 504), A("ones", 0, 1), A("ff", 128 + 64 * k, 192 + 64 * k), k == 0, k == 3)
+            act(row("junk", 0, 64), row("b7", 440, 504), F.Copy, bias=120.0 / 64.0, scale=16.0 * Q12, acc=row("cs", 0, 1))
 
         d["rnd"] = lambda: ts(row("cs", 1, 2), row("cs", 0, 1), 256.0 * MAGIC, O.add, 256.0 * MAGIC, O.subtract)
         d["lim"] = lambda: ts(row("lim", 0, 136), row("krow", 0, 136), row("cs", 0, 1), O.add, row("cs", 1, 2), O.subtract)
 
         def nm():
             for h in range(2):
-                o, a = A("b7", 288, 320), 128 * h
-                mm(o, A("zz2", a, a + 128), A("nb", 32 * h, 32 * h + 32), h == 0, False)
-                mm(o, A("zz2", a + 1, a + 129), A("nb", 64 + 32 * h, 96 + 32 * h), False, False)
-                mm(o, A("zin2", a + 1, a + 129), A("nb", 32 * h, 32 * h + 32), False, h == 1)
+                o, a = A("b7", 216, 264), 128 * h
+                mm(o, A("zz2", a, a + 128), A("nb", 48 * h, 48 * h + 48), h == 0, False)
+                mm(o, A("zz2", a + 1, a + 129), A("nb", 96 + 48 * h, 144 + 48 * h), False, False)
+                mm(o, A("zin2", a + 1, a + 129), A("nb", 48 * h, 48 * h + 48), False, h == 1)
 
-        def writers(tag, b0, b1):
+        def writers(h):
+            v0, turned = 12 * h, A("vct", 0, 128, 1, 0, 8)
+
+            def vt():
+                mm(A("b7", 312, 440, 1, 0, 8), A("vc", v0, v0 + 8), full("i16"))
+                act(turned, A("b7", 312, 440, 1, 0, 8), F.Copy)
+
             def dm():
-                mm(A("b7", 18 * b0, 18 * b1), ONE, row("crow", 288 + 18 * b0, 288 + 18 * b1), True, False)
+                mm(A("b7", 0, 216), ONE, row("crow", 288, 504), True, False)
                 for j in range(16):
-                    mm(A("b7", 18 * b0 + 16 - j, 18 * b1, 18), A("dj", 128 * j, 128 * j + 128), A("vc", b0, b1), False, False)
-                mm(A("b7", 18 * b0 + 17, 18 * b1, 18), full("i64"), A("vc", b0, b1), False, True)
-            d["dm" + tag] = dm
-            d["ds" + tag] = lambda: scan(A("ds", 18 * b0, 18 * b1), A("b7", 18 * b0, 18 * b1), A("rr", 18 * b0, 18 * b1), 0.0, O.mult, O.add)
-            d["h2" + tag] = lambda: ts(A("h2", b0, b1), A("ds", 18 * b0 + 17, 18 * b1, 18), 0.0, O.is_equal, 8192.0, O.mult)
-            d["uu" + tag] = lambda: tt(A("u16", b0, b1), A("h2", b0, b1), A("vc", b0, b1), O.add)
-            d["wo" + tag] = lambda: ts(A("wo", 2 * b0, 2 * b1, 2), A("u16", b0, b1), 1536.0, O.add, pc(DUMP), O.min)
-        writers("", 0, 16)
-        writers("0", 0, 8)
-        writers("1", 8, 16)
+                    mm(A("b7", 16 - j, 216, 18), A("dj", 128 * j, 128 * j + 128), A("vc", v0, v0 + 12), False, False)
+                mm(A("b7", 17, 144, 18), full("i64"), A("vc", v0, v0 + 8), False, False)
+                mm(A("b7", 144, 216), turned, A("pair", 0, 72, 1, 0, 8), False, True)
+            d["vt%d" % h], d["dm%d" % h] = vt, dm
+            d["ds%d" % h] = lambda: scan(full("ds", 216), A("b7", 0, 216), full("rr", 216), 0.0, O.mult, O.add)
+            d["h2%d" % h] = lambda: ts(A("h2", v0, v0 + 12), A("ds", 17, 216, 18), 0.0, O.is_equal, 8192.0, O.mult)
+            d["uu%d" % h] = lambda: tt(A("u16", 8 * h, 8 * h + 8), A("h2", v0, v0 + 8), A("vc", v0, v0 + 8), O.add)
+            d["uv%d" % h] = lambda: tt(A("u16", 8 * h + 1, 8 * h + 8, 2), A("u16", 8 * h + 1, 8 * h + 8, 2), A("h2", v0 + 8, v0 + 12), O.add)
+            d["we%d" % h] = lambda: ts(A("wo", 8 * h, 8 * h + 8, 2), A("u16", 8 * h, 8 * h + 8, 2), 1536.0, O.add, pc(DUMP), O.min)
+            d["wo%d" % h] = lambda: ts(A("wo", 8 * h + 1, 8 * h + 8, 2), A("u16", 8 * h + 1, 8 * h + 8, 2), 1536.0, O.add, pc(DUMP2), O.min)
+        writers(0)
+        writers(1)
 
         def shift(j, i):
             return A("sj", 144 * j + 15 - i, 144 * j + 143 - i)
 
         def ext():
             for i in range(16):
-                mm(A("b7", 320, 368), shift((i + 5 * t) % 16, i), A("me", i, 768, 16), i == 0, i == 15)
+                mm(A("b7", 264, 312), shift((i + 5 * t) % 16, i), A("me", i, 768, 16), i == 0, i == 15)
 
         def spread():
             mm(A("b4", 0, 512), full("i16"), A("me", 256, 768), True, False)
@@ -506,25 +545,23 @@ def rank_program(g, core, T, topo):
                 mm(A("b4", i, 512, 16), shift(i, (i + 5 * t) % 16), A("sp", 0, 32), False, False)
                 mm(A("b4", i, 512, 16), shift(i, (i + 5 * t) % 16), A("sp", 32, 64), False, i == 15)
 
-        if t:
-            d["pv"] = lambda: ts(full("prev", 16), A("cw%d" % t, 128, 144), -1536.0, O.add, Q12, O.mult)
-        d["dp"] = lambda: tt(A("sp", 32, 48), full("prev", 16), full("nas", 16), O.mult)
+        d["dp"] = lambda: tt(A("sp", 32, 48), A("wt_%d" % t, 256, 272), A("nas", 32, 48), O.mult)
 
-        todo = list(range(8, 16)) + list(range(8))
+        todo = list(range(4, 8)) + list(range(4))
 
         def scatter():
             b = todo.pop()
-            src = A("new", 16 * b, 16 * b + 16) if final else A(co, 16 * b + 16 * (b // 8), 16 * b + 16 * (b // 8) + 16)
-            cp(("ind", A("kf" if final else "kt", 0, W + 16), A("wo", 2 * b, 2 * b + 1)), src)
+            src = A("new", 32 * b, 32 * b + 32) if final else A(co, 32 * b + 16 * (b // 4), 32 * b + 16 * (b // 4) + 32)
+            cp(("ind", A("kf" if final else "kt", 0, W + 32), A("wo", 2 * b, 2 * b + 2)), src)
         d["cnt"], d["nm"], d["ext"], d["spread"], d["s"] = cnt, nm, ext, spread, scatter
         d["ck"] = lambda: act(full("me", 256), ("ind", KEYS, A(co, 128, 144)), F.Copy, scale=-1.0)
         d["nz"] = lambda: scan(full("zz2", 256), full("zm", 256), full("zin2", 256), 0.0, O.mult, O.add)
-        d["nas"] = lambda: cp(full("nas", 32), A("b7", 288, 320))
-        d["dk"] = lambda: tt(A("sp", 48, 64), A("b7", 320, 336), full("nas", 16), O.mult)
-        d["dq"] = lambda: tt(A("sp", 0, 32), A("b7", 336, 368), full("nas", 32), O.mult)
+        d["nas"] = lambda: cp(full("nas", 48), A("b7", 216, 264))
+        d["dk"] = lambda: tt(A("sp", 48, 64), A("b7", 264, 280), full("nas", 16), O.mult)
+        d["dq"] = lambda: tt(A("sp", 0, 32), A("b7", 280, 312), full("nas", 32), O.mult)
         d["mkc"] = lambda: act(A("me", 256, 768), A("b4", 0, 512), F.Copy)
         if t == STEPS - 2:
-            d["kf"] = lambda: m["copy"]("Y", full("kf", W + 16), full("kt", W + 16), "ld_kf")
+            d["kf"] = lambda: m["copy"]("Y", full("kf", W + 32), full("kt", W + 32), "ld_kf")
         return d
 
     def ymu0():
@@ -555,7 +592,7 @@ def rank_program(g, core, T, topo):
         if p and h == 0:
             ps = post(t - 1)
         calls.update(ps if p > 1 else start)
-        for name in ORDER[2 + p if p < 2 else 4 if t == STEPS else h].split():
+        for name in ORDER[2 + p if p < 2 else p - 7 if p > 10 else h].split():
             if name in calls:
                 calls[name]()
     m["finish"]([("arry0", link(home)[2]), ("arry1", link(home)[2])] + [("ld_" + x, 16) for x in LOADS])

@@ -4,6 +4,7 @@ W, L, STEPS = 3072, 256, 6
 MAGIC = 12582912.0
 BIG = 4000.0
 Q12 = 1.0 / 4096.0
+YD = (0, 192, 576, 1056, 1536)
 
 SCRATCH = {}
 
@@ -12,11 +13,11 @@ def _buffers():
     for dtype, names in (
         ("float32", "colf 144 cmf 256 pcol 32 m16 16 s1 16 s2 16 ct1 128 ct2 128 ct3 128 krow 136 kc 272 sc 272 r8 16 xk 256 nw 256 new 256 "
                     "rr 216 ds 216 h2 24 u16 16 cs 2 junk 128 my 256 mt 256 yl 256 ydb 1536"),
-        ("bfloat16", "featb 3072 keys 3072 cg 512 mk0 256 want0 256 ident 128 blk 128 blk16 8 pre 128 kw 144 fs 4096 da 4096 hit 256 selc 256"),
-        ("float16", "expn 512 xo 256 ni16 128 turn 136 ones 128 krow16 136 lim 136 bp 8 bn 8 nb 192 zm 256 zin 288 zz 288 zin2 272 zz2 272 rs 128 "
-                    "crow 512 sumf 144 sj 2304 dsrc 128 dj 2048 i64 128 i16 128 rk 384 me 768 ff 512 vc 24 vct 128 pair 72 nas 48 sp 64 "
+        ("bfloat16", "featb 6144 keys 3072 kcb 192 cg 512 mk0 256 want0 256 ident 128 blk 128 blk16 8 pre 128 kw 144 fs 4096 da 4096 hit 256 selc 256"),
+        ("float16", "expn 512 xo 256 ni16 128 turn 136 ones 128 krow16 136 lim 136 bp 8 bn 8 nb 256 zm 256 zin 288 zz 288 zin2 272 zz2 272 rs 128 "
+                    "crow 512 sumf 144 sj 2304 dsrc 128 dj 2048 i64 128 i16 128 rk 192 me 768 ff 512 vc 24 vct 128 pair 72 nas 64 sp 64 "
                     "last16 256 g8 144"),
-        ("int32", "candi 256 kt 3104 kf 3104 mobi 256 lasti 256 wti 1 pint 16"),
+        ("int32", "candi 256 kt 3104 mobi 256 lasti 256 wti 1 pint 16"),
         ("uint16", "el 16 wo 16"),
     ):
         words = names.split()
@@ -24,17 +25,19 @@ def _buffers():
             SCRATCH[words[k]] = ("sbuf", [128, int(words[k + 1])], dtype)
     for t in range(STEPS):
         SCRATCH["cw%d" % t] = ("sbuf", [128, 272], "uint16")
+        SCRATCH["cu%d" % t] = ("sbuf", [128, 256], "uint16")
         SCRATCH["co%d" % t] = ("sbuf", [128, 272], "uint16")
         SCRATCH["wt_%d" % t] = ("sbuf", [128, 528], "float16")
         SCRATCH["wn%d" % t] = ("sbuf", [128, 528], "float16")
+    SCRATCH["kd"] = ("dram", [8, W], "bfloat16")
     for b in range(8):
         SCRATCH["b%d" % b] = ("psum", [128, 512], "float32")
 
 
 _buffers()
-LOADS = ["cand", "feat0", "feat1", "want", "wts", "last", "mkey", "mobj", "kids", "kf"]
-SEMAPHORES = ["sv", "ss", "sp", "sg", "lsem", "arry0", "arry1", "oyn", "omu"] + ["ld_" + x for x in LOADS] + ["oyd%d" % k for k in range(4)]
-SEMAPHORES += ["arr%s%d%d" % (x, k, h) for x in "wc" for k in range(1, STEPS) for h in range(2)]
+LOADS = ["cand", "feat0", "feat1", "feat2", "want", "wts", "last", "mkey", "mobj", "kids", "kd"]
+SEMAPHORES = ["sv", "ss", "sp", "sg", "lsem", "skeys", "arry0", "arry1", "oyn0", "oyn1", "omu"] + ["ld_" + x for x in LOADS]
+SEMAPHORES += ["oyd%d" % k for k in range(4)] + ["arr%s%d%d" % (x, k, h) for x in "wc" for k in range(1, STEPS) for h in range(2)]
 
 
 def A(name, c0, c1, step=1, p0=0, p1=128):
@@ -165,7 +168,13 @@ def machine(g, T):
         order(e, [a], [out])
         q[e].dma_start(ap(out), ap(a)).then_inc(T.sem[s], 16)
         hist.setdefault(out[0], []).append([out, True, "D", s, 16, dict(clock[e])])
-        hist.setdefault(a[0], []).append([a, False, "D", s, 16, dict(clock[e])])
+
+    def rows(e, out, a, s):
+        order(e, [a], [out])
+        for i in range(16):
+            q[e].dma_start(T[out[0]][i:128:16, :], ap(a)).then_inc(T.sem[s], 16)
+        hist.setdefault(out[0], []).append([out, True, "D", s, 256, dict(clock[e])])
+        count[s] = 256
 
     def store(e, dst, a, s):
         order(e, a, [])
@@ -183,16 +192,17 @@ def machine(g, T):
             if clock["G"].get(s, 0) < v:
                 g.wait_ge(T.sem[s], v)
 
-    return dict(tt=tt, ts=ts, cp=cp, fill=fill, scan=scan, act=act, mm=mm, iota=iota, load=load, copy=copy, store=store, send=send, finish=finish)
+    return dict(tt=tt, ts=ts, cp=cp, fill=fill, scan=scan, act=act, mm=mm, iota=iota, load=load, copy=copy, rows=rows, store=store,
+                send=send, finish=finish)
 
 
 ORDER = [
-    'SCAN R NA vt0 OD Z dm0 ZM nz OL XO ds0 HIT ck X OC h20 uu0 FI uv0 nm G3 nas FE v0 v1 FM SELC KA cnt EM EL wo0 kc G2 VD W VC sub3 kcc KB rnd we0 FIX lim vt1 OUT v3 v2 dp s sub2 WABS sub0 dm1 ds1 s h21 uu1 s abs2 sub1 uv1 abs0 we1 ext s dk wo1 dq abs3 p0 abs1 sum p1 REST spread',
-    'v3 G2 SCAN s kc R G3 v0 OD Z ZM sub2 v1 sub0 mkc OL s HIT kcc X abs2 abs0 OC v2 s sub3 NA abs3 FI s sub1 FM SELC FE EM XO W KA abs1 p0 sum EL p1 VC KB FIX VD OUT WABS REST',
-    'd1 c1 c2 kc v1 kcc v3 j0 G2 G3 ks v0 sub2 d0 sub0 km m0 abs2 v2 k1 j1 sub1 d3 k0 d2 sub3 k3 abs0 abs1 k2 abs3 p0 sum p1',
-    'v0 kc v2 j2 G2 SCAN k5 k4 sub2 G3 R OD j3 Z l7 l6 abs2 v1 ZM OL sub0 abs0 v3 kcc NA OC HIT sub3 abs3 c3 X FI FE sub1 c4 XO FM SELC EM EL W abs1 p0 sum p1 VC WABS KA KB FIX VD l REST c5 OUT',
-    'kc G2 v0 s G3 SCAN sub2 v1 mkc R s OD kcc s Z abs2 ZM v2 s sub3 OL NA kf abs3 sub0 abs0 HIT v3 OC X FI FE sub1 FM SELC KA EM EL KB VC p0 VD abs1 sum p1 FIX OUT',
-    'SCAN R OD Z vt0 NA nz dm0 ds0 ZM OL ck h20 HIT uu0 nm we0 uv0 OC X FI FE ext nas dp wo0 dq FM SELC KA EM dk VC EL vt1 VD dm1 s KB s spread s s FIX ds1 h21 uu1 uv1 we1 wo1 s s my0 my1 s OUT my2 s yn yd2 yd1 yd0 yd3',
+    'vt0 dm0 SCAN R OD Z ZM NA nz OL HIT nm OC nas ck ds0 X FI XO W h20 G3 FE FM SELC cnt uu0 kc G2 WABS EM kcc g3 V0 sub3 KA VC vt1 EL KB VD rnd uv0 OUT we0 wo0 v2 sub2 abs2 FIX s lim sub0 dm1 s sub1 REST abs0 ds1 p0 p1 abs3 abs1 CO ext s sum h21 uu1 s uv1 we1 dq spread wo1',
+    'v2 G3 G2 SCAN s R OD mkc kc Z ZM V0 g3 sub2 sub0 OL NA HIT kcc abs2 s abs0 X sub3 XO FI s FM SELC FE s KA OC sub1 EM EL VC VD W KB FIX p0 abs3 p1 OUT CO abs1 sum WABS REST',
+    'G2 G3 kc kcc c0 c1 V0 ks sub2 abs2 sub3 abs3 V1 sub1 km j0 abs1 sub0 abs0 p0 p1 c2 sum m0',
+    'G2 c3 c4 SCAN j3 v1 R v0 G3 OD d2 Z kc j2 v2 sub2 sub0 ZM abs2 sub3 v3 sub1 abs3 OL d3 HIT kcc c5 X FI FM FE abs0 abs1 d0 OC SELC NA KA EM EL XO W VD l p0 p1 VC KB OUT j1 FIX sum d1 WABS REST CO',
+    'G2 v3 SCAN R sub2 s G3 OD v1 mkc Z v0 ZM abs2 sub3 abs3 OL s HIT sub0 abs0 v2 OC X FI s FE kc kcc NA sub1 FM SELC EM s KA EL VC KB VD FIX p0 p1 abs1 sum OUT',
+    'yn0 SCAN R OD vt0 NA Z dm0 ds0 ZM OL ck nz HIT nm h20 X FI uu0 FE uv0 wo0 ext FM nas OC SELC KA EM VC vt1 we0 VD EL KB FIX s OUT s dm1 ds1 yn1 s h21 dq uu1 s uv1 we1 wo1 s s s s spread my0 my1 my2 yd0 yd1 yd2 yd3',
 ]
 
 
@@ -235,9 +245,9 @@ def rank_program(g, core, T, topo):
 
     iota(full("pint", 1), [[0, 1]], 0, 1, False)
     iota(full("colf", 144), [[1, 144]], 0, 0)
-    iota(full("cmf", 256), [[0, 16], [1, 16]], 0, 0)
     iota(full("cg", 512), [[1, 32], [0, 16]], 0, 0)
     iota(row("krow", 0, 136), [[0, 8], [-1, 17]], 16, 0)
+    iota(full("cmf", 256), [[0, 16], [1, 16]], 0, 0)
     iota(full("rr", 144), [[0, 8], [-1, 18]], 16, 0)
     iota(A("ct3", 0, 72), [[2, 4], [0, 18]], 0, 0)
     iota(A("kt", W, W + 32), [[0, 32]], 0, 0, False)
@@ -278,25 +288,20 @@ def rank_program(g, core, T, topo):
     ts(full("turn", 136), full("colf", 136), pc(PP), O.is_equal, Q12, O.mult)
     ts(pc(PG8), pc(PG), 8.0, O.add)
     tt(pc(CA), pc(CB), pc(CA), O.subtract)
-    ts(pc(CB), pc(CB), -1.0, O.mult)
+    ts(pc(CB), pc(CB), -0.75, O.mult)
     for name, v in (("bp", 4096.0), ("bn", -4096.0)):
         ts(full(name, 8), full("colf", 8), pc(PG), O.is_equal, v, O.mult)
-    ts(full("ct1"), full("cmf"), pc(PM), O.is_gt, 2.0, O.mult)
-    ts(full("ct2"), full("cmf"), pc(PM), O.is_equal)
-    ts(full("blk"), full("cg"), pc(PG), O.is_equal)
-    ts(full("dsrc"), full("cg"), pc(PG), O.is_equal, 1.0 / 64.0, O.mult)
+    ts(pc(CA), pc(CA), 0.75, O.mult)
     ts(pc(WF), full("wti", 1), 1.0, O.mult)
-    tt(full("ct1"), full("ct1"), full("ct2"), O.subtract)
-    tt(full("dsrc"), full("dsrc"), full("junk"), O.add)
-    fill(A("krow", 0, 136, 17, 0, 1), BIG)
-    ts(full("expn", 512), full("cg", 512), pc(P32), O.is_equal, -1.0, O.mult)
     act(full("kw", 143), full("sumf", 143), F.Copy, scale=pc(WF))
+    ts(full("expn", 512), full("cg", 512), pc(P32), O.is_equal, -1.0, O.mult)
     for h in range(2):
         cp(A("cw0", 144 * h, 144 * h + 128), other("candi", h))
         mm(A("b5", 128 * h, 128 * h + 128), other("want0", h), full("ident"))
         act(part("wt_0", h, 1), other("candi", h), F.Copy, bias=-1536.0)
     for h in range(2):
         act(part("wt_0", h, 0), A("b5", 128 * h, 128 * h + 128), F.Copy)
+    fill(A("krow", 0, 136, 17, 0, 1), BIG)
     act(row("krow16", 0, 136), row("krow", 0, 136), F.Copy)
     act(row("lim", 0, 136), row("krow", 0, 136), F.Copy, bias=-1008.0)
     act(row("krow", 0, 136), row("krow", 0, 136), F.Copy, bias=-1128.0)
@@ -314,6 +319,14 @@ def rank_program(g, core, T, topo):
             mm(A("b7", 496, 512), A("g8", 15 - k, 143 - k, 1, 0, 8), A("last16", k, 256, 16, 0, 8), k == 0, k == 15)
         act(A("wt_0", 256, 272), A("b7", 496, 512), F.Copy)
 
+    def consts0():
+        ts(full("ct1"), full("cmf"), pc(PM), O.is_gt, 2.0, O.mult)
+        ts(full("ct2"), full("cmf"), pc(PM), O.is_equal)
+        ts(full("blk"), full("cg"), pc(PG), O.is_equal)
+        ts(full("dsrc"), full("cg"), pc(PG), O.is_equal, 1.0 / 64.0, O.mult)
+        tt(full("ct1"), full("ct1"), full("ct2"), O.subtract)
+        tt(full("dsrc"), full("dsrc"), full("junk"), O.add)
+
     def consts1():
         ts(full("zm", 256), full("cmf", 256), pc(PM), O.is_le)
         ts(full("ct2"), full("cmf"), 8.0, O.is_lt)
@@ -322,8 +335,8 @@ def rank_program(g, core, T, topo):
         ts(full("ct2"), full("ct2"), pc(CA), O.mult, pc(CB), O.add)
 
     def consts2():
-        fill(row("crow", 0, 128), -5632.0)
-        fill(row("crow", 128, 256), -4096.0)
+        fill(row("crow", 0, 128), -4608.0)
+        fill(row("crow", 128, 256), -3072.0)
         tt(full("rs"), full("ct2"), full("blk"), O.mult)
         fill(row("crow", 264, 280), 2047.0)
         fill(full("zin2", 272), 0.0)
@@ -335,7 +348,7 @@ def rank_program(g, core, T, topo):
         ts(pc(PM1), pc(PF), -1.0, O.add)
         ts(pc(G15), pc(PF), 16.0, O.mult, 15.0, O.add)
         for k in range(4):
-            ts(A("nb", 48 * k, 48 * k + 48), full("cmf", 48), pc(PG8 if k % 2 else PG), O.is_equal, 1.0 if k // 2 else -1.0, O.mult)
+            ts(A("nb", 64 * k, 64 * k + 64), full("cmf", 64), pc(PG8 if k % 2 else PG), O.is_equal, 1.0 if k // 2 else -1.0, O.mult)
 
     def consts4():
         ts(A("g8", 0, 143, 1, 0, 8), A("colf", 0, 143, 1, 0, 8), A("pcol", G15, G15 + 1, 1, 0, 8), O.is_equal)
@@ -352,7 +365,7 @@ def rank_program(g, core, T, topo):
         fill(A("pair", 0, 72, 18), 0.0)
         fill(A("pair", 17, 72, 18), 0.0)
         for k in range(4):
-            act(A("nb", 48 * k + 32, 48 * k + 48), A("nb", 48 * k + 32, 48 * k + 48), F.Copy, scale=Q12)
+            act(A("nb", 64 * k, 64 * k + 16), A("nb", 64 * k, 64 * k + 16), F.Copy, scale=Q12)
 
     def shifts(k0, k1):
         for k in range(k0, k1):
@@ -366,28 +379,18 @@ def rank_program(g, core, T, topo):
         for c in range(16):
             mm(A("b3", 0, 192), A("kw", 15 - c, 143 - c), A("featb", 192 * c, 192 * c + 192), c == 0, c == 15)
         act(full("rk", 192), A("b3", 0, 192), F.Copy, bias=1536.0 - 31.5 / 64.0, scale=1.0 / 64.0)
+        act(full("my", 192), full("rk", 192), F.Copy, bias=64.0 * 1536.0, scale=-64.0)
 
     def key_mod():
-        ts(full("my", 192), full("rk", 192), -64.0, O.mult, 64.0 * 1536.0, O.add)
-        tt(A("rk", 192, 384), A("b3", 0, 192), full("my", 192), O.add)
+        tt(full("kcb", 192), A("b3", 0, 192), full("my", 192), O.add)
+        m["copy"]("Y", A("kd", 0, W, 1, 0, 8), full("kcb", 192), "ld_kd")
+        m["rows"]("Y", full("keys", W), A("kd", 0, W, 1, 0, 8), "skeys")
+        load("Y", A("featb", W, 2 * W), T.feat[:, :], "ld_feat2")
 
-    def key_rows(k, e):
-        b = ("b5", "b7")[k % 2]
-        for c in (2 * k, 2 * k + 1):
-            o = A(b, 192 * (c % 2), 192 * (c % 2) + 192)
-            mm(o, A("dj", 128 * c, 128 * c + 128), A("rk", 192, 384), True, False)
-            mm(o, full("i64"), A("rk", 192, 384), False, True)
-        if e:
-            act(A("keys", 384 * k, 384 * k + 384), A(b, 0, 384), F.Copy, scale=64.0)
-        else:
-            ts(A("keys", 384 * k, 384 * k + 384), A(b, 0, 384), 64.0, O.mult)
-
-    start = {"c1": consts1, "c2": consts2, "c3": consts3, "c4": consts4, "c5": consts5, "m0": mounts0, "l": lasts0}
+    start = {"c0": consts0, "c1": consts1, "c2": consts2, "c3": consts3, "c4": consts4, "c5": consts5, "m0": mounts0, "l": lasts0,
+             "ks": key_sums, "km": key_mod}
     for k in range(4):
         start["j%d" % k], start["d%d" % k] = lambda k=k: shifts(4 * k, 4 * k + 4), lambda k=k: diffs(4 * k, 4 * k + 4)
-    start["ks"], start["km"] = key_sums, key_mod
-    for k in range(8):
-        start["k%d" % k], start["l%d" % k] = lambda k=k: key_rows(k, 0), lambda k=k: key_rows(k, 1)
 
     FEAT, KEYS, KIDS = full("featb", W), full("keys", W), A("kt", 0, W)
     ONE = row("ones", 0, 128)
@@ -399,7 +402,7 @@ def rank_program(g, core, T, topo):
         d = {}
 
         def gather(e, l0, l1):
-            out, src = A("fs", f0 + 16 * l0, f0 + 16 * l1), ("ind", FEAT, A(cw, c0 + l0, c0 + l1))
+            out, src = A("fs", f0 + 16 * l0, f0 + 16 * l1), ("ind", full("featb", 2 * W) if t else FEAT, A(cw, c0 + l0, c0 + l1))
             return (lambda: cp(out, src)) if e == "V" else (lambda: act(out, src, F.Copy))
 
         def sub(c, b):
@@ -412,14 +415,14 @@ def rank_program(g, core, T, topo):
 
         def sums():
             for k in range(16):
-                mm(A(pb, 16 - k, 136, 17), A("da", f0 + k, f0 + 2048, 16), full("blk16", 8), False, False)
+                mm(A(pb, 16 - k, 136, 17), A("da", f0 + k, f0 + 2048, 16), full("blk16", 8), False, k == 15)
         for c in range(8):
             d["v%d" % c], d["g%d" % c] = gather("V", 16 * c, 16 * c + 16), gather("S", 16 * c, 16 * c + 16)
         for c in range(4):
             d["V%d" % c], d["G%d" % c] = gather("V", 32 * c, 32 * c + 32), gather("S", 32 * c, 32 * c + 32)
         d["kc"], d["sum"] = kc, sums
         d["p0"] = lambda: mm(A(pb, 0, 136), part(wt, h, 1), full("turn", 136), True, False)
-        d["p1"] = lambda: mm(A(pb, 0, 136), ONE, row("lim", 0, 136), False, True)
+        d["p1"] = lambda: mm(A(pb, 0, 136), ONE, row("lim", 0, 136), False, False)
         d["kcc"] = lambda: act(A("kc", 136 * h, 136 * h + 136), A(pb, 136, 272), F.Copy)
         for j, c in enumerate((2, 0, 3, 1)):
             b = SUB[(4 * h + 8 * t + j) % 3]
@@ -462,8 +465,8 @@ def rank_program(g, core, T, topo):
             if final:
                 m["send"](A("new", a, b), other("yl", h), "arry%d" % h, *link(home))
             else:
-                ts(A(co, z0, z0 + 128), part(wn, h, 1), 1536.0, O.add)
-                m["send"](A(co, z0, z0 + 128), A("cw%d" % (t + 1), z0, z0 + 128), "arrc%d%d" % (t + 1, h), *link(nxt))
+                cp(A("cu%d" % t, a, b), A("nw", a, b))
+                m["send"](A("cu%d" % t, a, b), A("cw%d" % (t + 1), z0, z0 + 128), "arrc%d%d" % (t + 1, h), *link(nxt))
         d["SCAN"] = lambda: scan(A("sc", 136 * h, 136 * h + 136), A(pb, 0, 136), A("kc", 136 * h, 136 * h + 136), BIG, O.min, O.max)
         d["R"] = lambda: ts(r8, best, MAGIC, O.add, MAGIC, O.subtract)
         d["OD"] = lambda: tt(A("zin", z0, z0 + 128, 16), best, r8, O.subtract)
@@ -472,14 +475,16 @@ def rank_program(g, core, T, topo):
         d["ZM"], d["FM"], d["EM"], d["OUT"] = zm, fm, em, out
         if not final:
             d["W"], d["WABS"] = wm, lambda: act(part(wn, h, 0), wp, F.Abs)
-            d["REST"] = lambda: m["send"](A(wn, 264 * h, 264 * h + 264), A("wt_%d" % (t + 1), 264 * h, 264 * h + 264), "arrw%d%d" % (t + 1, h), *link(nxt))
+            d["REST"] = lambda: m["send"](A(wn, 264 * h, 264 * h + 264), A("wt_%d" % (t + 1), 264 * h, 264 * h + 264),
+                                          "arrw%d%d" % (t + 1, h), *link(nxt))
+            d["CO"] = lambda: ts(A(co, z0, z0 + 128), part(wn, h, 1), 1536.0, O.add)
             d["XO"] = lambda: act(A("xo", a, b), ("ind", FEAT, OL), F.Copy)
         d["OL"] = lambda: ts(OL, olp, 1536.0, O.add)
         d["HIT"] = lambda: tt(A("hit", a, b), ("ind", KEYS, OL), A("me", 512 + a, 512 + b), O.is_equal)
         d["X"] = lambda: mm(xp, full("pre"), A("hit", a, b))
         d["FI"] = lambda: ts(fi, xp, 0.0, O.is_lt, -4096.0, O.mult)
         d["FE"] = lambda: tt(fe, fi, A("b4", a, b), O.mult)
-        d["SELC"] = lambda: act(A("selc", a, b), fp, F.Copy, bias=-4096.0 if final else -7168.0, scale=-2.0)
+        d["SELC"] = lambda: act(A("selc", a, b), fp, F.Copy, bias=-3072.0 if final else -6144.0, scale=-2.0)
         d["EL"] = lambda: ts(el, ep, 1536.0, O.add)
         d["KA"] = lambda: tt(A("xk", a, b), ("ind", KIDS, OL), A("selc", a, b), O.add)
         d["KB"] = lambda: tt(A("nw", a, b), ("ind", KIDS, el), A("xk", a, b), O.max)
@@ -495,26 +500,26 @@ def rank_program(g, core, T, topo):
         d = {}
 
         def cnt():
-            for k in range(4):
-                mm(row("b7", 440, 504), A("ones", 0, 1), A("ff", 128 + 64 * k, 192 + 64 * k), k == 0, k == 3)
-            act(row("junk", 0, 64), row("b7", 440, 504), F.Copy, bias=120.0 / 64.0, scale=16.0 * Q12, acc=row("cs", 0, 1))
+            for k in range(8):
+                mm(row("b7", 472, 504), A("ones", 0, 1), A("ff", 128 + 32 * k, 160 + 32 * k), k == 0, k == 7)
+            act(row("junk", 0, 32), row("b7", 472, 504), F.Copy, bias=120.0 / 32.0, scale=16.0 * Q12, acc=row("cs", 0, 1))
 
         d["rnd"] = lambda: ts(row("cs", 1, 2), row("cs", 0, 1), 256.0 * MAGIC, O.add, 256.0 * MAGIC, O.subtract)
         d["lim"] = lambda: ts(row("lim", 0, 136), row("krow", 0, 136), row("cs", 0, 1), O.add, row("cs", 1, 2), O.subtract)
 
         def nm():
             for h in range(2):
-                o, a = A("b7", 216, 264), 128 * h
-                mm(o, A("zz2", a, a + 128), A("nb", 48 * h, 48 * h + 48), h == 0, False)
-                mm(o, A("zz2", a + 1, a + 129), A("nb", 96 + 48 * h, 144 + 48 * h), False, False)
-                mm(o, A("zin2", a + 1, a + 129), A("nb", 48 * h, 48 * h + 48), False, h == 1)
+                o, a = A("b7", 216, 280), 128 * h
+                mm(o, A("zz2", a, a + 128), A("nb", 64 * h, 64 * h + 64), h == 0, False)
+                mm(o, A("zz2", a + 1, a + 129), A("nb", 128 + 64 * h, 192 + 64 * h), False, False)
+                mm(o, A("zin2", a + 1, a + 129), A("nb", 64 * h, 64 * h + 64), False, h == 1)
 
         def writers(h):
             v0, turned = 12 * h, A("vct", 0, 128, 1, 0, 8)
 
             def vt():
-                mm(A("b7", 312, 440, 1, 0, 8), A("vc", v0, v0 + 8), full("i16"))
-                act(turned, A("b7", 312, 440, 1, 0, 8), F.Copy)
+                mm(A("b7", 344, 472, 1, 0, 8), A("vc", v0, v0 + 8), full("i16"))
+                act(turned, A("b7", 344, 472, 1, 0, 8), F.Copy)
 
             def dm():
                 mm(A("b7", 0, 216), ONE, row("crow", 288, 504), True, False)
@@ -536,8 +541,9 @@ def rank_program(g, core, T, topo):
             return A("sj", 144 * j + 15 - i, 144 * j + 143 - i)
 
         def ext():
+            mm(A("b7", 280, 296), full("i16"), A("wt_%d" % t, 256, 272), True, False)
             for i in range(16):
-                mm(A("b7", 264, 312), shift((i + 5 * t) % 16, i), A("me", i, 768, 16), i == 0, i == 15)
+                mm(A("b7", 296, 344), shift((i + 5 * t) % 16, i), A("me", i, 768, 16), False, i == 15)
 
         def spread():
             mm(A("b4", 0, 512), full("i16"), A("me", 256, 768), True, False)
@@ -545,23 +551,18 @@ def rank_program(g, core, T, topo):
                 mm(A("b4", i, 512, 16), shift(i, (i + 5 * t) % 16), A("sp", 0, 32), False, False)
                 mm(A("b4", i, 512, 16), shift(i, (i + 5 * t) % 16), A("sp", 32, 64), False, i == 15)
 
-        d["dp"] = lambda: tt(A("sp", 32, 48), A("wt_%d" % t, 256, 272), A("nas", 32, 48), O.mult)
-
         todo = list(range(4, 8)) + list(range(4))
 
         def scatter():
             b = todo.pop()
             src = A("new", 32 * b, 32 * b + 32) if final else A(co, 32 * b + 16 * (b // 4), 32 * b + 16 * (b // 4) + 32)
-            cp(("ind", A("kf" if final else "kt", 0, W + 32), A("wo", 2 * b, 2 * b + 2)), src)
+            cp(("ind", A("kt", 0, W + 32), A("wo", 2 * b, 2 * b + 2)), src)
         d["cnt"], d["nm"], d["ext"], d["spread"], d["s"] = cnt, nm, ext, spread, scatter
         d["ck"] = lambda: act(full("me", 256), ("ind", KEYS, A(co, 128, 144)), F.Copy, scale=-1.0)
         d["nz"] = lambda: scan(full("zz2", 256), full("zm", 256), full("zin2", 256), 0.0, O.mult, O.add)
-        d["nas"] = lambda: cp(full("nas", 48), A("b7", 216, 264))
-        d["dk"] = lambda: tt(A("sp", 48, 64), A("b7", 264, 280), full("nas", 16), O.mult)
-        d["dq"] = lambda: tt(A("sp", 0, 32), A("b7", 280, 312), full("nas", 32), O.mult)
+        d["nas"] = lambda: cp(full("nas", 64), A("b7", 216, 280))
+        d["dq"] = lambda: tt(full("sp", 64), A("b7", 280, 344), full("nas", 64), O.mult)
         d["mkc"] = lambda: act(A("me", 256, 768), A("b4", 0, 512), F.Copy)
-        if t == STEPS - 2:
-            d["kf"] = lambda: m["copy"]("Y", full("kf", W + 32), full("kt", W + 32), "ld_kf")
         return d
 
     def ymu0():
@@ -574,12 +575,14 @@ def rank_program(g, core, T, topo):
             m["store"]("Y", T.ymu[:, :], [full("my", 256)], "omu")
 
     def yd(k):
-        c0, c1 = 384 * k, 384 * k + 384
-        b = A(SUB[k % 3], 0, 384)
-        act(b, A("kf", 1536 + c0, 1536 + c1), F.Copy, scale=2.0)
-        tt(A("ydb", c0, c1), A("kf", c0, c1), b, O.add)
+        c0, c1 = YD[k], YD[k + 1]
+        b = A(SUB[k % 3], 0, c1 - c0)
+        act(b, A("kt", 1536 + c0, 1536 + c1), F.Copy, scale=2.0)
+        tt(A("ydb", c0, c1), A("kt", c0, c1), b, O.add)
         m["store"]("Y", T.yd[:, c0:c1], [A("ydb", c0, c1)], "oyd%d" % k)
-    ends = {"my0": ymu0, "my1": lambda: ymu1(0), "my2": lambda: ymu1(1), "yn": lambda: m["store"]("S", T.yn[:, :], [full("yl", 256)], "oyn")}
+    ends = {"my0": ymu0, "my1": lambda: ymu1(0), "my2": lambda: ymu1(1)}
+    for h in range(2):
+        ends["yn%d" % h] = lambda h=h: m["store"]("Y", T.yn[:, 128 - 128 * h:256 - 128 * h], [other("yl", h)], "oyn%d" % h)
     for k in range(4):
         ends["yd%d" % k] = lambda k=k: yd(k)
 

from concourse.mybir import AluOpType, ActivationFunctionType

W, L, STEPS = 3072, 256, 6
MAGIC = 12582912.0
BIG = 4000.0
Q12 = 1.0 / 4096.0
YD = (0, 192, 576, 1056, 1536)

SCRATCH = {}


def _buffers():
    for dtype, names in (
        ("float32", "colf 144 cmf 256 pcol 32 m16 16 s1 16 s2 16 ct1 128 ct2 128 ct3 128 krow 136 kc 272 sc 272 r8 16 xk 256 nw 256 new 256 "
                    "rr 216 ds 216 h2 24 u16 16 cs 2 junk 128 my 256 mt 256 yl 256 ydb 1536"),
        ("bfloat16", "featb 6144 keys 3072 kcb 192 cg 512 mk0 256 want0 256 ident 128 blk 128 blk16 8 pre 128 kw 144 fs 4096 da 4096 hit 256 selc 256"),
        ("float16", "expn 512 xo 256 ni16 128 turn 136 ones 128 krow16 136 lim 136 bp 8 bn 8 nb 256 zm 256 zin 288 zz 288 zin2 272 zz2 272 rs 128 "
                    "crow 512 sumf 144 sj 2304 dsrc 128 dj 2048 i64 128 i16 128 rk 192 me 768 ff 512 vc 24 vct 128 pair 72 nas 64 sp 64 "
                    "last16 256 g8 144"),
        ("int32", "candi 256 kt 3104 mobi 256 lasti 256 wti 1 pint 16"),
        ("uint16", "el 16 wo 16"),
    ):
        words = names.split()
        for k in range(0, len(words), 2):
            SCRATCH[words[k]] = ("sbuf", [128, int(words[k + 1])], dtype)
    for t in range(STEPS):
        SCRATCH["cw%d" % t] = ("sbuf", [128, 272], "uint16")
        SCRATCH["cu%d" % t] = ("sbuf", [128, 256], "uint16")
        SCRATCH["co%d" % t] = ("sbuf", [128, 272], "uint16")
        SCRATCH["wt_%d" % t] = ("sbuf", [128, 528], "float16")
        SCRATCH["wn%d" % t] = ("sbuf", [128, 528], "float16")
    SCRATCH["kd"] = ("dram", [8, W], "bfloat16")
    for b in range(8):
        SCRATCH["b%d" % b] = ("psum", [128, 512], "float32")


_buffers()
LOADS = ["cand", "feat0", "feat1", "feat2", "want", "wts", "last", "mkey", "mobj", "kids", "kd"]
SEMAPHORES = ["sv", "ss", "sp", "sg", "lsem", "skeys", "arry0", "arry1", "oyn0", "oyn1", "omu"] + ["ld_" + x for x in LOADS]
SEMAPHORES += ["oyd%d" % k for k in range(4)] + ["arr%s%d%d" % (x, k, h) for x in "wc" for k in range(1, STEPS) for h in range(2)]


def A(name, c0, c1, step=1, p0=0, p1=128):
    return (name, p0, p1, c0, c1, step)


def overlap(a, b):
    if a[1] >= b[2] or b[1] >= a[2] or a[3] >= b[4] or b[3] >= a[4]:
        return False
    if a[5] > 1 and a[5] == b[5] and (a[3] - b[3]) % a[5]:
        return False
    return True


def covers(a, b):
    return a[5] == 1 and a[1] <= b[1] and a[2] >= b[2] and a[3] <= b[3] and a[4] >= b[4]


def machine(g, T):
    q = {"V": g.vector, "S": g.scalar, "P": g.tensor, "G": g, "Y": g.sync}
    sem = {"V": "sv", "S": "ss", "P": "sp", "G": "sg"}
    count = {}
    clock = {e: {} for e in q}
    hist = {}

    def need(e, ent):
        s, v, ck = ent[3], ent[4], ent[5]
        mine = clock[e]
        if mine.get(s, 0) < v:
            q[e].wait_ge(T.sem[s], v)
            for k in ck:
                if mine.get(k, 0) < ck[k]:
                    mine[k] = ck[k]
            if mine.get(s, 0) < v:
                mine[s] = v

    def order(e, R, Wr, others=False):
        found = []
        for regs, w in ((R, False), (Wr, True)):
            for r in regs:
                psum = r[0][0] == "b" and r[0][1:].isdigit()
                for ent in hist.get(r[0], []):
                    if w and others and ent[2] == e:
                        continue
                    if (psum and ent[2] != e) or ((w or ent[1]) and overlap(r, ent[0])):
                        found.append(ent)
        found.sort(key=lambda ent: -ent[4])
        for ent in found:
            need(e, ent)

    def log(e, R, Wr, s, v):
        ck = dict(clock[e])
        for regs, w in ((R, False), (Wr, True)):
            for r in regs:
                h = hist.setdefault(r[0], [])
                if w:
                    h[:] = [x for x in h if not covers(r, x[0])]
                h[:] = [x for x in h if not (x[2] == e and x[3] == s and x[0] == r and x[1] == w)]
                h.append([r, w, e, s, v, ck])

    def ap(x):
        if x[0] == "ind":
            return ap(x[1]).indirect(ap(x[2]))
        t = T[x[0]]
        if x[5] == 1:
            return t[x[1]:x[2], x[3]:x[4]]
        return t[x[1]:x[2], x[3]:x[4]:x[5]]

    def run(e, call, R, Wr, acc=False):
        R2, W2 = [], []
        for x in R:
            if isinstance(x, tuple):
                R2 += [x[1], x[2]] if x[0] == "ind" else [x]
        for x in Wr:
            if x[0] == "ind":
                W2.append(x[1])
                R2.append(x[2])
            else:
                W2.append(x)
        order(e, R2, W2, acc)
        s = sem[e]
        count[s] = count.get(s, 0) + 1
        call().then_inc(T.sem[s], 1)
        log(e, R2, W2, s, count[s])

    def sc(x):
        return ap(x) if isinstance(x, tuple) else x

    def tt(out, a, b, op):
        run("V", lambda: g.vector.tensor_tensor(ap(out), ap(a), ap(b), op), [a, b], [out])

    def ts(out, a, s1, op0, s2=None, op1=None):
        if op1 is None:
            run("V", lambda: g.vector.tensor_scalar(ap(out), ap(a), sc(s1), None, op0), [a, s1], [out])
        else:
            run("V", lambda: g.vector.tensor_scalar(ap(out), ap(a), sc(s1), sc(s2), op0, op1), [a, s1, s2], [out])

    def cp(out, a):
        run("V", lambda: g.vector.tensor_copy(ap(out), ap(a)), [a], [out])

    def fill(out, c):
        run("V", lambda: g.vector.memset(ap(out), c), [], [out])

    def scan(out, d0, d1, init, op0, op1):
        run("V", lambda: g.vector.tensor_tensor_scan(ap(out), ap(d0), ap(d1), init, op0, op1), [d0, d1], [out])

    def act(out, a, func, bias=0.0, scale=1.0, acc=None):
        if acc is None:
            run("S", lambda: g.scalar.activation(ap(out), ap(a), func, bias=sc(bias), scale=sc(scale)), [a, bias, scale], [out])
        else:
            run("S", lambda: g.scalar.activation(ap(out), ap(a), func, bias=sc(bias), scale=sc(scale), accum_out=ap(acc)),
                [a, bias, scale], [out, acc])

    def mm(out, lhsT, rhs, start=True, stop=True):
        run("P", lambda: g.tensor.matmul(ap(out), ap(lhsT), ap(rhs), start, stop), [lhsT, rhs], [out], acc=not start)

    def iota(out, pattern, base, cm, small=True):
        if small:
            run("G", lambda: g.iota(ap(out), pattern, base, cm, allow_small_or_imprecise_dtypes=True), [], [out])
        else:
            run("G", lambda: g.iota(ap(out), pattern, base, cm), [], [out])

    def load(e, out, src, s):
        q[e].dma_start(ap(out), src).then_inc(T.sem[s], 16)
        hist.setdefault(out[0], []).append([out, True, "D", s, 16, {}])

    def copy(e, out, a, s):
        order(e, [a], [out])
        q[e].dma_start(ap(out), ap(a)).then_inc(T.sem[s], 16)
        hist.setdefault(out[0], []).append([out, True, "D", s, 16, dict(clock[e])])

    def rows(e, out, a, s):
        order(e, [a], [out])
        for i in range(16):
            q[e].dma_start(T[out[0]][i:128:16, :], ap(a)).then_inc(T.sem[s], 16)
        hist.setdefault(out[0], []).append([out, True, "D", s, 256, dict(clock[e])])
        count[s] = 256

    def store(e, dst, a, s):
        order(e, a, [])
        q[e].dma_start(dst, ap(a[0])).then_inc(T.sem[s], 16)
        count[s] = 16

    def send(a, out, s, addr, mask, n):
        order("G", [a], [])
        g.remote_dma(ap(out), ap(a), T.sem[s], T.sem["lsem"], addr[1], addr[0], mask)
        count["lsem"] = count.get("lsem", 0) + n
        hist.setdefault(out[0], []).append([out, True, "R", s, n, {}])

    def finish(extra):
        for s, v in list(count.items()) + extra:
            if clock["G"].get(s, 0) < v:
                g.wait_ge(T.sem[s], v)

    return dict(tt=tt, ts=ts, cp=cp, fill=fill, scan=scan, act=act, mm=mm, iota=iota, load=load, copy=copy, rows=rows, store=store,
                send=send, finish=finish)


ORDER = [
    'vt0 dm0 SCAN R OD Z ZM NA nz OL HIT nm OC nas ck ds0 X FI XO W h20 G3 FE FM SELC cnt uu0 kc G2 WABS EM kcc g3 V0 sub3 KA VC vt1 EL KB VD rnd uv0 OUT we0 wo0 v2 sub2 abs2 FIX s lim sub0 dm1 s sub1 REST abs0 ds1 p0 p1 abs3 abs1 CO ext s sum h21 uu1 s uv1 we1 dq spread wo1',
    'v2 G3 G2 SCAN s R OD mkc kc Z ZM V0 g3 sub2 sub0 OL NA HIT kcc abs2 s abs0 X sub3 XO FI s FM SELC FE s KA OC sub1 EM EL VC VD W KB FIX p0 abs3 p1 OUT CO abs1 sum WABS REST',
    'G2 G3 kc kcc c0 c1 V0 ks sub2 abs2 sub3 abs3 V1 sub1 km j0 abs1 sub0 abs0 p0 p1 c2 sum m0',
    'G2 c3 c4 SCAN j3 v1 R v0 G3 OD d2 Z kc j2 v2 sub2 sub0 ZM abs2 sub3 v3 sub1 abs3 OL d3 HIT kcc c5 X FI FM FE abs0 abs1 d0 OC SELC NA KA EM EL XO W VD l p0 p1 VC KB OUT j1 FIX sum d1 WABS REST CO',
    'G2 v3 SCAN R sub2 s G3 OD v1 mkc Z v0 ZM abs2 sub3 abs3 OL s HIT sub0 abs0 v2 OC X FI s FE kc kcc NA sub1 FM SELC EM s KA EL VC KB VD FIX p0 p1 abs1 sum OUT',
    'yn0 SCAN R OD vt0 NA Z dm0 ds0 ZM OL ck nz HIT nm h20 X FI uu0 FE uv0 wo0 ext FM nas OC SELC KA EM VC vt1 we0 VD EL KB FIX s OUT s dm1 ds1 yn1 s h21 dq uu1 s uv1 we1 wo1 s s s s spread my0 my1 my2 yd0 yd1 yd2 yd3',
]


def rank_program(g, core, T, topo):
    rank = T.rank_of(core)
    if rank is None:
        return
    O, F = AluOpType, ActivationFunctionType
    m = machine(g, T)
    tt, ts, cp, fill, scan, act, mm, iota = (m[k] for k in ("tt", "ts", "cp", "fill", "scan", "act", "mm", "iota"))
    n = len(T.cores)
    nxt, home = T.cores[(rank + 1) % n], T.cores[(rank - STEPS + 1) % n]

    def link(dst):
        return topo.addr(dst), topo.mask(core, dst), len(topo.engines(core, dst))

    def full(name, w=128):
        return A(name, 0, w)

    def row(name, c0, c1):
        return A(name, c0, c1, 1, 0, 1)

    def other(name, h, p1=128):
        return A(name, 128 - 128 * h, 256 - 128 * h, 1, 0, p1)

    def part(name, h, k):
        c0 = (0, 128, 256)[k] if h == 0 else (400, 272, 264)[k]
        return A(name, c0, c0 + (8 if k == 2 else 128))

    load = m["load"]
    load("Y", full("candi", 256), T.cand[:, :], "ld_cand")
    load("S", full("want0", 256), T.want[:, :], "ld_want")
    load("Y", full("wti", 1), T.wts[:, :], "ld_wts")
    load("S", A("featb", 0, W // 2), T.feat[:, 0:W // 2], "ld_feat0")
    load("Y", A("featb", W // 2, W), T.feat[:, W // 2:W], "ld_feat1")
    load("Y", full("mk0", 256), T.mkey[:, :], "ld_mkey")
    load("Y", full("mobi", 256), T.mobj[:, :], "ld_mobj")
    load("Y", A("kt", 0, W), T.kids[:, :], "ld_kids")
    load("Y", A("lasti", 0, 256, 1, 0, 8), T.last[:, :], "ld_last")

    iota(full("pint", 1), [[0, 1]], 0, 1, False)
    iota(full("colf", 144), [[1, 144]], 0, 0)
    iota(full("cg", 512), [[1, 32], [0, 16]], 0, 0)
    iota(row("krow", 0, 136), [[0, 8], [-1, 17]], 16, 0)
    iota(full("cmf", 256), [[0, 16], [1, 16]], 0, 0)
    iota(full("rr", 144), [[0, 8], [-1, 18]], 16, 0)
    iota(A("ct3", 0, 72), [[2, 4], [0, 18]], 0, 0)
    iota(A("kt", W, W + 32), [[0, 32]], 0, 0, False)

    def pi(k):
        return A("pint", k, k + 1)

    def pc(k):
        return A("pcol", k, k + 1)
    PF, PM, PG, P32, PP, P1615, CA, CB, WF, G15, DUMP, PG8, DUMP2, PM1 = range(14)

    fill(full("ones"), 1.0)
    for name, k in (("zin", 288), ("zz", 288)):
        fill(full(name, k), 0.0)
    ts(pi(2), pi(0), 4, O.arith_shift_right)
    ts(pi(1), pi(0), 15, O.bitwise_and)
    ts(pi(3), pi(0), 31, O.bitwise_and)
    cp(pc(PF), pi(0))
    fill(row("crow", 256, 512), 0.0)
    cp(pc(PG), pi(2))
    cp(pc(PM), pi(1))
    cp(pc(P32), pi(3))
    ts(full("ident"), full("colf"), pc(PF), O.is_equal)
    ts(pc(P1615), pc(PG), 16.0, O.mult, 15.0, O.add)
    ts(pc(PP), pc(PG), 17.0, O.mult, 16.0, O.add)
    ts(full("m16", 16), full("colf", 16), pc(PM), O.is_equal)
    ts(pc(CA), pc(PM), 11.0, O.is_lt)
    ts(pc(CB), pc(PM), 6.0, O.is_lt)
    ts(full("sumf", 143), full("colf", 143), pc(P1615), O.is_equal)
    for name, v in (("i16", 1.0), ("ni16", -1.0), ("i64", 1.0 / 64.0), ("junk", -2.0 / 64.0)):
        act(full(name), full("ident"), F.Copy, scale=v)
    tt(pc(PP), pc(PP), pc(PM), O.subtract)
    tt(pc(CB), pc(CB), pc(CA), O.subtract)
    ts(full("s1", 16), full("m16", 16), -1.0, O.add, 1.0 / 64.0, O.mult)
    ts(full("s2", 16), full("m16", 16), 1.0 / 64.0, O.mult)
    ts(full("blk16", 8), full("colf", 8), pc(PG), O.is_equal, 16.0, O.mult)
    ts(pc(CB), pc(CB), 1.0, O.add)
    ts(full("turn", 136), full("colf", 136), pc(PP), O.is_equal, Q12, O.mult)
    ts(pc(PG8), pc(PG), 8.0, O.add)
    tt(pc(CA), pc(CB), pc(CA), O.subtract)
    ts(pc(CB), pc(CB), -0.75, O.mult)
    for name, v in (("bp", 4096.0), ("bn", -4096.0)):
        ts(full(name, 8), full("colf", 8), pc(PG), O.is_equal, v, O.mult)
    ts(pc(CA), pc(CA), 0.75, O.mult)
    ts(pc(WF), full("wti", 1), 1.0, O.mult)
    act(full("kw", 143), full("sumf", 143), F.Copy, scale=pc(WF))
    ts(full("expn", 512), full("cg", 512), pc(P32), O.is_equal, -1.0, O.mult)
    for h in range(2):
        cp(A("cw0", 144 * h, 144 * h + 128), other("candi", h))
        mm(A("b5", 128 * h, 128 * h + 128), other("want0", h), full("ident"))
        act(part("wt_0", h, 1), other("candi", h), F.Copy, bias=-1536.0)
    for h in range(2):
        act(part("wt_0", h, 0), A("b5", 128 * h, 128 * h + 128), F.Copy)
    fill(A("krow", 0, 136, 17, 0, 1), BIG)
    act(row("krow16", 0, 136), row("krow", 0, 136), F.Copy)
    act(row("lim", 0, 136), row("krow", 0, 136), F.Copy, bias=-1008.0)
    act(row("krow", 0, 136), row("krow", 0, 136), F.Copy, bias=-1128.0)

    def mounts0():
        for h in range(2):
            act(A("me", 256 + 128 * h, 384 + 128 * h), other("mobi", h), F.Copy, bias=1536.0 * Q12, scale=-Q12)
            act(A("me", 512 + 128 * h, 640 + 128 * h), other("mk0", h), F.Copy)
        mm(A("b4", 0, 512), full("i16"), A("me", 256, 768))

    def lasts0():
        for h in range(2):
            act(A("last16", 128 * h, 128 * h + 128, 1, 0, 8), other("lasti", h, 8), F.Copy, bias=-1536.0)
        for k in range(16):
            mm(A("b7", 496, 512), A("g8", 15 - k, 143 - k, 1, 0, 8), A("last16", k, 256, 16, 0, 8), k == 0, k == 15)
        act(A("wt_0", 256, 272), A("b7", 496, 512), F.Copy)

    def consts0():
        ts(full("ct1"), full("cmf"), pc(PM), O.is_gt, 2.0, O.mult)
        ts(full("ct2"), full("cmf"), pc(PM), O.is_equal)
        ts(full("blk"), full("cg"), pc(PG), O.is_equal)
        ts(full("dsrc"), full("cg"), pc(PG), O.is_equal, 1.0 / 64.0, O.mult)
        tt(full("ct1"), full("ct1"), full("ct2"), O.subtract)
        tt(full("dsrc"), full("dsrc"), full("junk"), O.add)

    def consts1():
        ts(full("zm", 256), full("cmf", 256), pc(PM), O.is_le)
        ts(full("ct2"), full("cmf"), 8.0, O.is_lt)
        tt(full("pre"), full("ct1"), full("blk"), O.mult)
        fill(A("zm", 0, 256, 16), 0.0)
        ts(full("ct2"), full("ct2"), pc(CA), O.mult, pc(CB), O.add)

    def consts2():
        fill(row("crow", 0, 128), -4608.0)
        fill(row("crow", 128, 256), -3072.0)
        tt(full("rs"), full("ct2"), full("blk"), O.mult)
        fill(row("crow", 264, 280), 2047.0)
        fill(full("zin2", 272), 0.0)

    def consts3():
        fill(full("zz2", 272), 0.0)
        fill(A("crow", 288 + 17, 288 + 144, 18, 0, 1), -2047.0 / 64.0)
        fill(A("crow", 288 + 161, 288 + 216, 18, 0, 1), 1.0)
        ts(pc(PM1), pc(PF), -1.0, O.add)
        ts(pc(G15), pc(PF), 16.0, O.mult, 15.0, O.add)
        for k in range(4):
            ts(A("nb", 64 * k, 64 * k + 64), full("cmf", 64), pc(PG8 if k % 2 else PG), O.is_equal, 1.0 if k // 2 else -1.0, O.mult)

    def consts4():
        ts(A("g8", 0, 143, 1, 0, 8), A("colf", 0, 143, 1, 0, 8), A("pcol", G15, G15 + 1, 1, 0, 8), O.is_equal)
        ts(A("ds", 0, 72), A("ct3", 0, 72), pc(PF), O.is_equal, 1.0 / 64.0, O.mult)
        ts(A("ds", 72, 144), A("ct3", 0, 72), pc(PM1), O.is_equal, 1.0 / 64.0, O.mult)
        ts(full("rr", 144), full("rr", 144), pc(PM), O.is_equal)
        fill(A("rr", 144, 216), 0.0)
        tt(full("pair", 72), A("ds", 0, 72), A("ds", 72, 144), O.subtract)

    def consts5():
        ts(pc(DUMP), pc(PM), float(W), O.add)
        ts(pc(DUMP2), pc(PM), float(W + 16), O.add)
        fill(A("rr", 144, 216, 18), 1.0)
        fill(A("pair", 0, 72, 18), 0.0)
        fill(A("pair", 17, 72, 18), 0.0)
        for k in range(4):
            act(A("nb", 64 * k, 64 * k + 16), A("nb", 64 * k, 64 * k + 16), F.Copy, scale=Q12)

    def shifts(k0, k1):
        for k in range(k0, k1):
            act(A("sj", 144 * k, 144 * k + 143), full("sumf", 143), F.Copy, scale=A("m16", k, k + 1))

    def diffs(k0, k1):
        for k in range(k0, k1):
            ts(A("dj", 128 * k, 128 * k + 128), full("dsrc"), A("s1", k, k + 1), O.max, A("s2", k, k + 1), O.min)

    def key_sums():
        for c in range(16):
            mm(A("b3", 0, 192), A("kw", 15 - c, 143 - c), A("featb", 192 * c, 192 * c + 192), c == 0, c == 15)
        act(full("rk", 192), A("b3", 0, 192), F.Copy, bias=1536.0 - 31.5 / 64.0, scale=1.0 / 64.0)
        act(full("my", 192), full("rk", 192), F.Copy, bias=64.0 * 1536.0, scale=-64.0)

    def key_mod():
        tt(full("kcb", 192), A("b3", 0, 192), full("my", 192), O.add)
        m["copy"]("Y", A("kd", 0, W, 1, 0, 8), full("kcb", 192), "ld_kd")
        m["rows"]("Y", full("keys", W), A("kd", 0, W, 1, 0, 8), "skeys")
        load("Y", A("featb", W, 2 * W), T.feat[:, :], "ld_feat2")

    start = {"c0": consts0, "c1": consts1, "c2": consts2, "c3": consts3, "c4": consts4, "c5": consts5, "m0": mounts0, "l": lasts0,
             "ks": key_sums, "km": key_mod}
    for k in range(4):
        start["j%d" % k], start["d%d" % k] = lambda k=k: shifts(4 * k, 4 * k + 4), lambda k=k: diffs(4 * k, 4 * k + 4)

    FEAT, KEYS, KIDS = full("featb", W), full("keys", W), A("kt", 0, W)
    ONE = row("ones", 0, 128)
    SUB = ("b0", "b1", "b6")

    def dist(t, h):
        cw, wt, pb = "cw%d" % t, "wt_%d" % t, "b%d" % (2 + h)
        c0, f0 = 144 * h, 2048 * h
        d = {}

        def gather(e, l0, l1):
            out, src = A("fs", f0 + 16 * l0, f0 + 16 * l1), ("ind", full("featb", 2 * W) if t else FEAT, A(cw, c0 + l0, c0 + l1))
            return (lambda: cp(out, src)) if e == "V" else (lambda: act(out, src, F.Copy))

        def sub(c, b):
            mm(A(b, 0, 512), (wt, 32 * c, 32 * c + 32) + part(wt, h, 0)[3:], A("expn", 0, 512, 1, 32 * c, 32 * c + 32), True, False)
            mm(A(b, 0, 512), full("ident"), A("fs", f0 + 512 * c, f0 + 512 * c + 512), False, True)

        def kc():
            mm(A(pb, 136, 272), part(wt, h, 1), full("turn", 136), True, False)
            mm(A(pb, 136, 272), ONE, row("krow16", 0, 136), False, True)

        def sums():
            for k in range(16):
                mm(A(pb, 16 - k, 136, 17), A("da", f0 + k, f0 + 2048, 16), full("blk16", 8), False, k == 15)
        for c in range(8):
            d["v%d" % c], d["g%d" % c] = gather("V", 16 * c, 16 * c + 16), gather("S", 16 * c, 16 * c + 16)
        for c in range(4):
            d["V%d" % c], d["G%d" % c] = gather("V", 32 * c, 32 * c + 32), gather("S", 32 * c, 32 * c + 32)
        d["kc"], d["sum"] = kc, sums
        d["p0"] = lambda: mm(A(pb, 0, 136), part(wt, h, 1), full("turn", 136), True, False)
        d["p1"] = lambda: mm(A(pb, 0, 136), ONE, row("lim", 0, 136), False, False)
        d["kcc"] = lambda: act(A("kc", 136 * h, 136 * h + 136), A(pb, 136, 272), F.Copy)
        for j, c in enumerate((2, 0, 3, 1)):
            b = SUB[(4 * h + 8 * t + j) % 3]
            d["sub%d" % c] = lambda c=c, b=b: sub(c, b)
            d["abs%d" % c] = lambda c=c, b=b: act(A("da", f0 + 512 * c, f0 + 512 * c + 512), A(b, 0, 512), F.Abs)
        return d

    def chain(t, h):
        wt, wn, co, pb = "wt_%d" % t, "wn%d" % t, "co%d" % t, "b%d" % (2 + h)
        final = t == STEPS - 1
        a, b = 128 * h, 128 * h + 128
        best, r8 = A("sc", 136 * h + 16, 136 * h + 136, 17), A("r8", 8 * h, 8 * h + 8)
        z0 = 144 * h
        OL, olp = A(co, 128 + 8 * h, 136 + 8 * h), A(pb, 272, 280)
        fp, xp, wp = A("b5", 2 * a, 2 * a + 128), A(pb, 0, 128), A("b5", 2 * a + 128, 2 * a + 256)
        fe, fi = A("ff", 384 * h, 384 * h + 128), A("ff", 128 + a, 256 + a)
        ep, up = A(pb, 280 + 8 * h, 288 + 8 * h), A(pb, 288 - 8 * h, 296 - 8 * h)
        el = A("el", 8 * h, 8 * h + 8)
        d = {}

        def zm():
            mm(olp, A("zz", z0, z0 + 128), full("bp", 8), True, False)
            mm(olp, A("zz", z0 + 1, z0 + 129), full("bn", 8), False, False)
            mm(olp, A("zin", z0 + 1, z0 + 129), full("bp", 8), False, True)

        def wm():
            mm(wp, full("ni16"), part(wt, h, 0), True, False)
            mm(wp, A("xo", a, b), full("i16"), False, True)

        def fm():
            mm(fp, ONE, row("crow", 128 * final, 128 * final + 128), True, False)
            mm(fp, full("rs"), fi, False, True)

        def em():
            mm(A(pb, 280, 296), ONE, row("crow", 256 + 16 * h, 272 + 16 * h), True, False)
            for k in range(16):
                mm(A(pb, 280, 296), A("sumf", 15 - k, 143 - k), A("ff", 2 * a + k, 2 * a + 256, 16), False, k == 15)

        def out():
            if final:
                m["send"](A("new", a, b), other("yl", h), "arry%d" % h, *link(home))
            else:
                cp(A("cu%d" % t, a, b), A("nw", a, b))
                m["send"](A("cu%d" % t, a, b), A("cw%d" % (t + 1), z0, z0 + 128), "arrc%d%d" % (t + 1, h), *link(nxt))
        d["SCAN"] = lambda: scan(A("sc", 136 * h, 136 * h + 136), A(pb, 0, 136), A("kc", 136 * h, 136 * h + 136), BIG, O.min, O.max)
        d["R"] = lambda: ts(r8, best, MAGIC, O.add, MAGIC, O.subtract)
        d["OD"] = lambda: tt(A("zin", z0, z0 + 128, 16), best, r8, O.subtract)
        d["NA"] = lambda: ts(A("zin2", a, b, 16), best, 15.5, O.is_ge)
        d["Z"] = lambda: scan(A("zz", z0, z0 + 128), A("zm", 0, 128), A("zin", z0, z0 + 128), 0.0, O.mult, O.add)
        d["ZM"], d["FM"], d["EM"], d["OUT"] = zm, fm, em, out
        if not final:
            d["W"], d["WABS"] = wm, lambda: act(part(wn, h, 0), wp, F.Abs)
            d["REST"] = lambda: m["send"](A(wn, 264 * h, 264 * h + 264), A("wt_%d" % (t + 1), 264 * h, 264 * h + 264),
                                          "arrw%d%d" % (t + 1, h), *link(nxt))
            d["CO"] = lambda: ts(A(co, z0, z0 + 128), part(wn, h, 1), 1536.0, O.add)
            d["XO"] = lambda: act(A("xo", a, b), ("ind", FEAT, OL), F.Copy)
        d["OL"] = lambda: ts(OL, olp, 1536.0, O.add)
        d["HIT"] = lambda: tt(A("hit", a, b), ("ind", KEYS, OL), A("me", 512 + a, 512 + b), O.is_equal)
        d["X"] = lambda: mm(xp, full("pre"), A("hit", a, b))
        d["FI"] = lambda: ts(fi, xp, 0.0, O.is_lt, -4096.0, O.mult)
        d["FE"] = lambda: tt(fe, fi, A("b4", a, b), O.mult)
        d["SELC"] = lambda: act(A("selc", a, b), fp, F.Copy, bias=-3072.0 if final else -6144.0, scale=-2.0)
        d["EL"] = lambda: ts(el, ep, 1536.0, O.add)
        d["KA"] = lambda: tt(A("xk", a, b), ("ind", KIDS, OL), A("selc", a, b), O.add)
        d["KB"] = lambda: tt(A("nw", a, b), ("ind", KIDS, el), A("xk", a, b), O.max)
        d["FIX"] = lambda: tt(A("new", a, b) if final else part(wn, h, 1), A("nw", a, b), fp, O.add)
        d["OC"] = lambda: ts(part(wn, h, 2), OL, -1536.0, O.add)
        d["VC"] = lambda: tt(A("vc", 12 * h, 12 * h + 8), up, part(wn, h, 2), O.max)
        d["VD"] = lambda: tt(A("vc", 12 * h + 8, 12 * h + 12), up[:5] + (2,), part(wn, h, 2)[:5] + (2,), O.max)
        return d

    def post(t):
        co = "co%d" % t
        final = t == STEPS - 1
        d = {}

        def cnt():
            for k in range(8):
                mm(row("b7", 472, 504), A("ones", 0, 1), A("ff", 128 + 32 * k, 160 + 32 * k), k == 0, k == 7)
            act(row("junk", 0, 32), row("b7", 472, 504), F.Copy, bias=120.0 / 32.0, scale=16.0 * Q12, acc=row("cs", 0, 1))

        d["rnd"] = lambda: ts(row("cs", 1, 2), row("cs", 0, 1), 256.0 * MAGIC, O.add, 256.0 * MAGIC, O.subtract)
        d["lim"] = lambda: ts(row("lim", 0, 136), row("krow", 0, 136), row("cs", 0, 1), O.add, row("cs", 1, 2), O.subtract)

        def nm():
            for h in range(2):
                o, a = A("b7", 216, 280), 128 * h
                mm(o, A("zz2", a, a + 128), A("nb", 64 * h, 64 * h + 64), h == 0, False)
                mm(o, A("zz2", a + 1, a + 129), A("nb", 128 + 64 * h, 192 + 64 * h), False, False)
                mm(o, A("zin2", a + 1, a + 129), A("nb", 64 * h, 64 * h + 64), False, h == 1)

        def writers(h):
            v0, turned = 12 * h, A("vct", 0, 128, 1, 0, 8)

            def vt():
                mm(A("b7", 344, 472, 1, 0, 8), A("vc", v0, v0 + 8), full("i16"))
                act(turned, A("b7", 344, 472, 1, 0, 8), F.Copy)

            def dm():
                mm(A("b7", 0, 216), ONE, row("crow", 288, 504), True, False)
                for j in range(16):
                    mm(A("b7", 16 - j, 216, 18), A("dj", 128 * j, 128 * j + 128), A("vc", v0, v0 + 12), False, False)
                mm(A("b7", 17, 144, 18), full("i64"), A("vc", v0, v0 + 8), False, False)
                mm(A("b7", 144, 216), turned, A("pair", 0, 72, 1, 0, 8), False, True)
            d["vt%d" % h], d["dm%d" % h] = vt, dm
            d["ds%d" % h] = lambda: scan(full("ds", 216), A("b7", 0, 216), full("rr", 216), 0.0, O.mult, O.add)
            d["h2%d" % h] = lambda: ts(A("h2", v0, v0 + 12), A("ds", 17, 216, 18), 0.0, O.is_equal, 8192.0, O.mult)
            d["uu%d" % h] = lambda: tt(A("u16", 8 * h, 8 * h + 8), A("h2", v0, v0 + 8), A("vc", v0, v0 + 8), O.add)
            d["uv%d" % h] = lambda: tt(A("u16", 8 * h + 1, 8 * h + 8, 2), A("u16", 8 * h + 1, 8 * h + 8, 2), A("h2", v0 + 8, v0 + 12), O.add)
            d["we%d" % h] = lambda: ts(A("wo", 8 * h, 8 * h + 8, 2), A("u16", 8 * h, 8 * h + 8, 2), 1536.0, O.add, pc(DUMP), O.min)
            d["wo%d" % h] = lambda: ts(A("wo", 8 * h + 1, 8 * h + 8, 2), A("u16", 8 * h + 1, 8 * h + 8, 2), 1536.0, O.add, pc(DUMP2), O.min)
        writers(0)
        writers(1)

        def shift(j, i):
            return A("sj", 144 * j + 15 - i, 144 * j + 143 - i)

        def ext():
            mm(A("b7", 280, 296), full("i16"), A("wt_%d" % t, 256, 272), True, False)
            for i in range(16):
                mm(A("b7", 296, 344), shift((i + 5 * t) % 16, i), A("me", i, 768, 16), False, i == 15)

        def spread():
            mm(A("b4", 0, 512), full("i16"), A("me", 256, 768), True, False)
            for i in range(16):
                mm(A("b4", i, 512, 16), shift(i, (i + 5 * t) % 16), A("sp", 0, 32), False, False)
                mm(A("b4", i, 512, 16), shift(i, (i + 5 * t) % 16), A("sp", 32, 64), False, i == 15)

        todo = list(range(4, 8)) + list(range(4))

        def scatter():
            b = todo.pop()
            src = A("new", 32 * b, 32 * b + 32) if final else A(co, 32 * b + 16 * (b // 4), 32 * b + 16 * (b // 4) + 32)
            cp(("ind", A("kt", 0, W + 32), A("wo", 2 * b, 2 * b + 2)), src)
        d["cnt"], d["nm"], d["ext"], d["spread"], d["s"] = cnt, nm, ext, spread, scatter
        d["ck"] = lambda: act(full("me", 256), ("ind", KEYS, A(co, 128, 144)), F.Copy, scale=-1.0)
        d["nz"] = lambda: scan(full("zz2", 256), full("zm", 256), full("zin2", 256), 0.0, O.mult, O.add)
        d["nas"] = lambda: cp(full("nas", 64), A("b7", 216, 280))
        d["dq"] = lambda: tt(full("sp", 64), A("b7", 280, 344), full("nas", 64), O.mult)
        d["mkc"] = lambda: act(A("me", 256, 768), A("b4", 0, 512), F.Copy)
        return d

    def ymu0():
        for h in range(2):
            act(other("mt", h), A("b4", 128 * h, 128 * h + 128), F.Copy, scale=-262144.0, bias=98304.0)

    def ymu1(h):
        tt(other("my", h), other("mt", h), A("b4", 256 + 128 * h, 384 + 128 * h), O.add)
        if h:
            m["store"]("Y", T.ymu[:, :], [full("my", 256)], "omu")

    def yd(k):
        c0, c1 = YD[k], YD[k + 1]
        b = A(SUB[k % 3], 0, c1 - c0)
        act(b, A("kt", 1536 + c0, 1536 + c1), F.Copy, scale=2.0)
        tt(A("ydb", c0, c1), A("kt", c0, c1), b, O.add)
        m["store"]("Y", T.yd[:, c0:c1], [A("ydb", c0, c1)], "oyd%d" % k)
    ends = {"my0": ymu0, "my1": lambda: ymu1(0), "my2": lambda: ymu1(1)}
    for h in range(2):
        ends["yn%d" % h] = lambda h=h: m["store"]("Y", T.yn[:, 128 - 128 * h:256 - 128 * h], [other("yl", h)], "oyn%d" % h)
    for k in range(4):
        ends["yd%d" % k] = lambda k=k: yd(k)

    ps = {}
    for p in range(2 * STEPS + 1):
        t, h = p // 2, p % 2
        calls = dist(t, h) if t < STEPS else dict(ends)
        if p:
            calls.update(chain((p - 1) // 2, 1 - h))
        if p and h == 0:
            ps = post(t - 1)
        calls.update(ps if p > 1 else start)
        for name in ORDER[2 + p if p < 2 else p - 7 if p > 10 else h].split():
            if name in calls:
                calls[name]()
    m["finish"]([("arry0", link(home)[2]), ("arry1", link(home)[2])] + [("ld_" + x, 16) for x in LOADS])
